import numpy as np
import ml_dtypes


def mxq(x, axis, fmt="e4m3"):
    dtype, down = {"e4m3": (ml_dtypes.float8_e4m3fn, 7), "e5m2": (ml_dtypes.float8_e5m2, 14)}[fmt]
    v = np.moveaxis(np.asarray(x, np.float32).astype(ml_dtypes.bfloat16).astype(np.float64), axis, -1)
    blocks = v.reshape(v.shape[:-1] + (-1, 32))
    amax = np.abs(blocks).max(-1, keepdims=True)
    byte = np.maximum(np.where(amax > 0, np.frexp(amax)[1] - 1 + 127, 0) - down, 1)
    scale = np.exp2(byte - 127.0)
    codes = (blocks / scale).astype(np.float32).astype(dtype).astype(np.float64)
    return np.moveaxis((codes * scale).reshape(v.shape), -1, axis)


WIDE = False


def mx_kscale(k):
    if not WIDE:
        return np.ones(k)
    levels = np.array([18, -18])
    if k % 512:
        return np.exp2(np.random.permutation(np.resize(levels, k // 32))).repeat(32)
    a = np.empty((k // 512, 16))
    for p in range(k // 512):
        a[p, :8] = np.random.permutation(np.resize(levels, 8))
        for g in range(8):
            far = levels[np.abs(levels - a[p, g]) >= 10]
            a[p, g + 8] = far[np.random.randint(len(far))]
    return np.exp2(a.ravel()).repeat(32)


def f64(x):
    return np.asarray(x).astype(np.float64)


def striped(idx):
    return np.tile(np.asarray(idx).reshape(-1, 16).T, (8, 1)).astype(np.uint16)


def unstriped(offs):
    return offs[:16].T.reshape(-1).astype(np.int64)


B, N, T, D, R = 1, 512, 2048, 512, 1024


def setup_inputs():
    n = np.random.standard_normal
    idx = np.random.permutation(T)[:B * N]
    u = np.ones(T)
    u[idx] = mx_kscale(B * N)
    us = u[idx].reshape(B, N)
    z = mx_kscale(R)[:, None]
    act = n((B, R, N))
    s = mx_kscale(D)
    return {
        "zT": (act.transpose(0, 2, 1) * us[:, :, None]).astype(np.float32),
        "wT": (n((D, T)) / np.sqrt(N) / u * s[:, None]).astype(np.float32),
        "xm": (n((B, R, D)) * s).astype(np.float32),
        "wt": (np.random.uniform(0.5, 1.5, (B, R, 1)) / np.sqrt(R) * z).astype(np.float32),
        "zm": (act / z).astype(np.float32),
        "cs": np.tile(np.random.uniform(0.5, 1.5, D) / s, (128, 1)).astype(np.float32),
        "offs": striped(idx),
    }


def reference(zT, wT, xm, wt, zm, cs, offs):
    idx = unstriped(offs)
    pick = lambda x: x[:, idx].reshape(x.shape[0], B, N).transpose(1, 0, 2)
    w = pick(f64(wT))
    rec = mxq(f64(zT), 1, "e4m3").transpose(0, 2, 1) @ mxq(w, 2, "e4m3").transpose(0, 2, 1)
    q = f64(cs)[:1] * (rec - f64(xm))
    e = f64(wt) * f64(cs)[:1] * np.tanh(q)
    dw = mxq(e, 1, "e5m2").transpose(0, 2, 1) @ mxq(f64(zm), 1, "e4m3")
    gw = np.zeros((D, T))
    gw[:, idx] = dw.transpose(1, 0, 2).reshape(D, B * N)
    gz = mxq(e, 2, "e5m2") @ mxq(w, 1, "e4m3")
    return gw, gz

@@ -1,0 +1,321 @@
+from contextlib import ExitStack
+
+import concourse.mybir as mybir
+from concourse.masks import make_identity
+
+N, T, D, R = 512, 2048, 512, 1024
+FLOPS = 3 * 2 * R * D * N
+
+F32 = mybir.dt.float32
+BF16 = mybir.dt.bfloat16
+U32 = mybir.dt.uint32
+U16 = mybir.dt.uint16
+U8 = mybir.dt.uint8
+E4M3 = mybir.dt.float8_e4m3fn_x4
+E5M2 = mybir.dt.float8_e5m2_x4
+MULT = mybir.AluOpType.mult
+SUB = mybir.AluOpType.subtract
+ADD = mybir.AluOpType.add
+COPY = mybir.ActivationFunctionType.Copy
+TANH = mybir.ActivationFunctionType.Tanh
+
+P = 128
+PACK = 4
+KP = P * PACK
+G = R // KP
+
+
+def tile_attend_gdi_lch_wz_kernel(tc, zT, wT, xm, wt, zm, cs, offs, out_0, out_1):
+    nc = tc.nc
+    with ExitStack() as ctx:
+        keep = ctx.enter_context(tc.tile_pool(name="keep", bufs=1))
+        ring = ctx.enter_context(tc.tile_pool(name="ring", bufs=3))
+        psum = ctx.enter_context(tc.psum_pool(name="psum", bufs=2))
+
+        def held(name, shape, dtype):
+            return keep.tile(shape, dtype, name=name, align_bytes=64)
+
+        def mx_operand(name, width):
+            return held(name + "_codes", [P, width], U32), held(name + "_scales", [P, width], U8)
+
+        def quantize(operand, fmt, grouped):
+            codes, scales = operand
+            nc.vector.quantize_mx(out=codes.bitcast(fmt), scales=scales, in_=grouped)
+
+        def cols(operand, a, b):
+            return operand[0][:, a:b], operand[1][:, a:b]
+
+        def mm(out, lhsT, lhsT_fmt, rhs, start=True, stop=True):
+            nc.tensor.matmul_mx(
+                out=out, lhsT=lhsT[0].bitcast(lhsT_fmt), lhsT_scale=lhsT[1],
+                rhs=rhs[0].bitcast(E4M3), rhs_scale=rhs[1], start=start, stop=stop,
+            )
+
+        def interleave(copy, grouped, planes):
+            if copy is None:
+                nc.gpsimd.tensor_scalar(grouped, planes.rearrange("p t c -> p c t"), 1.0, 0.0, MULT, ADD)
+                return
+            copy(
+                out=grouped.rearrange("p (c i) t -> p c t i", i=4),
+                in_=planes.rearrange("p t (c i) -> p c t i", i=4),
+            )
+
+        vcopy, scopy, gcopy = nc.vector.tensor_copy, nc.scalar.copy, None
+
+        offsets = keep.tile([P, N // 16], U16, name="offsets")
+        wt_rows = held("wt_rows", [P, R // P], F32)
+        cs_cols = held("cs_cols", [P, PACK], F32)
+        table = [held("table%d" % t, [P, T], F32) for t in range(PACK)]
+        zT_raw = [held("zT_raw%d" % g, [P, PACK, KP], F32) for g in range(G)]
+        zm_raw = [held("zm_raw%d" % g, [P, PACK, N], F32) for g in range(G)]
+        xm_raw = [held("xm_raw%d" % g, [P, PACK, D], F32) for g in range(G)]
+        window = [held("window%d" % t, [P, T], F32) for t in range(PACK)]
+        ident = held("ident", [P, P], F32)
+        wt_all = held("wt_all", [P, R], F32)
+        gain = held("gain", [P, PACK, R], F32)
+        atoms = held("atoms", [P, PACK, N], F32)
+        wi_bf = [held("wi_bf%d" % u, [P, 2 * P, PACK], BF16) for u in range(2)]
+        e_planes = [held("e_planes%d" % g, [P, PACK, KP], BF16) for g in range(G)]
+        er_bf = [held("er_bf%d" % t, [P, G, P, PACK], BF16) for t in range(PACK)]
+        wi_mx = [mx_operand("wi%d" % u, 2 * P) for u in range(2)]
+        wd_mx = mx_operand("wd", N)
+        zT_mx = [mx_operand("zT%d" % g, KP) for g in range(G)]
+        zm_mx = [mx_operand("zm%d" % g, N) for g in range(G)]
+        er_mx = [mx_operand("er%d" % t, G * P) for t in range(PACK)]
+        ed_mx = [mx_operand("ed%d" % g, KP) for g in range(G)]
+        diff = {}
+
+        wT_planes = wT.rearrange("(p t) c -> p t c", t=PACK)
+        out0_planes = out_0.rearrange("(p t) c -> p t c", t=PACK)
+        zT_rows = zT[0].rearrange("(p j) r -> p j r", j=PACK)
+
+        def load_table(t):
+            nc.sync.dma_start(out=table[t][:], in_=wT_planes[:, t, :])
+
+        def load_zT(g):
+            nc.sync.dma_start(out=zT_raw[g][:], in_=zT_rows[:, :, g * KP : (g + 1) * KP])
+
+        def load_xm(g):
+            nc.sync.dma_start(out=xm_raw[g][:], in_=xm[0, g * KP : (g + 1) * KP, :].rearrange("(c p) d -> p c d", p=P))
+
+        def load_zm(g):
+            nc.sync.dma_start(out=zm_raw[g][:], in_=zm[0, g * KP : (g + 1) * KP, :].rearrange("(p j) i -> p j i", j=PACK))
+
+        def spread_wt(h):
+            bank = psum.tile([P, PACK, P], F32, name="bank", bufs=6)
+            for c in range(PACK):
+                col = PACK * h + c
+                nc.tensor.transpose(bank[:, c, :], wt_rows[:, col : col + 1].to_broadcast([P, P]), ident[:])
+            nc.scalar.copy(
+                out=wt_all[:].rearrange("p (n h c) -> p h n c", h=2, c=PACK)[:, h],
+                in_=bank[:].rearrange("p c n -> p n c"),
+            )
+
+        def zero(t, engine):
+            engine.memset(window[t][:], 0.0)
+
+        def make_gain(t, where):
+            if where == "v":
+                nc.vector.tensor_scalar(gain[:, t, :], wt_all[:], cs_cols[:, t : t + 1], None, MULT)
+            elif where == "s":
+                nc.scalar.activation(gain[:, t, :], wt_all[:], COPY, scale=cs_cols[:, t : t + 1])
+            else:
+                nc.gpsimd.tensor_scalar(gain[:, t, :], wt_all[:], cs_cols[:, t : t + 1], 0.0, MULT, ADD)
+
+        def gather(t):
+            nc.vector.tensor_copy(atoms[:, t, :], table[t][:].indirect(offsets[:]))
+
+        def turn_atoms(t, copy):
+            u, e = divmod(t, 2)
+            bank = psum.tile([P, PACK, P], F32, name="bank", bufs=6)
+            for s in range(PACK):
+                nc.tensor.transpose(bank[:, s, :], atoms[:, t, s:N:PACK], ident[:])
+            copy(out=wi_bf[u][:, e * P : (e + 1) * P, :], in_=bank[:].rearrange("p s m -> p m s"))
+
+        def quant_wi(u):
+            quantize(cols(wi_mx[u], 0, 2 * P), E4M3, wi_bf[u][:].rearrange("p c s -> p (c s)"))
+
+        planes = {"zT": zT_raw, "zm": zm_raw, "wd": [atoms], "ed": e_planes}
+        operand = {"zT": zT_mx, "zm": zm_mx, "wd": [wd_mx], "ed": ed_mx}
+        grouped, th, dw, gz = {}, {}, {}, {}
+
+        def group(what, g, part, parts, copy):
+            if part == 0:
+                grouped[what, g] = ring.tile([P, KP, PACK], BF16, name="grouped", align_bytes=64)
+            a, b = part * KP // parts, (part + 1) * KP // parts
+            interleave(copy, grouped[what, g][:, a:b, :], planes[what][g][:, :, a:b])
+
+        def quant(what, g, part, parts):
+            a, b = part * KP // parts, (part + 1) * KP // parts
+            fmt = E5M2 if what == "ed" else E4M3
+            quantize(cols(operand[what][g], a, b), fmt, grouped[what, g][:, a:b, :].rearrange("p c s -> p (c s)"))
+
+        def residual(u, g, h):
+            bank = psum.tile([P, 2, 2 * P], F32, name="rec")
+            for c in range(2):
+                first = (2 * h + c) * P
+                mm(bank[:, c, :], cols(zT_mx[g], first, first + P), E4M3, cols(wi_mx[u], 0, 2 * P))
+            d = ring.tile([P, 2, P, 2], F32, name="diff", bufs=8)
+            nc.vector.tensor_tensor(
+                d[:],
+                bank[:].rearrange("p c (e m) -> p c m e", e=2),
+                xm_raw[g][:, 2 * h : 2 * h + 2, :].rearrange("p c (m u e) -> p c m u e", u=2, e=2)[:, :, :, u, :],
+                SUB,
+            )
+            diff[u, g, h] = d
+
+        def squash(t, g):
+            u, e = divmod(t, 2)
+            bank = psum.tile([P, PACK, P], F32, name="bank", bufs=6)
+            for c in range(PACK):
+                nc.tensor.transpose(bank[:, c, :], diff[u, g, c // 2][:, c % 2, :, e], ident[:])
+            th[t, g] = ring.tile([P, KP], F32, name="th")
+            nc.scalar.activation(th[t, g][:], bank[:].rearrange("p c r -> p (c r)"), TANH, scale=cs_cols[:, t : t + 1])
+
+        def weigh(t, g, engine):
+            engine.tensor_tensor(e_planes[g][:, t, :], th[t, g][:], gain[:, t, g * KP : (g + 1) * KP], MULT)
+
+        def turn_error(t, g, copy):
+            words = e_planes[g][:, t, :].bitcast(F32)
+            bank = psum.tile([P, 2, P], F32, name="bank", bufs=6)
+            for v in range(2):
+                nc.tensor.transpose(bank[:, v, :], words[:, v : 2 * P : 2], ident[:])
+            copy(
+                out=er_bf[t][:, g].rearrange("p m s -> p (m s)").bitcast(F32).rearrange("p (m v) -> p m v", v=2),
+                in_=bank[:].rearrange("p v m -> p m v"),
+            )
+
+        def quant_er(t):
+            quantize(cols(er_mx[t], 0, G * P), E5M2, er_bf[t][:].rearrange("p g m s -> p (g m s)"))
+
+        def atom_grad(t, copy):
+            bank = psum.tile([P, N], F32, name="bank", bufs=6)
+            for g in range(G):
+                mm(bank[:], cols(er_mx[t], g * P, (g + 1) * P), E5M2, cols(zm_mx[g], 0, N), g == 0, g == G - 1)
+            dw[t] = ring.tile([P, N], F32, name="dw")
+            copy(out=dw[t][:], in_=bank[:])
+
+        def scatter(t):
+            nc.vector.tensor_copy(window[t][:].indirect(offsets[:]), dw[t][:])
+            nc.sync.dma_start(out=out0_planes[:, t, :], in_=window[t][:])
+
+        def code_grad(g, c, copy):
+            rows = out_1[0, g * KP : (g + 1) * KP, :].rearrange("(c p) i -> p c i", p=P)
+            bank = psum.tile([P, N], F32, name="bank", bufs=6)
+            mm(bank[:], cols(ed_mx[g], c * P, (c + 1) * P), E5M2, cols(wd_mx, 0, N))
+            if c % 2 == 0:
+                gz[g, c // 2] = ring.tile([P, 2, N], F32, name="gz")
+            copy(out=gz[g, c // 2][:, c % 2, :], in_=bank[:])
+            if c % 2 == 1:
+                nc.sync.dma_start(out=rows[:, c - 1 : c + 1, :], in_=gz[g, c // 2][:])
+
+        nc.sync.dma_start(offsets[:], offs)
+        nc.scalar.dma_start(out=wt_rows[:], in_=wt[0].rearrange("(p c) o -> p (c o)", p=P))
+        nc.scalar.dma_start(out=cs_cols[:], in_=cs[0].rearrange("(p t) -> p t", t=PACK))
+        make_identity(nc, ident[:])
+        load_table(0)
+        load_table(1)
+        load_xm(1)
+        load_zT(1)
+        group("zT", 1, 0, 2, vcopy)
+        group("zT", 1, 1, 2, scopy)
+        load_table(3)
+        load_zT(0)
+        gather(0)
+        group("zT", 0, 0, 2, vcopy)
+        spread_wt(0)
+        group("zT", 0, 1, 2, vcopy)
+        gather(1)
+        load_table(2)
+        load_xm(0)
+        gather(2)
+        quant("zT", 0, 0, 2)
+        turn_atoms(0, vcopy)
+        gather(3)
+        load_zm(1)
+        spread_wt(1)
+        turn_atoms(1, vcopy)
+        group("zm", 1, 0, 2, vcopy)
+        quant_wi(0)
+        turn_atoms(2, scopy)
+        residual(0, 0, 0)
+        turn_atoms(3, scopy)
+        zero(0, nc.vector)
+        zero(3, nc.vector)
+        quant("zT", 1, 0, 1)
+        residual(0, 1, 1)
+        load_zm(0)
+        make_gain(2, "s")
+        make_gain(3, "s")
+        quant("zT", 0, 1, 2)
+        make_gain(0, "s")
+        group("zm", 1, 1, 2, scopy)
+        quant("zm", 1, 0, 1)
+        residual(0, 0, 1)
+        zero(1, nc.vector)
+        quant_wi(1)
+        make_gain(1, "s")
+        squash(1, 0)
+        residual(1, 0, 1)
+        squash(0, 0)
+        group("zm", 0, 0, 2, scopy)
+        group("zm", 0, 1, 2, scopy)
+        group("wd", 0, 0, 2, scopy)
+        residual(0, 1, 0)
+        squash(0, 1)
+        residual(1, 1, 0)
+        residual(1, 0, 0)
+        residual(1, 1, 1)
+        weigh(0, 1, nc.vector)
+        group("wd", 0, 1, 2, scopy)
+        squash(3, 0)
+        squash(2, 1)
+        squash(3, 1)
+        squash(1, 1)
+        quant("wd", 0, 0, 1)
+        squash(2, 0)
+        weigh(2, 0, nc.vector)
+        weigh(3, 0, nc.vector)
+        zero(2, nc.vector)
+        weigh(2, 1, nc.vector)
+        weigh(0, 0, nc.vector)
+        turn_error(2, 0, scopy)
+        weigh(1, 0, nc.vector)
+        group("ed", 0, 0, 2, vcopy)
+        quant("ed", 0, 0, 2)
+        weigh(1, 1, nc.vector)
+        weigh(3, 1, nc.vector)
+        group("ed", 1, 0, 2, scopy)
+        turn_error(0, 1, scopy)
+        code_grad(0, 0, scopy)
+        turn_error(0, 0, scopy)
+        quant_er(0)
+        turn_error(2, 1, vcopy)
+        quant("ed", 1, 0, 2)
+        quant("zm", 0, 0, 1)
+        atom_grad(0, scopy)
+        turn_error(1, 0, scopy)
+        turn_error(1, 1, scopy)
+        quant_er(1)
+        code_grad(0, 1, scopy)
+        code_grad(1, 0, scopy)
+        group("ed", 0, 1, 2, scopy)
+        quant_er(2)
+        group("ed", 1, 1, 2, scopy)
+        atom_grad(2, scopy)
+        quant("ed", 1, 1, 2)
+        turn_error(3, 1, vcopy)
+        code_grad(1, 1, scopy)
+        turn_error(3, 0, scopy)
+        quant("ed", 0, 1, 2)
+        code_grad(0, 2, scopy)
+        code_grad(0, 3, scopy)
+        code_grad(1, 2, scopy)
+        atom_grad(1, scopy)
+        scatter(0)
+        code_grad(1, 3, scopy)
+        quant_er(3)
+        atom_grad(3, scopy)
+        scatter(1)
+        scatter(2)
+        scatter(3)

@@ -14,8 +14,8 @@ U8 = mybir.dt.uint8
 E4M3 = mybir.dt.float8_e4m3fn_x4
 E5M2 = mybir.dt.float8_e5m2_x4
 MULT = mybir.AluOpType.mult
-SUB = mybir.AluOpType.subtract
 ADD = mybir.AluOpType.add
+SUB = mybir.AluOpType.subtract
 COPY = mybir.ActivationFunctionType.Copy
 TANH = mybir.ActivationFunctionType.Tanh
 
@@ -23,6 +23,7 @@ P = 128
 PACK = 4
 KP = P * PACK
 G = R // KP
+HALF = KP // 2
 
 
 def tile_attend_gdi_lch_wz_kernel(tc, zT, wT, xm, wt, zm, cs, offs, out_0, out_1):
@@ -34,6 +35,9 @@ def tile_attend_gdi_lch_wz_kernel(tc, zT, wT, xm, wt, zm, cs, offs, out_0, out_1
 
         def held(name, shape, dtype):
             return keep.tile(shape, dtype, name=name, align_bytes=64)
+
+        def new_bank(shape):
+            return psum.tile(shape, F32, name="bank", bufs=4)
 
         def mx_operand(name, width):
             return held(name + "_codes", [P, width], U32), held(name + "_scales", [P, width], U8)
@@ -51,19 +55,13 @@ def tile_attend_gdi_lch_wz_kernel(tc, zT, wT, xm, wt, zm, cs, offs, out_0, out_1
                 rhs=rhs[0].bitcast(E4M3), rhs_scale=rhs[1], start=start, stop=stop,
             )
 
-        def interleave(copy, grouped, planes):
-            if copy is None:
-                nc.gpsimd.tensor_scalar(grouped, planes.rearrange("p t c -> p c t"), 1.0, 0.0, MULT, ADD)
-                return
-            copy(
-                out=grouped.rearrange("p (c i) t -> p c t i", i=4),
-                in_=planes.rearrange("p t (c i) -> p c t i", i=4),
-            )
+        def gcopy(out, in_):
+            nc.gpsimd.tensor_scalar(out, in_, 1.0, 0.0, MULT, ADD)
 
-        vcopy, scopy, gcopy = nc.vector.tensor_copy, nc.scalar.copy, None
+        vcopy, scopy = nc.vector.tensor_copy, nc.scalar.copy
 
         offsets = keep.tile([P, N // 16], U16, name="offsets")
-        wt_rows = held("wt_rows", [P, R // P], F32)
+        wt_rows = held("wt_rows", [P, G, PACK], F32)
         cs_cols = held("cs_cols", [P, PACK], F32)
         table = [held("table%d" % t, [P, T], F32) for t in range(PACK)]
         zT_raw = [held("zT_raw%d" % g, [P, PACK, KP], F32) for g in range(G)]
@@ -71,9 +69,8 @@ def tile_attend_gdi_lch_wz_kernel(tc, zT, wT, xm, wt, zm, cs, offs, out_0, out_1
         xm_raw = [held("xm_raw%d" % g, [P, PACK, D], F32) for g in range(G)]
         window = [held("window%d" % t, [P, T], F32) for t in range(PACK)]
         ident = held("ident", [P, P], F32)
-        wt_all = held("wt_all", [P, R], F32)
-        gain = held("gain", [P, PACK, R], F32)
         atoms = held("atoms", [P, PACK, N], F32)
+        atoms_bf = held("atoms_bf", [P, PACK, N], BF16)
         wi_bf = [held("wi_bf%d" % u, [P, 2 * P, PACK], BF16) for u in range(2)]
         e_planes = [held("e_planes%d" % g, [P, PACK, KP], BF16) for g in range(G)]
         er_bf = [held("er_bf%d" % t, [P, G, P, PACK], BF16) for t in range(PACK)]
@@ -83,7 +80,9 @@ def tile_attend_gdi_lch_wz_kernel(tc, zT, wT, xm, wt, zm, cs, offs, out_0, out_1
         zm_mx = [mx_operand("zm%d" % g, N) for g in range(G)]
         er_mx = [mx_operand("er%d" % t, G * P) for t in range(PACK)]
         ed_mx = [mx_operand("ed%d" % g, KP) for g in range(G)]
-        diff = {}
+        planes = {"zT": zT_raw, "zm": zm_raw, "wd": [atoms]}
+        operand = {"zT": zT_mx, "zm": zm_mx, "wd": [wd_mx], "ed": ed_mx}
+        wt_bank, grouped, diff, th, dw, gz = {}, {}, {}, {}, {}, {}
 
         wT_planes = wT.rearrange("(p t) c -> p t c", t=PACK)
         out0_planes = out_0.rearrange("(p t) c -> p t c", t=PACK)
@@ -101,49 +100,61 @@ def tile_attend_gdi_lch_wz_kernel(tc, zT, wT, xm, wt, zm, cs, offs, out_0, out_1
         def load_zm(g):
             nc.sync.dma_start(out=zm_raw[g][:], in_=zm[0, g * KP : (g + 1) * KP, :].rearrange("(p j) i -> p j i", j=PACK))
 
-        def spread_wt(h):
-            bank = psum.tile([P, PACK, P], F32, name="bank", bufs=6)
-            for c in range(PACK):
-                col = PACK * h + c
-                nc.tensor.transpose(bank[:, c, :], wt_rows[:, col : col + 1].to_broadcast([P, P]), ident[:])
-            nc.scalar.copy(
-                out=wt_all[:].rearrange("p (n h c) -> p h n c", h=2, c=PACK)[:, h],
-                in_=bank[:].rearrange("p c n -> p n c"),
-            )
+        def spread_wt(g):
+            wt_bank[g] = psum.tile([P, PACK, P], F32, name="wt_bank")
+            for s in range(PACK):
+                nc.tensor.transpose(wt_bank[g][:, s, :], wt_rows[:, g, s : s + 1].to_broadcast([P, P]), ident[:])
 
         def zero(t, engine):
             engine.memset(window[t][:], 0.0)
 
-        def make_gain(t, where):
-            if where == "v":
-                nc.vector.tensor_scalar(gain[:, t, :], wt_all[:], cs_cols[:, t : t + 1], None, MULT)
-            elif where == "s":
-                nc.scalar.activation(gain[:, t, :], wt_all[:], COPY, scale=cs_cols[:, t : t + 1])
-            else:
-                nc.gpsimd.tensor_scalar(gain[:, t, :], wt_all[:], cs_cols[:, t : t + 1], 0.0, MULT, ADD)
-
         def gather(t):
             nc.vector.tensor_copy(atoms[:, t, :], table[t][:].indirect(offsets[:]))
 
+        def round_atoms(t, copy):
+            copy(
+                out=atoms_bf[:, t, :].rearrange("p (v m e) -> p v m e", v=2, e=2),
+                in_=atoms[:, t, :].rearrange("p (m v e) -> p v m e", v=2, e=2),
+            )
+
+        def turn_words(plane):
+            words = plane.bitcast(F32)
+            bank = new_bank([P, 2, P])
+            for v in range(2):
+                nc.tensor.transpose(bank[:, v, :], words[:, v * P : (v + 1) * P], ident[:])
+            return bank
+
         def turn_atoms(t, copy):
             u, e = divmod(t, 2)
-            bank = psum.tile([P, PACK, P], F32, name="bank", bufs=6)
-            for s in range(PACK):
-                nc.tensor.transpose(bank[:, s, :], atoms[:, t, s:N:PACK], ident[:])
-            copy(out=wi_bf[u][:, e * P : (e + 1) * P, :], in_=bank[:].rearrange("p s m -> p m s"))
+            bank = turn_words(atoms_bf[:, t, :])
+            words = wi_bf[u][:].rearrange("p c s -> p (c s)").bitcast(F32)
+            copy(
+                out=words.rearrange("p (n e k v) -> p e n k v", e=2, k=2, v=2)[:, e],
+                in_=bank[:].rearrange("p v (n k) -> p n k v", k=2),
+            )
 
         def quant_wi(u):
             quantize(cols(wi_mx[u], 0, 2 * P), E4M3, wi_bf[u][:].rearrange("p c s -> p (c s)"))
 
-        planes = {"zT": zT_raw, "zm": zm_raw, "wd": [atoms], "ed": e_planes}
-        operand = {"zT": zT_mx, "zm": zm_mx, "wd": [wd_mx], "ed": ed_mx}
-        grouped, th, dw, gz = {}, {}, {}, {}
-
-        def group(what, g, part, parts, copy):
-            if part == 0:
-                grouped[what, g] = ring.tile([P, KP, PACK], BF16, name="grouped", align_bytes=64)
-            a, b = part * KP // parts, (part + 1) * KP // parts
-            interleave(copy, grouped[what, g][:, a:b, :], planes[what][g][:, :, a:b])
+        def group(what, g, half, copy):
+            if (what, g) not in grouped:
+                grouped[what, g] = ring.tile([P, KP, PACK], BF16, name="grouped", bufs=4, align_bytes=64)
+            dst = grouped[what, g][:, half * HALF : (half + 1) * HALF, :]
+            if what == "ed":
+                src = e_planes[g][:, :, half * HALF : (half + 1) * HALF]
+                if copy is gcopy:
+                    copy(out=dst.rearrange("p (e m) t -> p e m t", e=2), in_=src.rearrange("p t (m e) -> p e m t", e=2))
+                else:
+                    copy(
+                        out=dst.rearrange("p (e c i) t -> p e c t i", e=2, i=4),
+                        in_=src.rearrange("p t (c i e) -> p e c t i", e=2, i=4),
+                    )
+            else:
+                src = planes[what][g][:, :, half * HALF : (half + 1) * HALF]
+                if copy is gcopy:
+                    copy(out=dst, in_=src.rearrange("p t c -> p c t"))
+                else:
+                    copy(out=dst.rearrange("p (c i) t -> p c t i", i=4), in_=src.rearrange("p t (c i) -> p c t i", i=4))
 
         def quant(what, g, part, parts):
             a, b = part * KP // parts, (part + 1) * KP // parts
@@ -155,31 +166,41 @@ def tile_attend_gdi_lch_wz_kernel(tc, zT, wT, xm, wt, zm, cs, offs, out_0, out_1
             for c in range(2):
                 first = (2 * h + c) * P
                 mm(bank[:, c, :], cols(zT_mx[g], first, first + P), E4M3, cols(wi_mx[u], 0, 2 * P))
-            d = ring.tile([P, 2, P, 2], F32, name="diff", bufs=8)
+            diff[u, g, h] = ring.tile([P, 2, 2 * P], F32, name="diff", bufs=8)
+            rows = xm_raw[g][:, 2 * h : 2 * h + 2, :].rearrange("p c d -> p (c d)")
             nc.vector.tensor_tensor(
-                d[:],
-                bank[:].rearrange("p c (e m) -> p c m e", e=2),
-                xm_raw[g][:, 2 * h : 2 * h + 2, :].rearrange("p c (m u e) -> p c m u e", u=2, e=2)[:, :, :, u, :],
+                diff[u, g, h][:].rearrange("p e (n k) -> p n e k", k=2),
+                bank[:].rearrange("p c m -> p (c m)").rearrange("p (n e k) -> p n e k", e=2, k=2),
+                rows.rearrange("p (n k u e) -> p u n e k", k=2, u=2, e=2)[:, u],
                 SUB,
             )
-            diff[u, g, h] = d
 
         def squash(t, g):
             u, e = divmod(t, 2)
-            bank = psum.tile([P, PACK, P], F32, name="bank", bufs=6)
+            bank = new_bank([P, PACK, P])
             for c in range(PACK):
-                nc.tensor.transpose(bank[:, c, :], diff[u, g, c // 2][:, c % 2, :, e], ident[:])
-            th[t, g] = ring.tile([P, KP], F32, name="th")
-            nc.scalar.activation(th[t, g][:], bank[:].rearrange("p c r -> p (c r)"), TANH, scale=cs_cols[:, t : t + 1])
+                nc.tensor.transpose(bank[:, c, :], diff[u, g, c // 2][:, e, (c % 2) * P : (c % 2 + 1) * P], ident[:])
+            th[t, g] = ring.tile([P, KP], F32, name="th", bufs=4)
+            nc.scalar.activation(
+                th[t, g][:].rearrange("p (v m e) -> p v m e", v=2, e=2),
+                bank[:].rearrange("p c r -> p (c r)").rearrange("p (m v e) -> p v m e", v=2, e=2),
+                TANH,
+                scale=cs_cols[:, t : t + 1],
+            )
 
         def weigh(t, g, engine):
-            engine.tensor_tensor(e_planes[g][:, t, :], th[t, g][:], gain[:, t, g * KP : (g + 1) * KP], MULT)
+            for v in range(2):
+                engine.scalar_tensor_tensor(
+                    e_planes[g][:, t, v * HALF : (v + 1) * HALF].rearrange("p (m e) -> p m e", e=2),
+                    th[t, g][:, v * HALF : (v + 1) * HALF].rearrange("p (m e) -> p m e", e=2),
+                    cs_cols[:, t : t + 1],
+                    wt_bank[g][:, 2 * v : 2 * v + 2, :].rearrange("p e m -> p m e"),
+                    MULT,
+                    MULT,
+                )
 
         def turn_error(t, g, copy):
-            words = e_planes[g][:, t, :].bitcast(F32)
-            bank = psum.tile([P, 2, P], F32, name="bank", bufs=6)
-            for v in range(2):
-                nc.tensor.transpose(bank[:, v, :], words[:, v : 2 * P : 2], ident[:])
+            bank = turn_words(e_planes[g][:, t, :])
             copy(
                 out=er_bf[t][:, g].rearrange("p m s -> p (m s)").bitcast(F32).rearrange("p (m v) -> p m v", v=2),
                 in_=bank[:].rearrange("p v m -> p m v"),
@@ -189,133 +210,144 @@ def tile_attend_gdi_lch_wz_kernel(tc, zT, wT, xm, wt, zm, cs, offs, out_0, out_1
             quantize(cols(er_mx[t], 0, G * P), E5M2, er_bf[t][:].rearrange("p g m s -> p (g m s)"))
 
         def atom_grad(t, copy):
-            bank = psum.tile([P, N], F32, name="bank", bufs=6)
+            bank = new_bank([P, N])
             for g in range(G):
                 mm(bank[:], cols(er_mx[t], g * P, (g + 1) * P), E5M2, cols(zm_mx[g], 0, N), g == 0, g == G - 1)
-            dw[t] = ring.tile([P, N], F32, name="dw")
+            dw[t] = ring.tile([P, N], F32, name="dw", bufs=4)
             copy(out=dw[t][:], in_=bank[:])
 
         def scatter(t):
             nc.vector.tensor_copy(window[t][:].indirect(offsets[:]), dw[t][:])
             nc.sync.dma_start(out=out0_planes[:, t, :], in_=window[t][:])
 
-        def code_grad(g, c, copy):
-            rows = out_1[0, g * KP : (g + 1) * KP, :].rearrange("(c p) i -> p c i", p=P)
-            bank = psum.tile([P, N], F32, name="bank", bufs=6)
-            mm(bank[:], cols(ed_mx[g], c * P, (c + 1) * P), E5M2, cols(wd_mx, 0, N))
-            if c % 2 == 0:
-                gz[g, c // 2] = ring.tile([P, 2, N], F32, name="gz")
-            copy(out=gz[g, c // 2][:, c % 2, :], in_=bank[:])
-            if c % 2 == 1:
-                nc.sync.dma_start(out=rows[:, c - 1 : c + 1, :], in_=gz[g, c // 2][:])
+        def scat(t, h):
+            entries = offsets[:, h * (HALF // 16) : (h + 1) * (HALF // 16)]
+            nc.vector.tensor_copy(window[t][:].indirect(entries), dw[t][:, h * HALF : (h + 1) * HALF])
+            if h == 1:
+                nc.sync.dma_start(out=out0_planes[:, t, :], in_=window[t][:])
+
+        def code_grad(g, s, copy):
+            rows = out_1[0, g * KP : (g + 1) * KP, :].rearrange("(m s) i -> m s i", s=PACK)
+            bank = new_bank([P, N])
+            mm(bank[:], cols(ed_mx[g], s * P, (s + 1) * P), E5M2, cols(wd_mx, 0, N))
+            if s % 2 == 0:
+                gz[g, s // 2] = ring.tile([P, 2, N], F32, name="gz", bufs=4)
+            copy(out=gz[g, s // 2][:, s % 2, :], in_=bank[:])
+            if s % 2 == 1:
+                nc.sync.dma_start(out=rows[:, s - 1 : s + 1, :], in_=gz[g, s // 2][:])
 
         nc.sync.dma_start(offsets[:], offs)
-        nc.scalar.dma_start(out=wt_rows[:], in_=wt[0].rearrange("(p c) o -> p (c o)", p=P))
+        nc.scalar.dma_start(out=wt_rows[:], in_=wt[0].rearrange("(g p s) o -> p g (s o)", p=P, s=PACK))
         nc.scalar.dma_start(out=cs_cols[:], in_=cs[0].rearrange("(p t) -> p t", t=PACK))
         make_identity(nc, ident[:])
-        load_table(0)
-        load_table(1)
-        load_xm(1)
-        load_zT(1)
-        group("zT", 1, 0, 2, vcopy)
-        group("zT", 1, 1, 2, scopy)
-        load_table(3)
-        load_zT(0)
-        gather(0)
-        group("zT", 0, 0, 2, vcopy)
-        spread_wt(0)
-        group("zT", 0, 1, 2, vcopy)
-        gather(1)
         load_table(2)
-        load_xm(0)
-        gather(2)
-        quant("zT", 0, 0, 2)
-        turn_atoms(0, vcopy)
-        gather(3)
-        load_zm(1)
+        load_table(3)
         spread_wt(1)
-        turn_atoms(1, vcopy)
-        group("zm", 1, 0, 2, vcopy)
-        quant_wi(0)
-        turn_atoms(2, scopy)
-        residual(0, 0, 0)
-        turn_atoms(3, scopy)
+        load_table(1)
+        load_table(0)
         zero(0, nc.vector)
         zero(3, nc.vector)
-        quant("zT", 1, 0, 1)
-        residual(0, 1, 1)
-        load_zm(0)
-        make_gain(2, "s")
-        make_gain(3, "s")
-        quant("zT", 0, 1, 2)
-        make_gain(0, "s")
-        group("zm", 1, 1, 2, scopy)
-        quant("zm", 1, 0, 1)
-        residual(0, 0, 1)
+        gather(0)
+        load_zT(0)
         zero(1, nc.vector)
+        gather(2)
+        load_zT(1)
+        load_xm(0)
+        gather(3)
+        round_atoms(2, scopy)
+        gather(1)
+        round_atoms(3, scopy)
+        spread_wt(0)
+        turn_atoms(3, scopy)
+        round_atoms(1, scopy)
+        group("zT", 1, 0, vcopy)
+        group("zT", 0, 0, scopy)
+        turn_atoms(2, scopy)
+        group("zT", 1, 1, scopy)
+        round_atoms(0, scopy)
         quant_wi(1)
-        make_gain(1, "s")
-        squash(1, 0)
-        residual(1, 0, 1)
-        squash(0, 0)
-        group("zm", 0, 0, 2, scopy)
-        group("zm", 0, 1, 2, scopy)
-        group("wd", 0, 0, 2, scopy)
-        residual(0, 1, 0)
-        squash(0, 1)
-        residual(1, 1, 0)
+        group("zT", 0, 1, scopy)
+        turn_atoms(1, scopy)
+        quant("zT", 0, 0, 2)
+        quant("zT", 0, 1, 2)
+        quant("zT", 1, 0, 2)
+        turn_atoms(0, vcopy)
         residual(1, 0, 0)
-        residual(1, 1, 1)
-        weigh(0, 1, nc.vector)
-        group("wd", 0, 1, 2, scopy)
-        squash(3, 0)
-        squash(2, 1)
-        squash(3, 1)
-        squash(1, 1)
-        quant("wd", 0, 0, 1)
+        quant_wi(0)
+        residual(1, 0, 1)
+        group("wd", 0, 0, vcopy)
         squash(2, 0)
+        residual(0, 0, 0)
+        load_zm(1)
+        residual(0, 0, 1)
+        load_xm(1)
+        squash(3, 0)
         weigh(2, 0, nc.vector)
+        quant("zT", 1, 1, 2)
+        group("zm", 1, 0, vcopy)
         weigh(3, 0, nc.vector)
-        zero(2, nc.vector)
-        weigh(2, 1, nc.vector)
-        weigh(0, 0, nc.vector)
-        turn_error(2, 0, scopy)
+        load_zm(0)
+        squash(1, 0)
+        group("wd", 0, 1, vcopy)
+        squash(0, 0)
         weigh(1, 0, nc.vector)
-        group("ed", 0, 0, 2, vcopy)
+        group("zm", 1, 1, scopy)
+        residual(1, 1, 0)
+        weigh(0, 0, nc.vector)
+        quant("zm", 1, 0, 1)
+        residual(1, 1, 1)
+        group("ed", 0, 0, vcopy)
         quant("ed", 0, 0, 2)
-        weigh(1, 1, nc.vector)
+        residual(0, 1, 0)
+        turn_error(2, 0, scopy)
+        residual(0, 1, 1)
+        group("zm", 0, 0, vcopy)
+        squash(0, 1)
+        weigh(0, 1, nc.vector)
+        squash(3, 1)
         weigh(3, 1, nc.vector)
-        group("ed", 1, 0, 2, scopy)
-        turn_error(0, 1, scopy)
-        code_grad(0, 0, scopy)
-        turn_error(0, 0, scopy)
-        quant_er(0)
-        turn_error(2, 1, vcopy)
-        quant("ed", 1, 0, 2)
-        quant("zm", 0, 0, 1)
-        atom_grad(0, scopy)
-        turn_error(1, 0, scopy)
-        turn_error(1, 1, scopy)
-        quant_er(1)
-        code_grad(0, 1, scopy)
-        code_grad(1, 0, scopy)
-        group("ed", 0, 1, 2, scopy)
-        quant_er(2)
-        group("ed", 1, 1, 2, scopy)
-        atom_grad(2, scopy)
-        quant("ed", 1, 1, 2)
-        turn_error(3, 1, vcopy)
-        code_grad(1, 1, scopy)
+        squash(1, 1)
+        group("zm", 0, 1, scopy)
+        squash(2, 1)
+        quant("wd", 0, 0, 1)
+        weigh(1, 1, nc.vector)
         turn_error(3, 0, scopy)
+        group("ed", 0, 1, scopy)
+        turn_error(1, 0, scopy)
+        turn_error(0, 0, scopy)
+        quant("zm", 0, 0, 1)
+        turn_error(3, 1, scopy)
+        quant_er(3)
         quant("ed", 0, 1, 2)
         code_grad(0, 2, scopy)
+        weigh(2, 1, nc.vector)
+        group("ed", 1, 0, vcopy)
+        code_grad(0, 0, scopy)
+        quant("ed", 1, 0, 2)
+        turn_error(2, 1, scopy)
         code_grad(0, 3, scopy)
-        code_grad(1, 2, scopy)
-        atom_grad(1, scopy)
-        scatter(0)
-        code_grad(1, 3, scopy)
-        quant_er(3)
+        group("ed", 1, 1, scopy)
+        code_grad(1, 0, scopy)
+        code_grad(0, 1, scopy)
+        turn_error(0, 1, scopy)
+        quant("ed", 1, 1, 2)
+        turn_error(1, 1, scopy)
+        quant_er(0)
+        quant_er(1)
         atom_grad(3, scopy)
-        scatter(1)
-        scatter(2)
-        scatter(3)
+        scat(3, 0)
+        atom_grad(0, scopy)
+        code_grad(1, 1, scopy)
+        quant_er(2)
+        code_grad(1, 2, scopy)
+        scat(0, 0)
+        code_grad(1, 3, scopy)
+        atom_grad(1, scopy)
+        zero(2, nc.vector)
+        scat(1, 0)
+        scat(1, 1)
+        atom_grad(2, scopy)
+        scat(0, 1)
+        scat(2, 0)
+        scat(2, 1)
+        scat(3, 1)

@@ -24,6 +24,7 @@ PACK = 4
 KP = P * PACK
 G = R // KP
 HALF = KP // 2
+WINDOWS = 3
 
 
 def tile_attend_gdi_lch_wz_kernel(tc, zT, wT, xm, wt, zm, cs, offs, out_0, out_1):
@@ -67,7 +68,7 @@ def tile_attend_gdi_lch_wz_kernel(tc, zT, wT, xm, wt, zm, cs, offs, out_0, out_1
         zT_raw = [held("zT_raw%d" % g, [P, PACK, KP], F32) for g in range(G)]
         zm_raw = [held("zm_raw%d" % g, [P, PACK, N], F32) for g in range(G)]
         xm_raw = [held("xm_raw%d" % g, [P, PACK, D], F32) for g in range(G)]
-        window = [held("window%d" % t, [P, T], F32) for t in range(PACK)]
+        window = [held("window%d" % t, [P, T], F32) for t in range(WINDOWS)]
         ident = held("ident", [P, P], F32)
         atoms = held("atoms", [P, PACK, N], F32)
         atoms_bf = held("atoms_bf", [P, PACK, N], BF16)
@@ -217,14 +218,14 @@ def tile_attend_gdi_lch_wz_kernel(tc, zT, wT, xm, wt, zm, cs, offs, out_0, out_1
             copy(out=dw[t][:], in_=bank[:])
 
         def scatter(t):
-            nc.vector.tensor_copy(window[t][:].indirect(offsets[:]), dw[t][:])
-            nc.sync.dma_start(out=out0_planes[:, t, :], in_=window[t][:])
+            nc.vector.tensor_copy(window[t % WINDOWS][:].indirect(offsets[:]), dw[t][:])
+            nc.sync.dma_start(out=out0_planes[:, t, :], in_=window[t % WINDOWS][:])
 
         def scat(t, h):
             entries = offsets[:, h * (HALF // 16) : (h + 1) * (HALF // 16)]
-            nc.vector.tensor_copy(window[t][:].indirect(entries), dw[t][:, h * HALF : (h + 1) * HALF])
+            nc.vector.tensor_copy(window[t % WINDOWS][:].indirect(entries), dw[t][:, h * HALF : (h + 1) * HALF])
             if h == 1:
-                nc.sync.dma_start(out=out0_planes[:, t, :], in_=window[t][:])
+                nc.sync.dma_start(out=out0_planes[:, t, :], in_=window[t % WINDOWS][:])
 
         def code_grad(g, s, copy):
             rows = out_1[0, g * KP : (g + 1) * KP, :].rearrange("(m s) i -> m s i", s=PACK)
@@ -240,114 +241,109 @@ def tile_attend_gdi_lch_wz_kernel(tc, zT, wT, xm, wt, zm, cs, offs, out_0, out_1
         nc.scalar.dma_start(out=wt_rows[:], in_=wt[0].rearrange("(g p s) o -> p g (s o)", p=P, s=PACK))
         nc.scalar.dma_start(out=cs_cols[:], in_=cs[0].rearrange("(p t) -> p t", t=PACK))
         make_identity(nc, ident[:])
-        load_table(2)
-        load_table(3)
-        spread_wt(1)
-        load_table(1)
         load_table(0)
+        zero(2, nc.gpsimd)
         zero(0, nc.vector)
-        zero(3, nc.vector)
+        load_table(1)
         gather(0)
-        load_zT(0)
+        round_atoms(0, vcopy)
         zero(1, nc.vector)
-        gather(2)
-        load_zT(1)
-        load_xm(0)
-        gather(3)
-        round_atoms(2, scopy)
-        gather(1)
-        round_atoms(3, scopy)
-        spread_wt(0)
-        turn_atoms(3, scopy)
-        round_atoms(1, scopy)
-        group("zT", 1, 0, vcopy)
-        group("zT", 0, 0, scopy)
-        turn_atoms(2, scopy)
-        group("zT", 1, 1, scopy)
-        round_atoms(0, scopy)
-        quant_wi(1)
-        group("zT", 0, 1, scopy)
-        turn_atoms(1, scopy)
-        quant("zT", 0, 0, 2)
-        quant("zT", 0, 1, 2)
-        quant("zT", 1, 0, 2)
+        load_zT(0)
+        group("zT", 0, 0, gcopy)
         turn_atoms(0, vcopy)
-        residual(1, 0, 0)
+        group("zT", 0, 1, scopy)
+        load_table(3)
+        gather(1)
+        load_table(2)
+        quant("zT", 0, 0, 2)
+        spread_wt(0)
+        gather(3)
+        round_atoms(1, scopy)
+        turn_atoms(1, vcopy)
         quant_wi(0)
-        residual(1, 0, 1)
+        gather(2)
+        round_atoms(3, scopy)
+        turn_atoms(3, scopy)
+        load_xm(0)
+        load_zT(1)
+        round_atoms(2, scopy)
+        quant("zT", 0, 1, 2)
         group("wd", 0, 0, vcopy)
-        squash(2, 0)
-        residual(0, 0, 0)
-        load_zm(1)
-        residual(0, 0, 1)
-        load_xm(1)
-        squash(3, 0)
-        weigh(2, 0, nc.vector)
-        quant("zT", 1, 1, 2)
-        group("zm", 1, 0, vcopy)
-        weigh(3, 0, nc.vector)
-        load_zm(0)
-        squash(1, 0)
         group("wd", 0, 1, vcopy)
-        squash(0, 0)
+        residual(0, 0, 0)
+        turn_atoms(2, scopy)
+        quant_wi(1)
+        load_xm(1)
+        residual(0, 0, 1)
+        spread_wt(1)
+        load_zm(1)
+        group("zT", 1, 0, gcopy)
+        group("zT", 1, 1, scopy)
+        load_zm(0)
+        residual(1, 0, 0)
+        residual(1, 0, 1)
+        quant("zT", 1, 1, 2)
+        squash(1, 0)
+        quant("zT", 1, 0, 2)
         weigh(1, 0, nc.vector)
-        group("zm", 1, 1, scopy)
-        residual(1, 1, 0)
-        weigh(0, 0, nc.vector)
-        quant("zm", 1, 0, 1)
-        residual(1, 1, 1)
-        group("ed", 0, 0, vcopy)
-        quant("ed", 0, 0, 2)
-        residual(0, 1, 0)
-        turn_error(2, 0, scopy)
+        squash(0, 0)
         residual(0, 1, 1)
-        group("zm", 0, 0, vcopy)
+        squash(3, 0)
+        group("zm", 1, 0, scopy)
+        group("zm", 1, 1, gcopy)
+        quant("wd", 0, 0, 1)
+        residual(1, 1, 0)
+        squash(2, 0)
+        residual(0, 1, 0)
+        group("zm", 0, 0, gcopy)
+        weigh(0, 0, nc.vector)
+        residual(1, 1, 1)
+        weigh(3, 0, nc.vector)
         squash(0, 1)
-        weigh(0, 1, nc.vector)
-        squash(3, 1)
-        weigh(3, 1, nc.vector)
-        squash(1, 1)
+        weigh(2, 0, nc.vector)
         group("zm", 0, 1, scopy)
         squash(2, 1)
-        quant("wd", 0, 0, 1)
-        weigh(1, 1, nc.vector)
-        turn_error(3, 0, scopy)
-        group("ed", 0, 1, scopy)
-        turn_error(1, 0, scopy)
         turn_error(0, 0, scopy)
+        weigh(0, 1, nc.vector)
+        squash(1, 1)
+        group("ed", 0, 0, vcopy)
+        turn_error(2, 0, scopy)
         quant("zm", 0, 0, 1)
-        turn_error(3, 1, scopy)
-        quant_er(3)
+        turn_error(0, 1, scopy)
+        group("ed", 0, 1, scopy)
+        quant("zm", 1, 0, 1)
+        squash(3, 1)
+        quant("ed", 0, 0, 2)
+        code_grad(0, 0, scopy)
+        weigh(2, 1, nc.vector)
+        quant_er(0)
+        turn_error(2, 1, scopy)
+        weigh(1, 1, nc.vector)
+        code_grad(0, 1, scopy)
+        atom_grad(0, scopy)
         quant("ed", 0, 1, 2)
         code_grad(0, 2, scopy)
-        weigh(2, 1, nc.vector)
-        group("ed", 1, 0, vcopy)
-        code_grad(0, 0, scopy)
-        quant("ed", 1, 0, 2)
-        turn_error(2, 1, scopy)
         code_grad(0, 3, scopy)
-        group("ed", 1, 1, scopy)
-        code_grad(1, 0, scopy)
-        code_grad(0, 1, scopy)
-        turn_error(0, 1, scopy)
-        quant("ed", 1, 1, 2)
-        turn_error(1, 1, scopy)
-        quant_er(0)
-        quant_er(1)
-        atom_grad(3, scopy)
-        scat(3, 0)
-        atom_grad(0, scopy)
-        code_grad(1, 1, scopy)
+        weigh(3, 1, nc.vector)
+        group("ed", 1, 0, vcopy)
         quant_er(2)
-        code_grad(1, 2, scopy)
-        scat(0, 0)
-        code_grad(1, 3, scopy)
-        atom_grad(1, scopy)
-        zero(2, nc.vector)
-        scat(1, 0)
-        scat(1, 1)
+        quant("ed", 1, 0, 2)
+        turn_error(1, 1, scopy)
+        code_grad(1, 0, scopy)
+        scatter(0)
+        turn_error(1, 0, scopy)
+        group("ed", 1, 1, scopy)
+        quant_er(1)
         atom_grad(2, scopy)
-        scat(0, 1)
-        scat(2, 0)
-        scat(2, 1)
-        scat(3, 1)
+        code_grad(1, 1, scopy)
+        turn_error(3, 0, scopy)
+        quant("ed", 1, 1, 2)
+        code_grad(1, 2, scopy)
+        code_grad(1, 3, scopy)
+        scatter(2)
+        turn_error(3, 1, scopy)
+        quant_er(3)
+        atom_grad(1, scopy)
+        atom_grad(3, scopy)
+        scatter(1)
+        scatter(3)

@@ -25,6 +25,7 @@ KP = P * PACK
 G = R // KP
 HALF = KP // 2
 WINDOWS = 3
+BANKS = 6
 
 
 def tile_attend_gdi_lch_wz_kernel(tc, zT, wT, xm, wt, zm, cs, offs, out_0, out_1):
@@ -37,8 +38,14 @@ def tile_attend_gdi_lch_wz_kernel(tc, zT, wT, xm, wt, zm, cs, offs, out_0, out_1
         def held(name, shape, dtype):
             return keep.tile(shape, dtype, name=name, align_bytes=64)
 
-        def new_bank(shape):
-            return psum.tile(shape, F32, name="bank", bufs=4)
+        banks = [psum.tile([P, KP], F32, name="bank%d" % b, bufs=1) for b in range(BANKS)]
+        rotation, taken = list(range(BANKS)), []
+
+        def new_bank(parts, width, bank=None):
+            if bank is None:
+                bank = rotation[len(taken) % len(rotation)]
+                taken.append(bank)
+            return banks[bank][:, : parts * width].rearrange("p (a b) -> p a b", a=parts)
 
         def mx_operand(name, width):
             return held(name + "_codes", [P, width], U32), held(name + "_scales", [P, width], U8)
@@ -70,20 +77,23 @@ def tile_attend_gdi_lch_wz_kernel(tc, zT, wT, xm, wt, zm, cs, offs, out_0, out_1
         xm_raw = [held("xm_raw%d" % g, [P, PACK, D], F32) for g in range(G)]
         window = [held("window%d" % t, [P, T], F32) for t in range(WINDOWS)]
         ident = held("ident", [P, P], F32)
-        atoms = held("atoms", [P, PACK, N], F32)
-        atoms_bf = held("atoms_bf", [P, PACK, N], BF16)
-        wi_bf = [held("wi_bf%d" % u, [P, 2 * P, PACK], BF16) for u in range(2)]
-        e_planes = [held("e_planes%d" % g, [P, PACK, KP], BF16) for g in range(G)]
-        er_bf = [held("er_bf%d" % t, [P, G, P, PACK], BF16) for t in range(PACK)]
+        atoms_bf = held("atoms_bf", [P, PACK * N], BF16)[:].rearrange("p (t i) -> p t i", t=PACK)
+        wi_bf = [held("wi_bf%d" % u, [P, 2 * P * PACK], BF16) for u in range(2)]
+        e_planes = [held("e_planes%d" % g, [P, PACK * KP], BF16)[:].rearrange("p (t r) -> p t r", t=PACK) for g in range(G)]
+        th_tiles = [held("th%d" % t, [P, KP], F32) for t in range(PACK)]
+        words = [held("words%d" % k, [P, KP * PACK], BF16) for k in range(6)]
+        er_bf = [words[k][:, h * G * KP : (h + 1) * G * KP] for k, h in ((5, 1), (4, 1), (4, 0), (5, 0))]
+        dw = [held("dw%d" % t, [P, N], F32)[:] for t in range(PACK)]
         wi_mx = [mx_operand("wi%d" % u, 2 * P) for u in range(2)]
-        wd_mx = mx_operand("wd", N)
         zT_mx = [mx_operand("zT%d" % g, KP) for g in range(G)]
         zm_mx = [mx_operand("zm%d" % g, N) for g in range(G)]
-        er_mx = [mx_operand("er%d" % t, G * P) for t in range(PACK)]
+        pair_mx = [mx_operand("pair%d" % u, N) for u in range(2)]
+        er_mx = [cols(pair_mx[t // 2], t % 2 * G * P, (t % 2 + 1) * G * P) for t in range(PACK)]
+        wd_mx = mx_operand("wd", N)
         ed_mx = [mx_operand("ed%d" % g, KP) for g in range(G)]
-        planes = {"zT": zT_raw, "zm": zm_raw, "wd": [atoms]}
+        planes = {"zT": zT_raw, "zm": zm_raw, "wd": [atoms_bf], "ed": e_planes}
         operand = {"zT": zT_mx, "zm": zm_mx, "wd": [wd_mx], "ed": ed_mx}
-        wt_bank, grouped, diff, th, dw, gz = {}, {}, {}, {}, {}, {}
+        wt_bank, diff, th, gz = {}, {}, {}, {}
 
         wT_planes = wT.rearrange("(p t) c -> p t c", t=PACK)
         out0_planes = out_0.rearrange("(p t) c -> p t c", t=PACK)
@@ -110,60 +120,41 @@ def tile_attend_gdi_lch_wz_kernel(tc, zT, wT, xm, wt, zm, cs, offs, out_0, out_1
             engine.memset(window[t][:], 0.0)
 
         def gather(t):
-            nc.vector.tensor_copy(atoms[:, t, :], table[t][:].indirect(offsets[:]))
-
-        def round_atoms(t, copy):
-            copy(
-                out=atoms_bf[:, t, :].rearrange("p (v m e) -> p v m e", v=2, e=2),
-                in_=atoms[:, t, :].rearrange("p (m v e) -> p v m e", v=2, e=2),
-            )
+            nc.vector.tensor_copy(atoms_bf[:, t, :], table[t][:].indirect(offsets[:]))
 
         def turn_words(plane):
-            words = plane.bitcast(F32)
-            bank = new_bank([P, 2, P])
+            pairs = plane.bitcast(F32)
+            bank = new_bank(2, P)
             for v in range(2):
-                nc.tensor.transpose(bank[:, v, :], words[:, v * P : (v + 1) * P], ident[:])
+                nc.tensor.transpose(bank[:, v, :], pairs[:, v : 2 * P : 2], ident[:])
             return bank
 
         def turn_atoms(t, copy):
             u, e = divmod(t, 2)
             bank = turn_words(atoms_bf[:, t, :])
-            words = wi_bf[u][:].rearrange("p c s -> p (c s)").bitcast(F32)
+            pairs = wi_bf[u][:].bitcast(F32)
             copy(
-                out=words.rearrange("p (n e k v) -> p e n k v", e=2, k=2, v=2)[:, e],
+                out=pairs.rearrange("p (n e k v) -> p e n k v", e=2, k=2, v=2)[:, e],
                 in_=bank[:].rearrange("p v (n k) -> p n k v", k=2),
             )
 
         def quant_wi(u):
-            quantize(cols(wi_mx[u], 0, 2 * P), E4M3, wi_bf[u][:].rearrange("p c s -> p (c s)"))
+            quantize(cols(wi_mx[u], 0, 2 * P), E4M3, wi_bf[u][:])
 
-        def group(what, g, half, copy):
-            if (what, g) not in grouped:
-                grouped[what, g] = ring.tile([P, KP, PACK], BF16, name="grouped", bufs=4, align_bytes=64)
-            dst = grouped[what, g][:, half * HALF : (half + 1) * HALF, :]
-            if what == "ed":
-                src = e_planes[g][:, :, half * HALF : (half + 1) * HALF]
-                if copy is gcopy:
-                    copy(out=dst.rearrange("p (e m) t -> p e m t", e=2), in_=src.rearrange("p t (m e) -> p e m t", e=2))
-                else:
-                    copy(
-                        out=dst.rearrange("p (e c i) t -> p e c t i", e=2, i=4),
-                        in_=src.rearrange("p t (c i e) -> p e c t i", e=2, i=4),
-                    )
+        def group(what, g, a, b, copy):
+            dst = grouped[what, g][:, a * PACK : b * PACK].rearrange("p (c t) -> p c t", t=PACK)
+            src = planes[what][g][:, :, a:b]
+            if copy is gcopy:
+                copy(out=dst, in_=src.rearrange("p t c -> p c t"))
             else:
-                src = planes[what][g][:, :, half * HALF : (half + 1) * HALF]
-                if copy is gcopy:
-                    copy(out=dst, in_=src.rearrange("p t c -> p c t"))
-                else:
-                    copy(out=dst.rearrange("p (c i) t -> p c t i", i=4), in_=src.rearrange("p t (c i) -> p c t i", i=4))
+                copy(out=dst.rearrange("p (c i) t -> p c t i", i=4), in_=src.rearrange("p t (c i) -> p c t i", i=4))
 
-        def quant(what, g, part, parts):
-            a, b = part * KP // parts, (part + 1) * KP // parts
+        def quant(what, g, a, b):
             fmt = E5M2 if what == "ed" else E4M3
-            quantize(cols(operand[what][g], a, b), fmt, grouped[what, g][:, a:b, :].rearrange("p c s -> p (c s)"))
+            quantize(cols(operand[what][g], a, b), fmt, grouped[what, g][:, a * PACK : b * PACK])
 
         def residual(u, g, h):
-            bank = psum.tile([P, 2, 2 * P], F32, name="rec")
+            bank = new_bank(2, 2 * P)
             for c in range(2):
                 first = (2 * h + c) * P
                 mm(bank[:, c, :], cols(zT_mx[g], first, first + P), E4M3, cols(wi_mx[u], 0, 2 * P))
@@ -178,172 +169,145 @@ def tile_attend_gdi_lch_wz_kernel(tc, zT, wT, xm, wt, zm, cs, offs, out_0, out_1
 
         def squash(t, g):
             u, e = divmod(t, 2)
-            bank = new_bank([P, PACK, P])
+            bank = new_bank(PACK, P)
             for c in range(PACK):
                 nc.tensor.transpose(bank[:, c, :], diff[u, g, c // 2][:, e, (c % 2) * P : (c % 2 + 1) * P], ident[:])
-            th[t, g] = ring.tile([P, KP], F32, name="th", bufs=4)
-            nc.scalar.activation(
-                th[t, g][:].rearrange("p (v m e) -> p v m e", v=2, e=2),
-                bank[:].rearrange("p c r -> p (c r)").rearrange("p (m v e) -> p v m e", v=2, e=2),
-                TANH,
-                scale=cs_cols[:, t : t + 1],
-            )
+            th[t, g] = th_tiles[t]
+            nc.scalar.activation(th[t, g][:], bank[:].rearrange("p c r -> p (c r)"), TANH, scale=cs_cols[:, t : t + 1])
 
-        def weigh(t, g, engine):
-            for v in range(2):
-                engine.scalar_tensor_tensor(
-                    e_planes[g][:, t, v * HALF : (v + 1) * HALF].rearrange("p (m e) -> p m e", e=2),
-                    th[t, g][:, v * HALF : (v + 1) * HALF].rearrange("p (m e) -> p m e", e=2),
-                    cs_cols[:, t : t + 1],
-                    wt_bank[g][:, 2 * v : 2 * v + 2, :].rearrange("p e m -> p m e"),
-                    MULT,
-                    MULT,
-                )
+        def weigh(t, g):
+            nc.vector.scalar_tensor_tensor(
+                e_planes[g][:, t, :].rearrange("p (m s) -> p m s", s=PACK),
+                th[t, g][:].rearrange("p (m s) -> p m s", s=PACK),
+                cs_cols[:, t : t + 1],
+                wt_bank[g][:].rearrange("p s m -> p m s"),
+                MULT,
+                MULT,
+            )
 
         def turn_error(t, g, copy):
             bank = turn_words(e_planes[g][:, t, :])
             copy(
-                out=er_bf[t][:, g].rearrange("p m s -> p (m s)").bitcast(F32).rearrange("p (m v) -> p m v", v=2),
+                out=er_bf[t][:, g * KP : (g + 1) * KP].bitcast(F32).rearrange("p (m v) -> p m v", v=2),
                 in_=bank[:].rearrange("p v m -> p m v"),
             )
 
         def quant_er(t):
-            quantize(cols(er_mx[t], 0, G * P), E5M2, er_bf[t][:].rearrange("p g m s -> p (g m s)"))
+            quantize(cols(er_mx[t], 0, G * P), E5M2, er_bf[t])
 
-        def atom_grad(t, copy):
-            bank = new_bank([P, N])
+        def atom_grad(t, copy, bank):
+            bank = new_bank(1, N, bank)[:, 0, :]
             for g in range(G):
                 mm(bank[:], cols(er_mx[t], g * P, (g + 1) * P), E5M2, cols(zm_mx[g], 0, N), g == 0, g == G - 1)
-            dw[t] = ring.tile([P, N], F32, name="dw", bufs=4)
-            copy(out=dw[t][:], in_=bank[:])
+            copy(out=dw[t], in_=bank[:])
 
         def scatter(t):
-            nc.vector.tensor_copy(window[t % WINDOWS][:].indirect(offsets[:]), dw[t][:])
+            nc.vector.tensor_copy(window[t % WINDOWS][:].indirect(offsets[:]), dw[t])
             nc.sync.dma_start(out=out0_planes[:, t, :], in_=window[t % WINDOWS][:])
 
-        def scat(t, h):
-            entries = offsets[:, h * (HALF // 16) : (h + 1) * (HALF // 16)]
-            nc.vector.tensor_copy(window[t % WINDOWS][:].indirect(entries), dw[t][:, h * HALF : (h + 1) * HALF])
-            if h == 1:
-                nc.sync.dma_start(out=out0_planes[:, t, :], in_=window[t % WINDOWS][:])
-
         def code_grad(g, s, copy):
-            rows = out_1[0, g * KP : (g + 1) * KP, :].rearrange("(m s) i -> m s i", s=PACK)
-            bank = new_bank([P, N])
+            rows = out_1[0, g * KP : (g + 1) * KP, :].rearrange("(s m) i -> m s i", m=P)
+            bank = new_bank(1, N)[:, 0, :]
             mm(bank[:], cols(ed_mx[g], s * P, (s + 1) * P), E5M2, cols(wd_mx, 0, N))
             if s % 2 == 0:
                 gz[g, s // 2] = ring.tile([P, 2, N], F32, name="gz", bufs=4)
             copy(out=gz[g, s // 2][:, s % 2, :], in_=bank[:])
             if s % 2 == 1:
-                nc.sync.dma_start(out=rows[:, s - 1 : s + 1, :], in_=gz[g, s // 2][:])
+                nc.scalar.dma_start(out=rows[:, s - 1 : s + 1, :], in_=gz[g, s // 2][:])
 
+        load_table(0)
         nc.sync.dma_start(offsets[:], offs)
         nc.scalar.dma_start(out=wt_rows[:], in_=wt[0].rearrange("(g p s) o -> p g (s o)", p=P, s=PACK))
         nc.scalar.dma_start(out=cs_cols[:], in_=cs[0].rearrange("(p t) -> p t", t=PACK))
         make_identity(nc, ident[:])
-        load_table(0)
-        zero(2, nc.gpsimd)
-        zero(0, nc.vector)
-        load_table(1)
-        gather(0)
-        round_atoms(0, vcopy)
-        zero(1, nc.vector)
+        grouped = {("zT", 0): words[0], ("zT", 1): words[1], ("zm", 0): words[2], ("zm", 1): words[3], ("wd", 0): words[2], ("ed", 0): words[4], ("ed", 1): words[5]}
+        for t in range(1, PACK - 1):
+            load_table(t)
         load_zT(0)
-        group("zT", 0, 0, gcopy)
-        turn_atoms(0, vcopy)
-        group("zT", 0, 1, scopy)
-        load_table(3)
-        gather(1)
-        load_table(2)
-        quant("zT", 0, 0, 2)
-        spread_wt(0)
-        gather(3)
-        round_atoms(1, scopy)
-        turn_atoms(1, vcopy)
-        quant_wi(0)
-        gather(2)
-        round_atoms(3, scopy)
-        turn_atoms(3, scopy)
+        load_table(PACK - 1)
         load_xm(0)
         load_zT(1)
-        round_atoms(2, scopy)
-        quant("zT", 0, 1, 2)
-        group("wd", 0, 0, vcopy)
-        group("wd", 0, 1, vcopy)
-        residual(0, 0, 0)
-        turn_atoms(2, scopy)
-        quant_wi(1)
         load_xm(1)
-        residual(0, 0, 1)
-        spread_wt(1)
-        load_zm(1)
-        group("zT", 1, 0, gcopy)
-        group("zT", 1, 1, scopy)
-        load_zm(0)
-        residual(1, 0, 0)
-        residual(1, 0, 1)
-        quant("zT", 1, 1, 2)
-        squash(1, 0)
-        quant("zT", 1, 0, 2)
-        weigh(1, 0, nc.vector)
-        squash(0, 0)
-        residual(0, 1, 1)
-        squash(3, 0)
-        group("zm", 1, 0, scopy)
-        group("zm", 1, 1, gcopy)
-        quant("wd", 0, 0, 1)
-        residual(1, 1, 0)
-        squash(2, 0)
-        residual(0, 1, 0)
-        group("zm", 0, 0, gcopy)
-        weigh(0, 0, nc.vector)
-        residual(1, 1, 1)
-        weigh(3, 0, nc.vector)
-        squash(0, 1)
-        weigh(2, 0, nc.vector)
-        group("zm", 0, 1, scopy)
-        squash(2, 1)
-        turn_error(0, 0, scopy)
-        weigh(0, 1, nc.vector)
-        squash(1, 1)
-        group("ed", 0, 0, vcopy)
-        turn_error(2, 0, scopy)
-        quant("zm", 0, 0, 1)
-        turn_error(0, 1, scopy)
-        group("ed", 0, 1, scopy)
-        quant("zm", 1, 0, 1)
-        squash(3, 1)
-        quant("ed", 0, 0, 2)
-        code_grad(0, 0, scopy)
-        weigh(2, 1, nc.vector)
-        quant_er(0)
-        turn_error(2, 1, scopy)
-        weigh(1, 1, nc.vector)
-        code_grad(0, 1, scopy)
-        atom_grad(0, scopy)
-        quant("ed", 0, 1, 2)
-        code_grad(0, 2, scopy)
-        code_grad(0, 3, scopy)
-        weigh(3, 1, nc.vector)
-        group("ed", 1, 0, vcopy)
-        quant_er(2)
-        quant("ed", 1, 0, 2)
-        turn_error(1, 1, scopy)
-        code_grad(1, 0, scopy)
+        for g in range(G):
+            load_zm(g)
+        for t in range(WINDOWS):
+            zero(t, nc.vector)
+
+        def atoms_pair(u):
+            for t in (2 * u, 2 * u + 1):
+                gather(t)
+                turn_atoms(t, scopy)
+            quant_wi(u)
+
+        def halves(what, g, first, second):
+            group(what, g, 0, HALF, first)
+            group(what, g, HALF, KP, second)
+            quant(what, g, 0, HALF)
+            quant(what, g, HALF, KP)
+
+        def residuals(u, g):
+            for h in range(2):
+                residual(u, g, h)
+
+        def errors(u, g):
+            for t in (2 * u, 2 * u + 1):
+                squash(t, g)
+                weigh(t, g)
+            for t in (2 * u, 2 * u + 1):
+                turn_error(t, g, scopy)
+
+        def code_grads(g):
+            for s in range(PACK):
+                code_grad(g, s, scopy)
+
+        def error(t, g):
+            squash(t, g)
+            weigh(t, g)
+
+        atoms_pair(0)
+        for g in range(G):
+            spread_wt(g)
+        halves("zT", 0, vcopy, vcopy)
+        atoms_pair(1)
+        group("wd", 0, 0, HALF, gcopy)
+        group("wd", 0, HALF, KP, scopy)
+        for u in range(2):
+            residuals(u, 0)
+        quant("wd", 0, 0, KP)
+        halves("zT", 1, gcopy, scopy)
+        for t in range(PACK):
+            error(t, 0)
+        residuals(0, 1)
+        for t in range(2):
+            turn_error(t, 0, scopy)
+        residuals(1, 1)
+        for t in range(2, PACK):
+            turn_error(t, 0, scopy)
+        group("zm", 0, 0, HALF, gcopy)
+        group("zm", 0, HALF, KP, scopy)
+        quant("zm", 0, 0, KP)
+        for t in range(2):
+            error(t, 1)
+        halves("zm", 1, gcopy, scopy)
+        for t in range(2, PACK):
+            error(t, 1)
+        for t in range(PACK):
+            turn_error(t, 1, scopy)
+            quant_er(t)
+        sum_bank = taken[-2]
+        rotation.remove(sum_bank)
+        atom_grad(0, scopy, sum_bank)
+        group("ed", 0, 0, HALF, scopy)
+        group("ed", 0, HALF, KP, scopy)
+        group("ed", 1, 0, KP, gcopy)
         scatter(0)
-        turn_error(1, 0, scopy)
-        group("ed", 1, 1, scopy)
-        quant_er(1)
-        atom_grad(2, scopy)
-        code_grad(1, 1, scopy)
-        turn_error(3, 0, scopy)
-        quant("ed", 1, 1, 2)
-        code_grad(1, 2, scopy)
-        code_grad(1, 3, scopy)
-        scatter(2)
-        turn_error(3, 1, scopy)
-        quant_er(3)
-        atom_grad(1, scopy)
-        atom_grad(3, scopy)
+        for g in range(G):
+            quant("ed", g, 0, KP)
+        atom_grad(1, scopy, sum_bank)
         scatter(1)
+        atom_grad(2, scopy, sum_bank)
+        code_grads(0)
+        scatter(2)
+        atom_grad(3, scopy, sum_bank)
+        code_grads(1)
         scatter(3)

@@ -78,11 +78,12 @@ def tile_attend_gdi_lch_wz_kernel(tc, zT, wT, xm, wt, zm, cs, offs, out_0, out_1
         window = [held("window%d" % t, [P, T], F32) for t in range(WINDOWS)]
         ident = held("ident", [P, P], F32)
         atoms_bf = held("atoms_bf", [P, PACK * N], BF16)[:].rearrange("p (t i) -> p t i", t=PACK)
-        wi_bf = [held("wi_bf%d" % u, [P, 2 * P * PACK], BF16) for u in range(2)]
         e_planes = [held("e_planes%d" % g, [P, PACK * KP], BF16)[:].rearrange("p (t r) -> p t r", t=PACK) for g in range(G)]
         th_tiles = [held("th%d" % t, [P, KP], F32) for t in range(PACK)]
-        words = [held("words%d" % k, [P, KP * PACK], BF16) for k in range(6)]
-        er_bf = [words[k][:, h * G * KP : (h + 1) * G * KP] for k, h in ((5, 1), (4, 1), (4, 0), (5, 0))]
+        words = [held("words%d" % k, [P, KP * PACK], BF16) for k in range(5)]
+        wi_bf = [held("wi_bf0", [P, 2 * P * PACK], BF16), words[4][:, 2 * P * PACK :]]
+        late = held("late", [P, KP * PACK], BF16)
+        er_bf = [held("er_bf%d" % t, [P, G * KP], BF16)[:] for t in range(2)] + [late[:, a * KP : (a + G) * KP] for a in (0, 2)]
         dw = [held("dw%d" % t, [P, N], F32)[:] for t in range(PACK)]
         wi_mx = [mx_operand("wi%d" % u, 2 * P) for u in range(2)]
         zT_mx = [mx_operand("zT%d" % g, KP) for g in range(G)]
@@ -141,8 +142,11 @@ def tile_attend_gdi_lch_wz_kernel(tc, zT, wT, xm, wt, zm, cs, offs, out_0, out_1
         def quant_wi(u):
             quantize(cols(wi_mx[u], 0, 2 * P), E4M3, wi_bf[u][:])
 
+        def staged(what, g, a, b):
+            return grouped.get((what, g, a), grouped[what, g])[:, a * PACK : b * PACK]
+
         def group(what, g, a, b, copy):
-            dst = grouped[what, g][:, a * PACK : b * PACK].rearrange("p (c t) -> p c t", t=PACK)
+            dst = staged(what, g, a, b).rearrange("p (c t) -> p c t", t=PACK)
             src = planes[what][g][:, :, a:b]
             if copy is gcopy:
                 copy(out=dst, in_=src.rearrange("p t c -> p c t"))
@@ -151,7 +155,7 @@ def tile_attend_gdi_lch_wz_kernel(tc, zT, wT, xm, wt, zm, cs, offs, out_0, out_1
 
         def quant(what, g, a, b):
             fmt = E5M2 if what == "ed" else E4M3
-            quantize(cols(operand[what][g], a, b), fmt, grouped[what, g][:, a * PACK : b * PACK])
+            quantize(cols(operand[what][g], a, b), fmt, staged(what, g, a, b))
 
         def residual(u, g, h):
             bank = new_bank(2, 2 * P)
@@ -220,7 +224,11 @@ def tile_attend_gdi_lch_wz_kernel(tc, zT, wT, xm, wt, zm, cs, offs, out_0, out_1
         nc.scalar.dma_start(out=wt_rows[:], in_=wt[0].rearrange("(g p s) o -> p g (s o)", p=P, s=PACK))
         nc.scalar.dma_start(out=cs_cols[:], in_=cs[0].rearrange("(p t) -> p t", t=PACK))
         make_identity(nc, ident[:])
-        grouped = {("zT", 0): words[0], ("zT", 1): words[1], ("zm", 0): words[2], ("zm", 1): words[3], ("wd", 0): words[2], ("ed", 0): words[4], ("ed", 1): words[5]}
+        grouped = {("zT", 0): words[0], ("zT", 1): words[1], ("zm", 0): words[2], ("zm", 1): words[3]}
+        grouped["wd", 0] = words[4]
+        grouped["ed", 0] = words[0]
+        grouped["ed", 0, HALF] = words[3]
+        grouped["ed", 1] = late
         for t in range(1, PACK - 1):
             load_table(t)
         load_zT(0)
@@ -269,44 +277,46 @@ def tile_attend_gdi_lch_wz_kernel(tc, zT, wT, xm, wt, zm, cs, offs, out_0, out_1
             spread_wt(g)
         halves("zT", 0, vcopy, vcopy)
         atoms_pair(1)
-        group("wd", 0, 0, HALF, gcopy)
+        group("wd", 0, 0, HALF, vcopy)
         group("wd", 0, HALF, KP, scopy)
         for u in range(2):
             residuals(u, 0)
-        quant("wd", 0, 0, KP)
         halves("zT", 1, gcopy, scopy)
+        quant("wd", 0, 0, KP)
+        group("zm", 0, 0, KP, gcopy)
         for t in range(PACK):
             error(t, 0)
         residuals(0, 1)
         for t in range(2):
             turn_error(t, 0, scopy)
         residuals(1, 1)
-        for t in range(2, PACK):
-            turn_error(t, 0, scopy)
-        group("zm", 0, 0, HALF, gcopy)
-        group("zm", 0, HALF, KP, scopy)
+        error(0, 1)
+        turn_error(0, 1, scopy)
+        quant_er(0)
+        error(1, 1)
+        halves("zm", 1, vcopy, scopy)
         quant("zm", 0, 0, KP)
-        for t in range(2):
-            error(t, 1)
-        halves("zm", 1, gcopy, scopy)
-        for t in range(2, PACK):
-            error(t, 1)
-        for t in range(PACK):
-            turn_error(t, 1, scopy)
-            quant_er(t)
         sum_bank = taken[-2]
         rotation.remove(sum_bank)
         atom_grad(0, scopy, sum_bank)
-        group("ed", 0, 0, HALF, scopy)
-        group("ed", 0, HALF, KP, scopy)
-        group("ed", 1, 0, KP, gcopy)
+        for t in range(2, PACK):
+            error(t, 1)
+        turn_error(1, 1, scopy)
+        quant_er(1)
+        halves("ed", 0, scopy, scopy)
+        for t in range(2, PACK):
+            for g in range(G):
+                turn_error(t, g, scopy)
+        code_grads(0)
         scatter(0)
-        for g in range(G):
-            quant("ed", g, 0, KP)
+        for t in range(2, PACK):
+            quant_er(t)
         atom_grad(1, scopy, sum_bank)
         scatter(1)
+        group("ed", 1, 0, HALF, scopy)
+        group("ed", 1, HALF, KP, scopy)
+        quant("ed", 1, 0, KP)
         atom_grad(2, scopy, sum_bank)
-        code_grads(0)
         scatter(2)
         atom_grad(3, scopy, sum_bank)
         code_grads(1)

@@ -36,7 +36,7 @@ def tile_attend_gdi_lch_wz_kernel(tc, zT, wT, xm, wt, zm, cs, offs, out_0, out_1
         psum = ctx.enter_context(tc.psum_pool(name="psum", bufs=2))
 
         def held(name, shape, dtype):
-            return keep.tile(shape, dtype, name=name, align_bytes=64)
+            return keep.tile(shape, dtype, name=name, align_bytes=256)
 
         banks = [psum.tile([P, KP], F32, name="bank%d" % b, bufs=1) for b in range(BANKS)]
         rotation, taken = list(range(BANKS)), []
@@ -80,17 +80,19 @@ def tile_attend_gdi_lch_wz_kernel(tc, zT, wT, xm, wt, zm, cs, offs, out_0, out_1
         atoms_bf = held("atoms_bf", [P, PACK * N], BF16)[:].rearrange("p (t i) -> p t i", t=PACK)
         e_planes = [held("e_planes%d" % g, [P, PACK * KP], BF16)[:].rearrange("p (t r) -> p t r", t=PACK) for g in range(G)]
         th_tiles = [held("th%d" % t, [P, KP], F32) for t in range(PACK)]
-        words = [held("words%d" % k, [P, KP * PACK], BF16) for k in range(5)]
-        wi_bf = [held("wi_bf0", [P, 2 * P * PACK], BF16), words[4][:, 2 * P * PACK :]]
+        words = [held("words%d" % k, [P, KP * PACK], BF16) for k in range(2)]
+        early = held("early", [P, 7 * HALF * PACK], BF16)
+        wi_bf = [held("wi_bf0", [P, 2 * P * PACK], BF16), early[:, : HALF * PACK]]
         late = held("late", [P, KP * PACK], BF16)
         er_bf = [held("er_bf%d" % t, [P, G * KP], BF16)[:] for t in range(2)] + [late[:, a * KP : (a + G) * KP] for a in (0, 2)]
         dw = [held("dw%d" % t, [P, N], F32)[:] for t in range(PACK)]
-        wi_mx = [mx_operand("wi%d" % u, 2 * P) for u in range(2)]
-        zT_mx = [mx_operand("zT%d" % g, KP) for g in range(G)]
+        early_mx = mx_operand("early", 7 * HALF)
+        wi_mx = [mx_operand("wi0", 2 * P), cols(early_mx, 0, HALF)]
+        zT_mx = [cols(early_mx, a * HALF, (a + 2) * HALF) for a in (1, 5)]
         zm_mx = [mx_operand("zm%d" % g, N) for g in range(G)]
         pair_mx = [mx_operand("pair%d" % u, N) for u in range(2)]
         er_mx = [cols(pair_mx[t // 2], t % 2 * G * P, (t % 2 + 1) * G * P) for t in range(PACK)]
-        wd_mx = mx_operand("wd", N)
+        wd_mx = cols(early_mx, 3 * HALF, 5 * HALF)
         ed_mx = [mx_operand("ed%d" % g, KP) for g in range(G)]
         planes = {"zT": zT_raw, "zm": zm_raw, "wd": [atoms_bf], "ed": e_planes}
         operand = {"zT": zT_mx, "zm": zm_mx, "wd": [wd_mx], "ed": ed_mx}
@@ -162,7 +164,7 @@ def tile_attend_gdi_lch_wz_kernel(tc, zT, wT, xm, wt, zm, cs, offs, out_0, out_1
             for c in range(2):
                 first = (2 * h + c) * P
                 mm(bank[:, c, :], cols(zT_mx[g], first, first + P), E4M3, cols(wi_mx[u], 0, 2 * P))
-            diff[u, g, h] = ring.tile([P, 2, 2 * P], F32, name="diff", bufs=8)
+            diff[u, g, h] = ring.tile([P, 2, 2 * P], F32, name="diff", bufs=8, align_bytes=256)
             rows = xm_raw[g][:, 2 * h : 2 * h + 2, :].rearrange("p c d -> p (c d)")
             nc.vector.tensor_tensor(
                 diff[u, g, h][:].rearrange("p e (n k) -> p n e k", k=2),
@@ -171,9 +173,9 @@ def tile_attend_gdi_lch_wz_kernel(tc, zT, wT, xm, wt, zm, cs, offs, out_0, out_1
                 SUB,
             )
 
-        def squash(t, g):
+        def squash(t, g, bank=None):
             u, e = divmod(t, 2)
-            bank = new_bank(PACK, P)
+            bank = new_bank(PACK, P, bank)
             for c in range(PACK):
                 nc.tensor.transpose(bank[:, c, :], diff[u, g, c // 2][:, e, (c % 2) * P : (c % 2 + 1) * P], ident[:])
             th[t, g] = th_tiles[t]
@@ -199,6 +201,12 @@ def tile_attend_gdi_lch_wz_kernel(tc, zT, wT, xm, wt, zm, cs, offs, out_0, out_1
         def quant_er(t):
             quantize(cols(er_mx[t], 0, G * P), E5M2, er_bf[t])
 
+        def quant_early(a, b):
+            quantize(cols(early_mx, a * HALF, b * HALF), E4M3, early[:, a * HALF * PACK : b * HALF * PACK])
+
+        def quant_late_er():
+            quantize(pair_mx[1], E5M2, late[:])
+
         def atom_grad(t, copy, bank):
             bank = new_bank(1, N, bank)[:, 0, :]
             for g in range(G):
@@ -214,7 +222,7 @@ def tile_attend_gdi_lch_wz_kernel(tc, zT, wT, xm, wt, zm, cs, offs, out_0, out_1
             bank = new_bank(1, N)[:, 0, :]
             mm(bank[:], cols(ed_mx[g], s * P, (s + 1) * P), E5M2, cols(wd_mx, 0, N))
             if s % 2 == 0:
-                gz[g, s // 2] = ring.tile([P, 2, N], F32, name="gz", bufs=4)
+                gz[g, s // 2] = ring.tile([P, 2, N], F32, name="gz", bufs=4, align_bytes=256)
             copy(out=gz[g, s // 2][:, s % 2, :], in_=bank[:])
             if s % 2 == 1:
                 nc.scalar.dma_start(out=rows[:, s - 1 : s + 1, :], in_=gz[g, s // 2][:])
@@ -224,18 +232,17 @@ def tile_attend_gdi_lch_wz_kernel(tc, zT, wT, xm, wt, zm, cs, offs, out_0, out_1
         nc.scalar.dma_start(out=wt_rows[:], in_=wt[0].rearrange("(g p s) o -> p g (s o)", p=P, s=PACK))
         nc.scalar.dma_start(out=cs_cols[:], in_=cs[0].rearrange("(p t) -> p t", t=PACK))
         make_identity(nc, ident[:])
-        grouped = {("zT", 0): words[0], ("zT", 1): words[1], ("zm", 0): words[2], ("zm", 1): words[3]}
-        grouped["wd", 0] = words[4]
-        grouped["ed", 0] = words[0]
-        grouped["ed", 0, HALF] = words[3]
+        grouped = {("zm", 0): words[0], ("zm", 1): words[1]}
+        for key, a in ((("zT", 0), 1), (("wd", 0), 3), (("zT", 1), 5)):
+            grouped[key] = early[:, a * HALF * PACK : (a + 2) * HALF * PACK]
+        grouped["ed", 0] = grouped["zT", 0]
+        grouped["ed", 0, HALF] = words[1]
         grouped["ed", 1] = late
-        for t in range(1, PACK - 1):
+        for t in range(1, PACK):
             load_table(t)
-        load_zT(0)
-        load_table(PACK - 1)
-        load_xm(0)
-        load_zT(1)
-        load_xm(1)
+        for g in range(G):
+            load_zT(g)
+            load_xm(g)
         for g in range(G):
             load_zm(g)
         for t in range(WINDOWS):
@@ -275,14 +282,22 @@ def tile_attend_gdi_lch_wz_kernel(tc, zT, wT, xm, wt, zm, cs, offs, out_0, out_1
         atoms_pair(0)
         for g in range(G):
             spread_wt(g)
-        halves("zT", 0, vcopy, vcopy)
-        atoms_pair(1)
+        for t in range(2, PACK):
+            gather(t)
+            turn_atoms(t, scopy)
+        group("zT", 0, 0, HALF, vcopy)
+        group("zT", 0, HALF, KP, scopy)
         group("wd", 0, 0, HALF, vcopy)
         group("wd", 0, HALF, KP, scopy)
-        for u in range(2):
-            residuals(u, 0)
-        halves("zT", 1, gcopy, scopy)
-        quant("wd", 0, 0, KP)
+        quant_early(0, 2)
+        quant_early(2, 4)
+        for h in range(2):
+            for u in range(2):
+                residual(u, 0, h)
+        group("zT", 1, 0, HALF, gcopy)
+        group("zT", 1, HALF, KP, scopy)
+        quant_early(4, 6)
+        quant_early(6, 7)
         group("zm", 0, 0, KP, gcopy)
         for t in range(PACK):
             error(t, 0)
@@ -309,8 +324,7 @@ def tile_attend_gdi_lch_wz_kernel(tc, zT, wT, xm, wt, zm, cs, offs, out_0, out_1
                 turn_error(t, g, scopy)
         code_grads(0)
         scatter(0)
-        for t in range(2, PACK):
-            quant_er(t)
+        quant_late_er()
         atom_grad(1, scopy, sum_bank)
         scatter(1)
         group("ed", 1, 0, HALF, scopy)

@@ -320,18 +320,22 @@ def tile_attend_gdi_lch_wz_kernel(tc, zT, wT, xm, wt, zm, cs, offs, out_0, out_1
         quant_er(1)
         halves("ed", 0, scopy, scopy)
         for t in range(2, PACK):
-            for g in range(G):
-                turn_error(t, g, scopy)
-        code_grads(0)
+            turn_error(t, 0, scopy)
+        for s in range(2):
+            code_grad(0, s, scopy)
+        for t in range(2, PACK):
+            turn_error(t, 1, scopy)
         scatter(0)
         quant_late_er()
         atom_grad(1, scopy, sum_bank)
+        for s in range(2, PACK):
+            code_grad(0, s, scopy)
         scatter(1)
         group("ed", 1, 0, HALF, scopy)
         group("ed", 1, HALF, KP, scopy)
         quant("ed", 1, 0, KP)
         atom_grad(2, scopy, sum_bank)
         scatter(2)
-        atom_grad(3, scopy, sum_bank)
+        atom_grad(3, scopy, None)
         code_grads(1)
         scatter(3)

@@ -115,9 +115,9 @@ def tile_attend_gdi_lch_wz_kernel(tc, zT, wT, xm, wt, zm, cs, offs, out_0, out_1
             nc.sync.dma_start(out=zm_raw[g][:], in_=zm[0, g * KP : (g + 1) * KP, :].rearrange("(p j) i -> p j i", j=PACK))
 
         def spread_wt(g):
-            wt_bank[g] = psum.tile([P, PACK, P], F32, name="wt_bank")
+            wt_bank[g] = psum.tile([P, KP], F32, name="wt_bank")
             for s in range(PACK):
-                nc.tensor.transpose(wt_bank[g][:, s, :], wt_rows[:, g, s : s + 1].to_broadcast([P, P]), ident[:])
+                nc.tensor.transpose(wt_bank[g][:, s:KP:PACK], wt_rows[:, g, s : s + 1].to_broadcast([P, P]), ident[:])
 
         def zero(t, engine):
             engine.memset(window[t][:], 0.0)
@@ -167,9 +167,9 @@ def tile_attend_gdi_lch_wz_kernel(tc, zT, wT, xm, wt, zm, cs, offs, out_0, out_1
             diff[u, g, h] = ring.tile([P, 2, 2 * P], F32, name="diff", bufs=8, align_bytes=256)
             rows = xm_raw[g][:, 2 * h : 2 * h + 2, :].rearrange("p c d -> p (c d)")
             nc.vector.tensor_tensor(
-                diff[u, g, h][:].rearrange("p e (n k) -> p n e k", k=2),
-                bank[:].rearrange("p c m -> p (c m)").rearrange("p (n e k) -> p n e k", e=2, k=2),
-                rows.rearrange("p (n k u e) -> p u n e k", k=2, u=2, e=2)[:, u],
+                diff[u, g, h][:].rearrange("p c (n k e) -> p (c n) k e", k=2, e=2),
+                bank[:].rearrange("p c (n e k) -> p (c n) k e", e=2, k=2),
+                rows.rearrange("p (n k u e) -> p u n k e", k=2, u=2, e=2)[:, u],
                 SUB,
             )
 
@@ -177,16 +177,16 @@ def tile_attend_gdi_lch_wz_kernel(tc, zT, wT, xm, wt, zm, cs, offs, out_0, out_1
             u, e = divmod(t, 2)
             bank = new_bank(PACK, P, bank)
             for c in range(PACK):
-                nc.tensor.transpose(bank[:, c, :], diff[u, g, c // 2][:, e, (c % 2) * P : (c % 2 + 1) * P], ident[:])
+                nc.tensor.transpose(bank[:, c, :], diff[u, g, c // 2][:, c % 2, e : 2 * P : 2], ident[:])
             th[t, g] = th_tiles[t]
             nc.scalar.activation(th[t, g][:], bank[:].rearrange("p c r -> p (c r)"), TANH, scale=cs_cols[:, t : t + 1])
 
         def weigh(t, g):
             nc.vector.scalar_tensor_tensor(
-                e_planes[g][:, t, :].rearrange("p (m s) -> p m s", s=PACK),
-                th[t, g][:].rearrange("p (m s) -> p m s", s=PACK),
+                e_planes[g][:, t, :],
+                th[t, g][:],
                 cs_cols[:, t : t + 1],
-                wt_bank[g][:].rearrange("p s m -> p m s"),
+                wt_bank[g][:],
                 MULT,
                 MULT,
             )

@@ -25,7 +25,7 @@ KP = P * PACK
 G = R // KP
 HALF = KP // 2
 WINDOWS = 3
-BANKS = 6
+BANKS = 8
 
 
 def tile_attend_gdi_lch_wz_kernel(tc, zT, wT, xm, wt, zm, cs, offs, out_0, out_1):
@@ -39,12 +39,8 @@ def tile_attend_gdi_lch_wz_kernel(tc, zT, wT, xm, wt, zm, cs, offs, out_0, out_1
             return keep.tile(shape, dtype, name=name, align_bytes=256)
 
         banks = [psum.tile([P, KP], F32, name="bank%d" % b, bufs=1) for b in range(BANKS)]
-        rotation, taken = list(range(BANKS)), []
 
-        def new_bank(parts, width, bank=None):
-            if bank is None:
-                bank = rotation[len(taken) % len(rotation)]
-                taken.append(bank)
+        def new_bank(parts, width, bank):
             return banks[bank][:, : parts * width].rearrange("p (a b) -> p a b", a=parts)
 
         def mx_operand(name, width):
@@ -79,21 +75,23 @@ def tile_attend_gdi_lch_wz_kernel(tc, zT, wT, xm, wt, zm, cs, offs, out_0, out_1
         ident = held("ident", [P, P], F32)
         atoms_bf = held("atoms_bf", [P, PACK * N], BF16)[:].rearrange("p (t i) -> p t i", t=PACK)
         e_planes = [held("e_planes%d" % g, [P, PACK * KP], BF16)[:].rearrange("p (t r) -> p t r", t=PACK) for g in range(G)]
-        th_tiles = [held("th%d" % t, [P, KP], F32) for t in range(PACK)]
-        words = [held("words%d" % k, [P, KP * PACK], BF16) for k in range(2)]
+        th_tiles = [zT_raw[k // PACK][:, k % PACK, :] for k in range(G * PACK)]
+        zm_words = held("zm_words", [P, G * N * PACK], BF16)
+        last = held("last", [P, 5 * HALF * PACK], BF16)
         early = held("early", [P, 7 * HALF * PACK], BF16)
         wi_bf = [held("wi_bf0", [P, 2 * P * PACK], BF16), early[:, : HALF * PACK]]
-        late = held("late", [P, KP * PACK], BF16)
-        er_bf = [held("er_bf%d" % t, [P, G * KP], BF16)[:] for t in range(2)] + [late[:, a * KP : (a + G) * KP] for a in (0, 2)]
+        er_bf = [held("er_bf0", [P, G * KP], BF16)[:]] + [last[:, a * G * KP : (a + 1) * G * KP] for a in (1, 3, 4)]
         dw = [held("dw%d" % t, [P, N], F32)[:] for t in range(PACK)]
         early_mx = mx_operand("early", 7 * HALF)
         wi_mx = [mx_operand("wi0", 2 * P), cols(early_mx, 0, HALF)]
         zT_mx = [cols(early_mx, a * HALF, (a + 2) * HALF) for a in (1, 5)]
-        zm_mx = [mx_operand("zm%d" % g, N) for g in range(G)]
-        pair_mx = [mx_operand("pair%d" % u, N) for u in range(2)]
-        er_mx = [cols(pair_mx[t // 2], t % 2 * G * P, (t % 2 + 1) * G * P) for t in range(PACK)]
+        zm_both = mx_operand("zm", G * N)
+        zm_mx = [cols(zm_both, g * N, (g + 1) * N) for g in range(G)]
+        last_mx = mx_operand("last", KP + N)
+        mid_mx = mx_operand("mid", KP)
+        er_mx = [mx_operand("er0", HALF), cols(mid_mx, HALF, KP), cols(last_mx, KP, KP + HALF), cols(last_mx, KP + HALF, 2 * KP)]
         wd_mx = cols(early_mx, 3 * HALF, 5 * HALF)
-        ed_mx = [mx_operand("ed%d" % g, KP) for g in range(G)]
+        ed_mx = [[cols(mid_mx, 0, HALF), mx_operand("ed0b", HALF)], [cols(last_mx, 0, HALF), cols(last_mx, HALF, KP)]]
         planes = {"zT": zT_raw, "zm": zm_raw, "wd": [atoms_bf], "ed": e_planes}
         operand = {"zT": zT_mx, "zm": zm_mx, "wd": [wd_mx], "ed": ed_mx}
         wt_bank, diff, th, gz = {}, {}, {}, {}
@@ -114,8 +112,8 @@ def tile_attend_gdi_lch_wz_kernel(tc, zT, wT, xm, wt, zm, cs, offs, out_0, out_1
         def load_zm(g):
             nc.sync.dma_start(out=zm_raw[g][:], in_=zm[0, g * KP : (g + 1) * KP, :].rearrange("(p j) i -> p j i", j=PACK))
 
-        def spread_wt(g):
-            wt_bank[g] = psum.tile([P, KP], F32, name="wt_bank")
+        def spread_wt(g, b):
+            wt_bank[g] = banks[b]
             for s in range(PACK):
                 nc.tensor.transpose(wt_bank[g][:, s:KP:PACK], wt_rows[:, g, s : s + 1].to_broadcast([P, P]), ident[:])
 
@@ -125,16 +123,16 @@ def tile_attend_gdi_lch_wz_kernel(tc, zT, wT, xm, wt, zm, cs, offs, out_0, out_1
         def gather(t):
             nc.vector.tensor_copy(atoms_bf[:, t, :], table[t][:].indirect(offsets[:]))
 
-        def turn_words(plane):
+        def turn_words(plane, b):
             pairs = plane.bitcast(F32)
-            bank = new_bank(2, P)
+            bank = new_bank(2, P, b)
             for v in range(2):
                 nc.tensor.transpose(bank[:, v, :], pairs[:, v : 2 * P : 2], ident[:])
             return bank
 
         def turn_atoms(t, copy):
             u, e = divmod(t, 2)
-            bank = turn_words(atoms_bf[:, t, :])
+            bank = turn_words(atoms_bf[:, t, :], (PACK + t) % 6)
             pairs = wi_bf[u][:].bitcast(F32)
             copy(
                 out=pairs.rearrange("p (n e k v) -> p e n k v", e=2, k=2, v=2)[:, e],
@@ -145,7 +143,9 @@ def tile_attend_gdi_lch_wz_kernel(tc, zT, wT, xm, wt, zm, cs, offs, out_0, out_1
             quantize(cols(wi_mx[u], 0, 2 * P), E4M3, wi_bf[u][:])
 
         def staged(what, g, a, b):
-            return grouped.get((what, g, a), grouped[what, g])[:, a * PACK : b * PACK]
+            if (what, g) == ("ed", 0):
+                return last[:, : HALF * PACK]
+            return grouped[what, g][:, a * PACK : b * PACK]
 
         def group(what, g, a, b, copy):
             dst = staged(what, g, a, b).rearrange("p (c t) -> p c t", t=PACK)
@@ -160,7 +160,7 @@ def tile_attend_gdi_lch_wz_kernel(tc, zT, wT, xm, wt, zm, cs, offs, out_0, out_1
             quantize(cols(operand[what][g], a, b), fmt, staged(what, g, a, b))
 
         def residual(u, g, h):
-            bank = new_bank(2, 2 * P)
+            bank = new_bank(2, 2 * P, (PACK * g + 2 * u + h) % 6)
             for c in range(2):
                 first = (2 * h + c) * P
                 mm(bank[:, c, :], cols(zT_mx[g], first, first + P), E4M3, cols(wi_mx[u], 0, 2 * P))
@@ -173,12 +173,12 @@ def tile_attend_gdi_lch_wz_kernel(tc, zT, wT, xm, wt, zm, cs, offs, out_0, out_1
                 SUB,
             )
 
-        def squash(t, g, bank=None):
+        def squash(t, g, bank):
             u, e = divmod(t, 2)
             bank = new_bank(PACK, P, bank)
             for c in range(PACK):
                 nc.tensor.transpose(bank[:, c, :], diff[u, g, c // 2][:, c % 2, e : 2 * P : 2], ident[:])
-            th[t, g] = th_tiles[t]
+            th[t, g] = th_tiles[PACK * g + t]
             nc.scalar.activation(th[t, g][:], bank[:].rearrange("p c r -> p (c r)"), TANH, scale=cs_cols[:, t : t + 1])
 
         def weigh(t, g):
@@ -191,8 +191,8 @@ def tile_attend_gdi_lch_wz_kernel(tc, zT, wT, xm, wt, zm, cs, offs, out_0, out_1
                 MULT,
             )
 
-        def turn_error(t, g, copy):
-            bank = turn_words(e_planes[g][:, t, :])
+        def turn_error(t, g, copy, b):
+            bank = turn_words(e_planes[g][:, t, :], b)
             copy(
                 out=er_bf[t][:, g * KP : (g + 1) * KP].bitcast(F32).rearrange("p (m v) -> p m v", v=2),
                 in_=bank[:].rearrange("p v m -> p m v"),
@@ -205,7 +205,7 @@ def tile_attend_gdi_lch_wz_kernel(tc, zT, wT, xm, wt, zm, cs, offs, out_0, out_1
             quantize(cols(early_mx, a * HALF, b * HALF), E4M3, early[:, a * HALF * PACK : b * HALF * PACK])
 
         def quant_late_er():
-            quantize(pair_mx[1], E5M2, late[:])
+            quantize(cols(last_mx, 0, 2 * KP), E5M2, last[:, HALF * PACK :])
 
         def atom_grad(t, copy, bank):
             bank = new_bank(1, N, bank)[:, 0, :]
@@ -217,10 +217,10 @@ def tile_attend_gdi_lch_wz_kernel(tc, zT, wT, xm, wt, zm, cs, offs, out_0, out_1
             nc.vector.tensor_copy(window[t % WINDOWS][:].indirect(offsets[:]), dw[t])
             nc.sync.dma_start(out=out0_planes[:, t, :], in_=window[t % WINDOWS][:])
 
-        def code_grad(g, s, copy):
+        def code_grad(g, s, copy, b):
             rows = out_1[0, g * KP : (g + 1) * KP, :].rearrange("(s m) i -> m s i", m=P)
-            bank = new_bank(1, N)[:, 0, :]
-            mm(bank[:], cols(ed_mx[g], s * P, (s + 1) * P), E5M2, cols(wd_mx, 0, N))
+            bank = new_bank(1, N, b)[:, 0, :]
+            mm(bank[:], cols(ed_mx[g][s // 2], s % 2 * P, (s % 2 + 1) * P), E5M2, cols(wd_mx, 0, N))
             if s % 2 == 0:
                 gz[g, s // 2] = ring.tile([P, 2, N], F32, name="gz", bufs=4, align_bytes=256)
             copy(out=gz[g, s // 2][:, s % 2, :], in_=bank[:])
@@ -232,16 +232,15 @@ def tile_attend_gdi_lch_wz_kernel(tc, zT, wT, xm, wt, zm, cs, offs, out_0, out_1
         nc.scalar.dma_start(out=wt_rows[:], in_=wt[0].rearrange("(g p s) o -> p g (s o)", p=P, s=PACK))
         nc.scalar.dma_start(out=cs_cols[:], in_=cs[0].rearrange("(p t) -> p t", t=PACK))
         make_identity(nc, ident[:])
-        grouped = {("zm", 0): words[0], ("zm", 1): words[1]}
+        grouped = {("zm", g): zm_words[:, g * N * PACK : (g + 1) * N * PACK] for g in range(G)}
         for key, a in ((("zT", 0), 1), (("wd", 0), 3), (("zT", 1), 5)):
             grouped[key] = early[:, a * HALF * PACK : (a + 2) * HALF * PACK]
-        grouped["ed", 0] = grouped["zT", 0]
-        grouped["ed", 0, HALF] = words[1]
-        grouped["ed", 1] = late
+        grouped["ed", 1] = last[:, HALF * PACK : 3 * HALF * PACK]
         for t in range(1, PACK):
             load_table(t)
         for g in range(G):
             load_zT(g)
+        for g in range(G):
             load_xm(g)
         for g in range(G):
             load_zm(g)
@@ -264,24 +263,9 @@ def tile_attend_gdi_lch_wz_kernel(tc, zT, wT, xm, wt, zm, cs, offs, out_0, out_1
             for h in range(2):
                 residual(u, g, h)
 
-        def errors(u, g):
-            for t in (2 * u, 2 * u + 1):
-                squash(t, g)
-                weigh(t, g)
-            for t in (2 * u, 2 * u + 1):
-                turn_error(t, g, scopy)
-
-        def code_grads(g):
-            for s in range(PACK):
-                code_grad(g, s, scopy)
-
-        def error(t, g):
-            squash(t, g)
-            weigh(t, g)
-
         atoms_pair(0)
         for g in range(G):
-            spread_wt(g)
+            spread_wt(g, 6 + g)
         for t in range(2, PACK):
             gather(t)
             turn_atoms(t, scopy)
@@ -291,51 +275,54 @@ def tile_attend_gdi_lch_wz_kernel(tc, zT, wT, xm, wt, zm, cs, offs, out_0, out_1
         group("wd", 0, HALF, KP, scopy)
         quant_early(0, 2)
         quant_early(2, 4)
-        for h in range(2):
-            for u in range(2):
-                residual(u, 0, h)
-        group("zT", 1, 0, HALF, gcopy)
+        group("zT", 1, 0, HALF, vcopy)
         group("zT", 1, HALF, KP, scopy)
         quant_early(4, 6)
         quant_early(6, 7)
         group("zm", 0, 0, KP, gcopy)
-        for t in range(PACK):
-            error(t, 0)
-        residuals(0, 1)
-        for t in range(2):
-            turn_error(t, 0, scopy)
-        residuals(1, 1)
-        error(0, 1)
-        turn_error(0, 1, scopy)
+        for g in range(G):
+            for u in range(2):
+                residuals(u, g)
+        for g in range(G):
+            for t in range(2):
+                squash(t, g, 2 + 2 * g + t)
+        for g in range(G):
+            for t in range(2):
+                weigh(t, g)
+            turn_error(0, g, scopy, g)
+        for t in range(2, PACK):
+            squash(t, 0, t)
+            weigh(t, 0)
+        group("zm", 1, 0, HALF, gcopy)
+        group("zm", 1, HALF, KP, vcopy)
+        quantize(cols(zm_both, 0, G * N), E4M3, zm_words[:])
         quant_er(0)
-        error(1, 1)
-        halves("zm", 1, vcopy, scopy)
-        quant("zm", 0, 0, KP)
-        sum_bank = taken[-2]
-        rotation.remove(sum_bank)
-        atom_grad(0, scopy, sum_bank)
+        atom_grad(0, scopy, 1)
+        for g in range(G):
+            turn_error(1, g, scopy, PACK + g)
+        group("ed", 0, 0, HALF, scopy)
+        quantize(cols(mid_mx, 0, KP), E5M2, last[:, : KP * PACK])
         for t in range(2, PACK):
-            error(t, 1)
-        turn_error(1, 1, scopy)
-        quant_er(1)
-        halves("ed", 0, scopy, scopy)
+            squash(t, 1, (0, PACK)[t - 2])
+            weigh(t, 1)
         for t in range(2, PACK):
-            turn_error(t, 0, scopy)
+            turn_error(t, 0, scopy, t)
         for s in range(2):
-            code_grad(0, s, scopy)
+            code_grad(0, s, scopy, 5 + s)
         for t in range(2, PACK):
-            turn_error(t, 1, scopy)
+            turn_error(t, 1, scopy, t)
+        group("ed", 0, HALF, KP, gcopy)
+        group("ed", 1, 0, KP, gcopy)
         scatter(0)
+        quantize(cols(ed_mx[0][1], 0, HALF), E5M2, last[:, : HALF * PACK])
         quant_late_er()
-        atom_grad(1, scopy, sum_bank)
-        for s in range(2, PACK):
-            code_grad(0, s, scopy)
+        atom_grad(1, scopy, 1)
         scatter(1)
-        group("ed", 1, 0, HALF, scopy)
-        group("ed", 1, HALF, KP, scopy)
-        quant("ed", 1, 0, KP)
-        atom_grad(2, scopy, sum_bank)
+        for s in range(2, PACK):
+            code_grad(0, s, scopy, 3 + s)
+        atom_grad(2, scopy, 0)
+        for s in range(PACK):
+            code_grad(1, s, scopy, (2, 3, 4, 7)[s])
         scatter(2)
-        atom_grad(3, scopy, None)
-        code_grads(1)
+        atom_grad(3, scopy, 1)
         scatter(3)

@@ -16,7 +16,6 @@ E5M2 = mybir.dt.float8_e5m2_x4
 MULT = mybir.AluOpType.mult
 ADD = mybir.AluOpType.add
 SUB = mybir.AluOpType.subtract
-COPY = mybir.ActivationFunctionType.Copy
 TANH = mybir.ActivationFunctionType.Tanh
 
 P = 128
@@ -24,34 +23,32 @@ PACK = 4
 KP = P * PACK
 G = R // KP
 HALF = KP // 2
+SLOT = HALF * PACK
 WINDOWS = 3
-BANKS = 8
+WORK_BANKS = 6
 
 
 def tile_attend_gdi_lch_wz_kernel(tc, zT, wT, xm, wt, zm, cs, offs, out_0, out_1):
     nc = tc.nc
     with ExitStack() as ctx:
         keep = ctx.enter_context(tc.tile_pool(name="keep", bufs=1))
-        ring = ctx.enter_context(tc.tile_pool(name="ring", bufs=3))
-        psum = ctx.enter_context(tc.psum_pool(name="psum", bufs=2))
+        ring = ctx.enter_context(tc.tile_pool(name="ring", bufs=1))
+        psum = ctx.enter_context(tc.psum_pool(name="psum", bufs=1))
 
         def held(name, shape, dtype):
             return keep.tile(shape, dtype, name=name, align_bytes=256)
 
-        banks = [psum.tile([P, KP], F32, name="bank%d" % b, bufs=1) for b in range(BANKS)]
-
-        def new_bank(parts, width, bank):
-            return banks[bank][:, : parts * width].rearrange("p (a b) -> p a b", a=parts)
-
         def mx_operand(name, width):
             return held(name + "_codes", [P, width], U32), held(name + "_scales", [P, width], U8)
 
-        def quantize(operand, fmt, grouped):
-            codes, scales = operand
-            nc.vector.quantize_mx(out=codes.bitcast(fmt), scales=scales, in_=grouped)
-
         def cols(operand, a, b):
             return operand[0][:, a:b], operand[1][:, a:b]
+
+        def slots(tile, a, b):
+            return tile[:, a * SLOT : b * SLOT]
+
+        def quantize(operand, fmt, words):
+            nc.vector.quantize_mx(out=operand[0].bitcast(fmt), scales=operand[1], in_=words)
 
         def mm(out, lhsT, lhsT_fmt, rhs, start=True, stop=True):
             nc.tensor.matmul_mx(
@@ -59,10 +56,8 @@ def tile_attend_gdi_lch_wz_kernel(tc, zT, wT, xm, wt, zm, cs, offs, out_0, out_1
                 rhs=rhs[0].bitcast(E4M3), rhs_scale=rhs[1], start=start, stop=stop,
             )
 
-        def gcopy(out, in_):
-            nc.gpsimd.tensor_scalar(out, in_, 1.0, 0.0, MULT, ADD)
-
-        vcopy, scopy = nc.vector.tensor_copy, nc.scalar.copy
+        banks = [psum.tile([P, KP], F32, name="bank%d" % b) for b in range(WORK_BANKS + G)]
+        wt_bank = banks[WORK_BANKS:]
 
         offsets = keep.tile([P, N // 16], U16, name="offsets")
         wt_rows = held("wt_rows", [P, G, PACK], F32)
@@ -73,256 +68,202 @@ def tile_attend_gdi_lch_wz_kernel(tc, zT, wT, xm, wt, zm, cs, offs, out_0, out_1
         xm_raw = [held("xm_raw%d" % g, [P, PACK, D], F32) for g in range(G)]
         window = [held("window%d" % t, [P, T], F32) for t in range(WINDOWS)]
         ident = held("ident", [P, P], F32)
-        atoms_bf = held("atoms_bf", [P, PACK * N], BF16)[:].rearrange("p (t i) -> p t i", t=PACK)
-        e_planes = [held("e_planes%d" % g, [P, PACK * KP], BF16)[:].rearrange("p (t r) -> p t r", t=PACK) for g in range(G)]
-        th_tiles = [zT_raw[k // PACK][:, k % PACK, :] for k in range(G * PACK)]
+        atoms = held("atoms", [P, PACK * N], BF16)[:].rearrange("p (t i) -> p t i", t=PACK)
+        e_planes = [held("e%d" % g, [P, PACK * KP], BF16)[:].rearrange("p (t r) -> p t r", t=PACK) for g in range(G)]
+        th = zT_raw
+
         zm_words = held("zm_words", [P, G * N * PACK], BF16)
-        last = held("last", [P, 5 * HALF * PACK], BF16)
-        early = held("early", [P, 7 * HALF * PACK], BF16)
-        wi_bf = [held("wi_bf0", [P, 2 * P * PACK], BF16), early[:, : HALF * PACK]]
-        er_bf = [held("er_bf0", [P, G * KP], BF16)[:]] + [last[:, a * G * KP : (a + 1) * G * KP] for a in (1, 3, 4)]
-        dw = [held("dw%d" % t, [P, N], F32)[:] for t in range(PACK)]
+        last = held("last", [P, 5 * SLOT], BF16)
+        early = held("early", [P, 7 * SLOT], BF16)
+        wi_words = [held("wi0_words", [P, SLOT], BF16)[:], slots(early, 0, 1)]
+        er_words = [held("er0_words", [P, SLOT], BF16)[:]] + [slots(last, a, a + 1) for a in range(2, 5)]
+        zT_words = [slots(early, 1, 3), slots(early, 5, 7)]
+        wd_words = slots(early, 3, 5)
+        ed_words = [slots(last, 0, 2), slots(last, 1, 3)]
+        dw = [held("dw%d" % t, [P, N], F32) for t in range(PACK)]
+
         early_mx = mx_operand("early", 7 * HALF)
-        wi_mx = [mx_operand("wi0", 2 * P), cols(early_mx, 0, HALF)]
-        zT_mx = [cols(early_mx, a * HALF, (a + 2) * HALF) for a in (1, 5)]
+        wi_mx = [cols(mx_operand("wi0", HALF), 0, HALF), cols(early_mx, 0, HALF)]
+        zT_mx = [cols(early_mx, HALF, 3 * HALF), cols(early_mx, 5 * HALF, 7 * HALF)]
+        wd_mx = cols(early_mx, 3 * HALF, 5 * HALF)
         zm_both = mx_operand("zm", G * N)
         zm_mx = [cols(zm_both, g * N, (g + 1) * N) for g in range(G)]
-        last_mx = mx_operand("last", KP + N)
-        mid_mx = mx_operand("mid", KP)
-        er_mx = [mx_operand("er0", HALF), cols(mid_mx, HALF, KP), cols(last_mx, KP, KP + HALF), cols(last_mx, KP + HALF, 2 * KP)]
-        wd_mx = cols(early_mx, 3 * HALF, 5 * HALF)
-        ed_mx = [[cols(mid_mx, 0, HALF), mx_operand("ed0b", HALF)], [cols(last_mx, 0, HALF), cols(last_mx, HALF, KP)]]
-        planes = {"zT": zT_raw, "zm": zm_raw, "wd": [atoms_bf], "ed": e_planes}
-        operand = {"zT": zT_mx, "zm": zm_mx, "wd": [wd_mx], "ed": ed_mx}
-        wt_bank, diff, th, gz = {}, {}, {}, {}
+        last_mx = mx_operand("last", 4 * HALF)
+        er_mx = [cols(mx_operand("er%d" % t, HALF), 0, HALF) for t in range(2)]
+        er_mx += [cols(last_mx, t * HALF, (t + 1) * HALF) for t in range(2, PACK)]
+        ed_mx = [cols(mx_operand("ed0", KP), 0, KP), cols(last_mx, 0, KP)]
+        diff, gz = {}, {}
 
         wT_planes = wT.rearrange("(p t) c -> p t c", t=PACK)
         out0_planes = out_0.rearrange("(p t) c -> p t c", t=PACK)
-        zT_rows = zT[0].rearrange("(p j) r -> p j r", j=PACK)
 
-        def load_table(t):
-            nc.sync.dma_start(out=table[t][:], in_=wT_planes[:, t, :])
+        def interleave(engine, words, planes, a, b):
+            dst = words[:, a * PACK : b * PACK].rearrange("p (c t) -> p c t", t=PACK)
+            src = planes[:, :, a:b]
+            if engine is nc.gpsimd:
+                engine.tensor_scalar(dst, src.rearrange("p t c -> p c t"), 1.0, 0.0, MULT, ADD)
+                return
+            copy = engine.tensor_copy if engine is nc.vector else engine.copy
+            copy(out=dst.rearrange("p (c i) t -> p c t i", i=4), in_=src.rearrange("p t (c i) -> p c t i", i=4))
 
-        def load_zT(g):
-            nc.sync.dma_start(out=zT_raw[g][:], in_=zT_rows[:, :, g * KP : (g + 1) * KP])
+        def interleave_shared(words, planes):
+            interleave(nc.vector, words, planes, 0, HALF)
+            interleave(nc.scalar, words, planes, HALF, KP)
 
-        def load_xm(g):
-            nc.sync.dma_start(out=xm_raw[g][:], in_=xm[0, g * KP : (g + 1) * KP, :].rearrange("(c p) d -> p c d", p=P))
-
-        def load_zm(g):
-            nc.sync.dma_start(out=zm_raw[g][:], in_=zm[0, g * KP : (g + 1) * KP, :].rearrange("(p j) i -> p j i", j=PACK))
-
-        def spread_wt(g, b):
-            wt_bank[g] = banks[b]
-            for s in range(PACK):
-                nc.tensor.transpose(wt_bank[g][:, s:KP:PACK], wt_rows[:, g, s : s + 1].to_broadcast([P, P]), ident[:])
-
-        def zero(t, engine):
-            engine.memset(window[t][:], 0.0)
-
-        def gather(t):
-            nc.vector.tensor_copy(atoms_bf[:, t, :], table[t][:].indirect(offsets[:]))
+        def quantize_early(a, b):
+            quantize(cols(early_mx, a * HALF, b * HALF), E4M3, slots(early, a, b))
 
         def turn_words(plane, b):
             pairs = plane.bitcast(F32)
-            bank = new_bank(2, P, b)
+            bank = banks[b][:, : 2 * P].rearrange("p (v m) -> p v m", v=2)
             for v in range(2):
                 nc.tensor.transpose(bank[:, v, :], pairs[:, v : 2 * P : 2], ident[:])
             return bank
 
-        def turn_atoms(t, copy):
+        def gather_and_turn(t):
             u, e = divmod(t, 2)
-            bank = turn_words(atoms_bf[:, t, :], (PACK + t) % 6)
-            pairs = wi_bf[u][:].bitcast(F32)
-            copy(
-                out=pairs.rearrange("p (n e k v) -> p e n k v", e=2, k=2, v=2)[:, e],
-                in_=bank[:].rearrange("p v (n k) -> p n k v", k=2),
+            nc.vector.tensor_copy(atoms[:, t, :], table[t][:].indirect(offsets[:]))
+            bank = turn_words(atoms[:, t, :], (PACK + t) % WORK_BANKS)
+            nc.scalar.copy(
+                out=wi_words[u].bitcast(F32).rearrange("p (n e k v) -> p e n k v", e=2, k=2, v=2)[:, e],
+                in_=bank.rearrange("p v (n k) -> p n k v", k=2),
             )
 
-        def quant_wi(u):
-            quantize(cols(wi_mx[u], 0, 2 * P), E4M3, wi_bf[u][:])
-
-        def staged(what, g, a, b):
-            if (what, g) == ("ed", 0):
-                return last[:, : HALF * PACK]
-            return grouped[what, g][:, a * PACK : b * PACK]
-
-        def group(what, g, a, b, copy):
-            dst = staged(what, g, a, b).rearrange("p (c t) -> p c t", t=PACK)
-            src = planes[what][g][:, :, a:b]
-            if copy is gcopy:
-                copy(out=dst, in_=src.rearrange("p t c -> p c t"))
-            else:
-                copy(out=dst.rearrange("p (c i) t -> p c t i", i=4), in_=src.rearrange("p t (c i) -> p c t i", i=4))
-
-        def quant(what, g, a, b):
-            fmt = E5M2 if what == "ed" else E4M3
-            quantize(cols(operand[what][g], a, b), fmt, staged(what, g, a, b))
+        def spread_wt(g):
+            for s in range(PACK):
+                nc.tensor.transpose(wt_bank[g][:, s:KP:PACK], wt_rows[:, g, s : s + 1].to_broadcast([P, P]), ident[:])
 
         def residual(u, g, h):
-            bank = new_bank(2, 2 * P, (PACK * g + 2 * u + h) % 6)
+            bank = banks[(PACK * g + 2 * u + h) % WORK_BANKS][:].rearrange("p (c m) -> p c m", c=2)
             for c in range(2):
                 first = (2 * h + c) * P
-                mm(bank[:, c, :], cols(zT_mx[g], first, first + P), E4M3, cols(wi_mx[u], 0, 2 * P))
-            diff[u, g, h] = ring.tile([P, 2, 2 * P], F32, name="diff", bufs=8, align_bytes=256)
+                mm(bank[:, c, :], cols(zT_mx[g], first, first + P), E4M3, wi_mx[u])
+            diff[u, g, h] = ring.tile([P, 2, 2 * P], F32, name="diff", bufs=2 * PACK, align_bytes=256)
             rows = xm_raw[g][:, 2 * h : 2 * h + 2, :].rearrange("p c d -> p (c d)")
             nc.vector.tensor_tensor(
                 diff[u, g, h][:].rearrange("p c (n k e) -> p (c n) k e", k=2, e=2),
-                bank[:].rearrange("p c (n e k) -> p (c n) k e", e=2, k=2),
+                bank.rearrange("p c (n e k) -> p (c n) k e", e=2, k=2),
                 rows.rearrange("p (n k u e) -> p u n k e", k=2, u=2, e=2)[:, u],
                 SUB,
             )
 
-        def squash(t, g, bank):
+        def squash(t, g, b):
             u, e = divmod(t, 2)
-            bank = new_bank(PACK, P, bank)
             for c in range(PACK):
-                nc.tensor.transpose(bank[:, c, :], diff[u, g, c // 2][:, c % 2, e : 2 * P : 2], ident[:])
-            th[t, g] = th_tiles[PACK * g + t]
-            nc.scalar.activation(th[t, g][:], bank[:].rearrange("p c r -> p (c r)"), TANH, scale=cs_cols[:, t : t + 1])
+                nc.tensor.transpose(
+                    banks[b][:, c * P : (c + 1) * P], diff[u, g, c // 2][:, c % 2, e : 2 * P : 2], ident[:]
+                )
+            nc.scalar.activation(th[g][:, t, :], banks[b][:], TANH, scale=cs_cols[:, t : t + 1])
 
         def weigh(t, g):
             nc.vector.scalar_tensor_tensor(
-                e_planes[g][:, t, :],
-                th[t, g][:],
-                cs_cols[:, t : t + 1],
-                wt_bank[g][:],
-                MULT,
-                MULT,
+                e_planes[g][:, t, :], th[g][:, t, :], cs_cols[:, t : t + 1], wt_bank[g][:], MULT, MULT
             )
 
-        def turn_error(t, g, copy, b):
+        def turn_error(t, g, b):
             bank = turn_words(e_planes[g][:, t, :], b)
-            copy(
-                out=er_bf[t][:, g * KP : (g + 1) * KP].bitcast(F32).rearrange("p (m v) -> p m v", v=2),
-                in_=bank[:].rearrange("p v m -> p m v"),
+            nc.scalar.copy(
+                out=er_words[t][:, g * KP : (g + 1) * KP].bitcast(F32).rearrange("p (m v) -> p m v", v=2),
+                in_=bank.rearrange("p v m -> p m v"),
             )
 
-        def quant_er(t):
-            quantize(cols(er_mx[t], 0, G * P), E5M2, er_bf[t])
-
-        def quant_early(a, b):
-            quantize(cols(early_mx, a * HALF, b * HALF), E4M3, early[:, a * HALF * PACK : b * HALF * PACK])
-
-        def quant_late_er():
-            quantize(cols(last_mx, 0, 2 * KP), E5M2, last[:, HALF * PACK :])
-
-        def atom_grad(t, copy, bank):
-            bank = new_bank(1, N, bank)[:, 0, :]
+        def atom_grad(t, b):
             for g in range(G):
-                mm(bank[:], cols(er_mx[t], g * P, (g + 1) * P), E5M2, cols(zm_mx[g], 0, N), g == 0, g == G - 1)
-            copy(out=dw[t], in_=bank[:])
+                mm(banks[b][:], cols(er_mx[t], g * P, (g + 1) * P), E5M2, zm_mx[g], g == 0, g == G - 1)
+            nc.scalar.copy(out=dw[t][:], in_=banks[b][:])
 
         def scatter(t):
-            nc.vector.tensor_copy(window[t % WINDOWS][:].indirect(offsets[:]), dw[t])
+            nc.vector.tensor_copy(window[t % WINDOWS][:].indirect(offsets[:]), dw[t][:])
             nc.sync.dma_start(out=out0_planes[:, t, :], in_=window[t % WINDOWS][:])
 
-        def code_grad(g, s, copy, b):
-            rows = out_1[0, g * KP : (g + 1) * KP, :].rearrange("(s m) i -> m s i", m=P)
-            bank = new_bank(1, N, b)[:, 0, :]
-            mm(bank[:], cols(ed_mx[g][s // 2], s % 2 * P, (s % 2 + 1) * P), E5M2, cols(wd_mx, 0, N))
+        def code_grad(g, s, b):
+            mm(banks[b][:], cols(ed_mx[g], s * P, (s + 1) * P), E5M2, wd_mx)
             if s % 2 == 0:
-                gz[g, s // 2] = ring.tile([P, 2, N], F32, name="gz", bufs=4, align_bytes=256)
-            copy(out=gz[g, s // 2][:, s % 2, :], in_=bank[:])
+                gz[g, s // 2] = ring.tile([P, 2, N], F32, name="gz", bufs=PACK, align_bytes=256)
+            nc.scalar.copy(out=gz[g, s // 2][:, s % 2, :], in_=banks[b][:])
             if s % 2 == 1:
+                rows = out_1[0, g * KP : (g + 1) * KP, :].rearrange("(s m) i -> m s i", m=P)
                 nc.scalar.dma_start(out=rows[:, s - 1 : s + 1, :], in_=gz[g, s // 2][:])
 
-        load_table(0)
+        nc.sync.dma_start(out=table[0][:], in_=wT_planes[:, 0, :])
         nc.sync.dma_start(offsets[:], offs)
         nc.scalar.dma_start(out=wt_rows[:], in_=wt[0].rearrange("(g p s) o -> p g (s o)", p=P, s=PACK))
         nc.scalar.dma_start(out=cs_cols[:], in_=cs[0].rearrange("(p t) -> p t", t=PACK))
         make_identity(nc, ident[:])
-        grouped = {("zm", g): zm_words[:, g * N * PACK : (g + 1) * N * PACK] for g in range(G)}
-        for key, a in ((("zT", 0), 1), (("wd", 0), 3), (("zT", 1), 5)):
-            grouped[key] = early[:, a * HALF * PACK : (a + 2) * HALF * PACK]
-        grouped["ed", 1] = last[:, HALF * PACK : 3 * HALF * PACK]
         for t in range(1, PACK):
-            load_table(t)
+            nc.sync.dma_start(out=table[t][:], in_=wT_planes[:, t, :])
+        zT_rows = zT[0].rearrange("(p j) r -> p j r", j=PACK)
         for g in range(G):
-            load_zT(g)
+            nc.sync.dma_start(out=zT_raw[g][:], in_=zT_rows[:, :, g * KP : (g + 1) * KP])
         for g in range(G):
-            load_xm(g)
+            nc.sync.dma_start(out=xm_raw[g][:], in_=xm[0, g * KP : (g + 1) * KP, :].rearrange("(c p) d -> p c d", p=P))
         for g in range(G):
-            load_zm(g)
+            nc.sync.dma_start(out=zm_raw[g][:], in_=zm[0, g * KP : (g + 1) * KP, :].rearrange("(p j) i -> p j i", j=PACK))
         for t in range(WINDOWS):
-            zero(t, nc.vector)
+            nc.vector.memset(window[t][:], 0.0)
 
-        def atoms_pair(u):
-            for t in (2 * u, 2 * u + 1):
-                gather(t)
-                turn_atoms(t, scopy)
-            quant_wi(u)
-
-        def halves(what, g, first, second):
-            group(what, g, 0, HALF, first)
-            group(what, g, HALF, KP, second)
-            quant(what, g, 0, HALF)
-            quant(what, g, HALF, KP)
-
-        def residuals(u, g):
-            for h in range(2):
-                residual(u, g, h)
-
-        atoms_pair(0)
+        for t in range(2):
+            gather_and_turn(t)
+        quantize(wi_mx[0], E4M3, wi_words[0])
         for g in range(G):
-            spread_wt(g, 6 + g)
+            spread_wt(g)
         for t in range(2, PACK):
-            gather(t)
-            turn_atoms(t, scopy)
-        group("zT", 0, 0, HALF, vcopy)
-        group("zT", 0, HALF, KP, scopy)
-        group("wd", 0, 0, HALF, vcopy)
-        group("wd", 0, HALF, KP, scopy)
-        quant_early(0, 2)
-        quant_early(2, 4)
-        group("zT", 1, 0, HALF, vcopy)
-        group("zT", 1, HALF, KP, scopy)
-        quant_early(4, 6)
-        quant_early(6, 7)
-        group("zm", 0, 0, KP, gcopy)
+            gather_and_turn(t)
+        interleave_shared(zT_words[0], zT_raw[0])
+        interleave_shared(wd_words, atoms)
+        quantize_early(0, 2)
+        quantize_early(2, 4)
+        interleave_shared(zT_words[1], zT_raw[1])
+        quantize_early(4, 6)
+        quantize_early(6, 7)
+        interleave(nc.gpsimd, zm_words[:, : N * PACK], zm_raw[0], 0, N)
+
         for g in range(G):
             for u in range(2):
-                residuals(u, g)
+                for h in range(2):
+                    residual(u, g, h)
         for g in range(G):
             for t in range(2):
                 squash(t, g, 2 + 2 * g + t)
         for g in range(G):
             for t in range(2):
                 weigh(t, g)
-            turn_error(0, g, scopy, g)
+            turn_error(0, g, g)
         for t in range(2, PACK):
             squash(t, 0, t)
             weigh(t, 0)
-        group("zm", 1, 0, HALF, gcopy)
-        group("zm", 1, HALF, KP, vcopy)
-        quantize(cols(zm_both, 0, G * N), E4M3, zm_words[:])
-        quant_er(0)
-        atom_grad(0, scopy, 1)
+
+        quantize(zm_mx[0], E4M3, zm_words[:, : N * PACK])
+        interleave(nc.vector, zm_words[:, N * PACK :], zm_raw[1], 0, N)
+        quantize(zm_mx[1], E4M3, zm_words[:, N * PACK :])
+        quantize(er_mx[0], E5M2, er_words[0])
+        atom_grad(0, 1)
         for g in range(G):
-            turn_error(1, g, scopy, PACK + g)
-        group("ed", 0, 0, HALF, scopy)
-        quantize(cols(mid_mx, 0, KP), E5M2, last[:, : KP * PACK])
-        for t in range(2, PACK):
-            squash(t, 1, (0, PACK)[t - 2])
+            turn_error(1, g, PACK + g)
+        quantize(er_mx[1], E5M2, er_words[1])
+        for t, b in ((2, 0), (3, 4)):
+            squash(t, 1, b)
             weigh(t, 1)
-        for t in range(2, PACK):
-            turn_error(t, 0, scopy, t)
-        for s in range(2):
-            code_grad(0, s, scopy, 5 + s)
-        for t in range(2, PACK):
-            turn_error(t, 1, scopy, t)
-        group("ed", 0, HALF, KP, gcopy)
-        group("ed", 1, 0, KP, gcopy)
+        interleave(nc.scalar, ed_words[0], e_planes[0], 0, HALF)
+        interleave(nc.scalar, ed_words[0], e_planes[0], HALF, KP)
+        quantize(ed_mx[0], E5M2, ed_words[0])
+
+        for g, first, second in ((0, 2, 3), (1, 0, 4)):
+            turn_error(2, g, first)
+            turn_error(3, g, second)
+        code_grad(0, 0, 5)
+        code_grad(0, 1, 6)
+        interleave(nc.gpsimd, ed_words[1], e_planes[1], 0, KP)
         scatter(0)
-        quantize(cols(ed_mx[0][1], 0, HALF), E5M2, last[:, : HALF * PACK])
-        quant_late_er()
-        atom_grad(1, scopy, 1)
+        quantize(cols(last_mx, 0, 4 * HALF), E5M2, slots(last, 1, 5))
+        atom_grad(1, 5)
+        code_grad(0, 2, 6)
+        code_grad(0, 3, 2)
+
         scatter(1)
-        for s in range(2, PACK):
-            code_grad(0, s, scopy, 3 + s)
-        atom_grad(2, scopy, 0)
-        for s in range(PACK):
-            code_grad(1, s, scopy, (2, 3, 4, 7)[s])
+        atom_grad(2, 1)
+        for s, b in enumerate((0, 4, 3, 7)):
+            code_grad(1, s, b)
         scatter(2)
-        atom_grad(3, scopy, 1)
+        atom_grad(3, 1)
         scatter(3)

@@ -24,6 +24,7 @@ KP = P * PACK
 G = R // KP
 HALF = KP // 2
 SLOT = HALF * PACK
+SHARE = 64
 WINDOWS = 3
 WORK_BANKS = 6
 
@@ -65,27 +66,30 @@ def tile_attend_gdi_lch_wz_kernel(tc, zT, wT, xm, wt, zm, cs, offs, out_0, out_1
         table = [held("table%d" % t, [P, T], F32) for t in range(PACK)]
         zT_raw = [held("zT_raw%d" % g, [P, PACK, KP], F32) for g in range(G)]
         zm_raw = [held("zm_raw%d" % g, [P, PACK, N], F32) for g in range(G)]
-        xm_raw = [held("xm_raw%d" % g, [P, PACK, D], F32) for g in range(G)]
+        xm_raw = [[held("xm_raw%d%d" % (g, h), [P, 2, D], F32) for h in range(2)] for g in range(G)]
         window = [held("window%d" % t, [P, T], F32) for t in range(WINDOWS)]
         ident = held("ident", [P, P], F32)
         atoms = held("atoms", [P, PACK * N], BF16)[:].rearrange("p (t i) -> p t i", t=PACK)
-        e_planes = [held("e%d" % g, [P, PACK * KP], BF16)[:].rearrange("p (t r) -> p t r", t=PACK) for g in range(G)]
-        th = zT_raw
+        e_tiles = [held("e%d" % g, [P, PACK * KP], BF16) for g in range(G)]
+        e_planes = [e_tiles[g][:].rearrange("p (t r) -> p t r", t=PACK) for g in range(G)]
+        th = {(t, g): zT_raw[g][:, t, :] for t in range(PACK) for g in range(G)}
+        th.update({(2 + e, 1): e_tiles[0][:, 2 * e * KP : 2 * (e + 1) * KP].bitcast(F32) for e in range(2)})
 
-        zm_words = held("zm_words", [P, G * N * PACK], BF16)
-        last = held("last", [P, 5 * SLOT], BF16)
         early = held("early", [P, 7 * SLOT], BF16)
+        last = held("last", [P, 4 * SLOT], BF16)
+        zm_words = [held("zm%d_words" % g, [P, 2 * SLOT], BF16)[:] for g in range(G)]
         wi_words = [held("wi0_words", [P, SLOT], BF16)[:], slots(early, 0, 1)]
-        er_words = [held("er0_words", [P, SLOT], BF16)[:]] + [slots(last, a, a + 1) for a in range(2, 5)]
-        zT_words = [slots(early, 1, 3), slots(early, 5, 7)]
-        wd_words = slots(early, 3, 5)
-        ed_words = [slots(last, 0, 2), slots(last, 1, 3)]
-        dw = [held("dw%d" % t, [P, N], F32) for t in range(PACK)]
+        er_words = [held("er0_words", [P, SLOT], BF16)[:], held("er1_words", [P, SLOT], BF16)[:], slots(last, 2, 3), slots(last, 3, 4)]
+        zT_words = [slots(early, 3, 5), slots(early, 5, 7)]
+        wd_words = slots(early, 1, 3)
+        ed_words = [held("ed0_words", [P, 2 * SLOT], BF16)[:], slots(last, 0, 2)]
+        dw = [held("dw%d" % t, [P, N], F32)[:] for t in (0, 2, 3)]
+        dw.insert(1, e_tiles[1][:, : 2 * N].bitcast(F32))
 
         early_mx = mx_operand("early", 7 * HALF)
         wi_mx = [cols(mx_operand("wi0", HALF), 0, HALF), cols(early_mx, 0, HALF)]
-        zT_mx = [cols(early_mx, HALF, 3 * HALF), cols(early_mx, 5 * HALF, 7 * HALF)]
-        wd_mx = cols(early_mx, 3 * HALF, 5 * HALF)
+        zT_mx = [cols(early_mx, 3 * HALF, 5 * HALF), cols(early_mx, 5 * HALF, 7 * HALF)]
+        wd_mx = cols(early_mx, HALF, 3 * HALF)
         zm_both = mx_operand("zm", G * N)
         zm_mx = [cols(zm_both, g * N, (g + 1) * N) for g in range(G)]
         last_mx = mx_operand("last", 4 * HALF)
@@ -106,16 +110,33 @@ def tile_attend_gdi_lch_wz_kernel(tc, zT, wT, xm, wt, zm, cs, offs, out_0, out_1
             copy = engine.tensor_copy if engine is nc.vector else engine.copy
             copy(out=dst.rearrange("p (c i) t -> p c t i", i=4), in_=src.rearrange("p t (c i) -> p c t i", i=4))
 
-        def interleave_shared(words, planes):
-            interleave(nc.vector, words, planes, 0, HALF)
-            interleave(nc.scalar, words, planes, HALF, KP)
+        def deal(engine, words, planes, h, a, b):
+            dst = words[:, h * SLOT : (h + 1) * SLOT].rearrange("p (c m t) -> p c m t", c=2, t=PACK)[:, :, a // 2 : b // 2]
+            src = planes[:, :, h * HALF + a : h * HALF + b]
+            if engine is nc.gpsimd:
+                engine.tensor_scalar(dst, src.rearrange("p t (m c) -> p c m t", c=2), 1.0, 0.0, MULT, ADD)
+                return
+            copy = engine.tensor_copy if engine is nc.vector else engine.copy
+            copy(
+                out=dst.rearrange("p c (n k) t -> p n t k c", k=2),
+                in_=src.rearrange("p t (n k c) -> p n t k c", k=2, c=2),
+            )
+
+        def interleave_shared(words, planes, split):
+            interleave(nc.vector, words, planes, 0, split)
+            interleave(nc.scalar, words, planes, split, KP)
+
+        def deal_shared(words, planes):
+            deal(nc.vector, words, planes, 0, 0, HALF)
+            deal(nc.scalar, words, planes, 1, SHARE, HALF)
+            deal(nc.vector, words, planes, 1, 0, SHARE)
 
         def quantize_early(a, b):
             quantize(cols(early_mx, a * HALF, b * HALF), E4M3, slots(early, a, b))
 
-        def turn_words(plane, b):
+        def turn_words(plane, b, half=0):
             pairs = plane.bitcast(F32)
-            bank = banks[b][:, : 2 * P].rearrange("p (v m) -> p v m", v=2)
+            bank = banks[b][:, half * HALF : (half + 1) * HALF].rearrange("p (v m) -> p v m", v=2)
             for v in range(2):
                 nc.tensor.transpose(bank[:, v, :], pairs[:, v : 2 * P : 2], ident[:])
             return bank
@@ -133,13 +154,13 @@ def tile_attend_gdi_lch_wz_kernel(tc, zT, wT, xm, wt, zm, cs, offs, out_0, out_1
             for s in range(PACK):
                 nc.tensor.transpose(wt_bank[g][:, s:KP:PACK], wt_rows[:, g, s : s + 1].to_broadcast([P, P]), ident[:])
 
-        def residual(u, g, h):
-            bank = banks[(PACK * g + 2 * u + h) % WORK_BANKS][:].rearrange("p (c m) -> p c m", c=2)
+        def residual(u, g, h, b):
+            bank = banks[b][:].rearrange("p (c m) -> p c m", c=2)
             for c in range(2):
                 first = (2 * h + c) * P
                 mm(bank[:, c, :], cols(zT_mx[g], first, first + P), E4M3, wi_mx[u])
             diff[u, g, h] = ring.tile([P, 2, 2 * P], F32, name="diff", bufs=2 * PACK, align_bytes=256)
-            rows = xm_raw[g][:, 2 * h : 2 * h + 2, :].rearrange("p c d -> p (c d)")
+            rows = xm_raw[g][h][:].rearrange("p c d -> p (c d)")
             nc.vector.tensor_tensor(
                 diff[u, g, h][:].rearrange("p c (n k e) -> p (c n) k e", k=2, e=2),
                 bank.rearrange("p c (n e k) -> p (c n) k e", e=2, k=2),
@@ -153,27 +174,33 @@ def tile_attend_gdi_lch_wz_kernel(tc, zT, wT, xm, wt, zm, cs, offs, out_0, out_1
                 nc.tensor.transpose(
                     banks[b][:, c * P : (c + 1) * P], diff[u, g, c // 2][:, c % 2, e : 2 * P : 2], ident[:]
                 )
-            nc.scalar.activation(th[g][:, t, :], banks[b][:], TANH, scale=cs_cols[:, t : t + 1])
+            nc.scalar.activation(
+                th[t, g].rearrange("p (h m c) -> p h m c", h=2, c=2),
+                banks[b][:].rearrange("p (h c m) -> p h m c", h=2, c=2),
+                TANH,
+                scale=cs_cols[:, t : t + 1],
+            )
 
         def weigh(t, g):
             nc.vector.scalar_tensor_tensor(
-                e_planes[g][:, t, :], th[g][:, t, :], cs_cols[:, t : t + 1], wt_bank[g][:], MULT, MULT
+                e_planes[g][:, t, :], th[t, g], cs_cols[:, t : t + 1], wt_bank[g][:], MULT, MULT
             )
 
-        def turn_error(t, g, b):
-            bank = turn_words(e_planes[g][:, t, :], b)
+        def turn_error(t, b, first=0):
+            for g in range(first, G):
+                turn_words(e_planes[g][:, t, :], b, g)
             nc.scalar.copy(
-                out=er_words[t][:, g * KP : (g + 1) * KP].bitcast(F32).rearrange("p (m v) -> p m v", v=2),
-                in_=bank.rearrange("p v m -> p m v"),
+                out=er_words[t].bitcast(F32).rearrange("p (g m v) -> p g m v", g=G, v=2),
+                in_=banks[b][:].rearrange("p (g v m) -> p g m v", g=G, v=2),
             )
 
         def atom_grad(t, b):
             for g in range(G):
                 mm(banks[b][:], cols(er_mx[t], g * P, (g + 1) * P), E5M2, zm_mx[g], g == 0, g == G - 1)
-            nc.scalar.copy(out=dw[t][:], in_=banks[b][:])
+            nc.scalar.copy(out=dw[t], in_=banks[b][:])
 
         def scatter(t):
-            nc.vector.tensor_copy(window[t % WINDOWS][:].indirect(offsets[:]), dw[t][:])
+            nc.vector.tensor_copy(window[t % WINDOWS][:].indirect(offsets[:]), dw[t])
             nc.sync.dma_start(out=out0_planes[:, t, :], in_=window[t % WINDOWS][:])
 
         def code_grad(g, s, b):
@@ -182,8 +209,8 @@ def tile_attend_gdi_lch_wz_kernel(tc, zT, wT, xm, wt, zm, cs, offs, out_0, out_1
                 gz[g, s // 2] = ring.tile([P, 2, N], F32, name="gz", bufs=PACK, align_bytes=256)
             nc.scalar.copy(out=gz[g, s // 2][:, s % 2, :], in_=banks[b][:])
             if s % 2 == 1:
-                rows = out_1[0, g * KP : (g + 1) * KP, :].rearrange("(s m) i -> m s i", m=P)
-                nc.scalar.dma_start(out=rows[:, s - 1 : s + 1, :], in_=gz[g, s // 2][:])
+                rows = out_1[0, g * KP : (g + 1) * KP, :].rearrange("(h m c) i -> m h c i", h=2, c=2)
+                nc.scalar.dma_start(out=rows[:, s // 2], in_=gz[g, s // 2][:])
 
         nc.sync.dma_start(out=table[0][:], in_=wT_planes[:, 0, :])
         nc.sync.dma_start(offsets[:], offs)
@@ -196,11 +223,14 @@ def tile_attend_gdi_lch_wz_kernel(tc, zT, wT, xm, wt, zm, cs, offs, out_0, out_1
         for g in range(G):
             nc.sync.dma_start(out=zT_raw[g][:], in_=zT_rows[:, :, g * KP : (g + 1) * KP])
         for g in range(G):
-            nc.sync.dma_start(out=xm_raw[g][:], in_=xm[0, g * KP : (g + 1) * KP, :].rearrange("(c p) d -> p c d", p=P))
+            rows = xm[0, g * KP : (g + 1) * KP, :].rearrange("(h p c) d -> p h c d", h=2, c=2)
+            for h in range(2):
+                nc.sync.dma_start(out=xm_raw[g][h][:], in_=rows[:, h])
         for g in range(G):
             nc.sync.dma_start(out=zm_raw[g][:], in_=zm[0, g * KP : (g + 1) * KP, :].rearrange("(p j) i -> p j i", j=PACK))
-        for t in range(WINDOWS):
-            nc.vector.memset(window[t][:], 0.0)
+        nc.vector.memset(window[0][:], 0.0)
+        for t in range(1, WINDOWS):
+            nc.gpsimd.memset(window[t][:], 0.0)
 
         for t in range(2):
             gather_and_turn(t)
@@ -209,61 +239,58 @@ def tile_attend_gdi_lch_wz_kernel(tc, zT, wT, xm, wt, zm, cs, offs, out_0, out_1
             spread_wt(g)
         for t in range(2, PACK):
             gather_and_turn(t)
-        interleave_shared(zT_words[0], zT_raw[0])
-        interleave_shared(wd_words, atoms)
-        quantize_early(0, 2)
-        quantize_early(2, 4)
-        interleave_shared(zT_words[1], zT_raw[1])
-        quantize_early(4, 6)
-        quantize_early(6, 7)
-        interleave(nc.gpsimd, zm_words[:, : N * PACK], zm_raw[0], 0, N)
+        interleave_shared(wd_words, atoms, HALF)
+        quantize_early(0, 1)
+        deal_shared(zT_words[0], zT_raw[0])
+        quantize_early(3, 5)
+        quantize_early(1, 3)
+        deal_shared(zT_words[1], zT_raw[1])
+        quantize_early(5, 7)
+        interleave(nc.gpsimd, zm_words[0], zm_raw[0], 0, N)
 
         for g in range(G):
-            for u in range(2):
-                for h in range(2):
-                    residual(u, g, h)
+            for h in range(2):
+                for u in range(2):
+                    residual(u, g, h, (PACK * g + 2 * h + u) % WORK_BANKS)
         for g in range(G):
-            for t in range(2):
-                squash(t, g, 2 + 2 * g + t)
-        for g in range(G):
-            for t in range(2):
+            for t in range(PACK if g == 0 else 2):
+                squash(t, g, (2 + PACK * g + t) % WORK_BANKS)
                 weigh(t, g)
-            turn_error(0, g, g)
-        for t in range(2, PACK):
-            squash(t, 0, t)
-            weigh(t, 0)
-
-        quantize(zm_mx[0], E4M3, zm_words[:, : N * PACK])
-        interleave(nc.vector, zm_words[:, N * PACK :], zm_raw[1], 0, N)
-        quantize(zm_mx[1], E4M3, zm_words[:, N * PACK :])
+        interleave(nc.vector, zm_words[1], zm_raw[1], 0, N)
+        turn_error(0, 4)
+        quantize(zm_mx[0], E4M3, zm_words[0])
         quantize(er_mx[0], E5M2, er_words[0])
-        atom_grad(0, 1)
-        for g in range(G):
-            turn_error(1, g, PACK + g)
-        quantize(er_mx[1], E5M2, er_words[1])
-        for t, b in ((2, 0), (3, 4)):
-            squash(t, 1, b)
-            weigh(t, 1)
-        interleave(nc.scalar, ed_words[0], e_planes[0], 0, HALF)
-        interleave(nc.scalar, ed_words[0], e_planes[0], HALF, KP)
+        quantize(zm_mx[1], E4M3, zm_words[1])
+        atom_grad(0, 6)
+        for h in range(2):
+            deal(nc.scalar, ed_words[0], e_planes[0], h, 0, HALF)
+        turn_error(1, 5)
+        for t in range(2, PACK):
+            turn_words(e_planes[0][:, t, :], t - 2, 0)
         quantize(ed_mx[0], E5M2, ed_words[0])
+        quantize(er_mx[1], E5M2, er_words[1])
+        for t in range(2, PACK):
+            squash(t, 1, t)
+            weigh(t, 1)
 
-        for g, first, second in ((0, 2, 3), (1, 0, 4)):
-            turn_error(2, g, first)
-            turn_error(3, g, second)
-        code_grad(0, 0, 5)
-        code_grad(0, 1, 6)
-        interleave(nc.gpsimd, ed_words[1], e_planes[1], 0, KP)
-        scatter(0)
-        quantize(cols(last_mx, 0, 4 * HALF), E5M2, slots(last, 1, 5))
+        code_grad(0, 0, 4)
+        turn_error(2, 0, 1)
+        turn_error(3, 1, 1)
+        code_grad(0, 1, 5)
+        deal(nc.gpsimd, ed_words[1], e_planes[1], 0, 0, HALF)
+        deal(nc.gpsimd, ed_words[1], e_planes[1], 1, 0, P)
+        deal(nc.scalar, ed_words[1], e_planes[1], 1, P, HALF)
         atom_grad(1, 5)
-        code_grad(0, 2, 6)
-        code_grad(0, 3, 2)
-
+        code_grad(0, 2, 0)
+        code_grad(0, 3, 1)
+        scatter(0)
+        quantize(cols(last_mx, 0, 4 * HALF), E5M2, last[:])
         scatter(1)
-        atom_grad(2, 1)
-        for s, b in enumerate((0, 4, 3, 7)):
+        atom_grad(2, 6)
+        for s, b in enumerate((2, 3)):
             code_grad(1, s, b)
+        atom_grad(3, 4)
+        for s, b in enumerate((7, 0)):
+            code_grad(1, 2 + s, b)
         scatter(2)
-        atom_grad(3, 1)
         scatter(3)

@@ -80,16 +80,16 @@ def tile_attend_gdi_lch_wz_kernel(tc, zT, wT, xm, wt, zm, cs, offs, out_0, out_1
         zm_words = [held("zm%d_words" % g, [P, 2 * SLOT], BF16)[:] for g in range(G)]
         wi_words = [held("wi0_words", [P, SLOT], BF16)[:], slots(early, 0, 1)]
         er_words = [held("er0_words", [P, SLOT], BF16)[:], held("er1_words", [P, SLOT], BF16)[:], slots(last, 2, 3), slots(last, 3, 4)]
-        zT_words = [slots(early, 3, 5), slots(early, 5, 7)]
-        wd_words = slots(early, 1, 3)
+        zT_words = [slots(early, 1, 3), slots(early, 5, 7)]
+        wd_words = slots(early, 3, 5)
         ed_words = [held("ed0_words", [P, 2 * SLOT], BF16)[:], slots(last, 0, 2)]
         dw = [held("dw%d" % t, [P, N], F32)[:] for t in (0, 2, 3)]
         dw.insert(1, e_tiles[1][:, : 2 * N].bitcast(F32))
 
         early_mx = mx_operand("early", 7 * HALF)
         wi_mx = [cols(mx_operand("wi0", HALF), 0, HALF), cols(early_mx, 0, HALF)]
-        zT_mx = [cols(early_mx, 3 * HALF, 5 * HALF), cols(early_mx, 5 * HALF, 7 * HALF)]
-        wd_mx = cols(early_mx, HALF, 3 * HALF)
+        zT_mx = [cols(early_mx, HALF, 3 * HALF), cols(early_mx, 5 * HALF, 7 * HALF)]
+        wd_mx = cols(early_mx, 3 * HALF, 5 * HALF)
         zm_both = mx_operand("zm", G * N)
         zm_mx = [cols(zm_both, g * N, (g + 1) * N) for g in range(G)]
         last_mx = mx_operand("last", 4 * HALF)
@@ -126,10 +126,11 @@ def tile_attend_gdi_lch_wz_kernel(tc, zT, wT, xm, wt, zm, cs, offs, out_0, out_1
             interleave(nc.vector, words, planes, 0, split)
             interleave(nc.scalar, words, planes, split, KP)
 
-        def deal_shared(words, planes):
+        def deal_shared(words, planes, share):
             deal(nc.vector, words, planes, 0, 0, HALF)
-            deal(nc.scalar, words, planes, 1, SHARE, HALF)
-            deal(nc.vector, words, planes, 1, 0, SHARE)
+            deal(nc.scalar, words, planes, 1, share, HALF)
+            if share:
+                deal(nc.vector, words, planes, 1, 0, share)
 
         def quantize_early(a, b):
             quantize(cols(early_mx, a * HALF, b * HALF), E4M3, slots(early, a, b))
@@ -240,18 +241,20 @@ def tile_attend_gdi_lch_wz_kernel(tc, zT, wT, xm, wt, zm, cs, offs, out_0, out_1
         for t in range(2, PACK):
             gather_and_turn(t)
         interleave_shared(wd_words, atoms, HALF)
-        quantize_early(0, 1)
-        deal_shared(zT_words[0], zT_raw[0])
+        for h in range(2):
+            deal(nc.vector, zT_words[0], zT_raw[0], h, 0, HALF)
+        quantize_early(0, 2)
+        quantize_early(2, 3)
+        deal_shared(zT_words[1], zT_raw[1], 0)
         quantize_early(3, 5)
-        quantize_early(1, 3)
-        deal_shared(zT_words[1], zT_raw[1])
-        quantize_early(5, 7)
         interleave(nc.gpsimd, zm_words[0], zm_raw[0], 0, N)
 
         for g in range(G):
             for h in range(2):
                 for u in range(2):
                     residual(u, g, h, (PACK * g + 2 * h + u) % WORK_BANKS)
+                    if (g, h, u) == (0, 0, 0):
+                        quantize_early(5, 7)
         for g in range(G):
             for t in range(PACK if g == 0 else 2):
                 squash(t, g, (2 + PACK * g + t) % WORK_BANKS)

@@ -70,8 +70,8 @@ def tile_attend_gdi_lch_wz_kernel(tc, zT, wT, xm, wt, zm, cs, offs, out_0, out_1
         window = [held("window%d" % t, [P, T], F32) for t in range(WINDOWS)]
         ident = held("ident", [P, P], F32)
         atoms = held("atoms", [P, PACK * N], BF16)[:].rearrange("p (t i) -> p t i", t=PACK)
-        e_tiles = [held("e%d" % g, [P, PACK * KP], BF16) for g in range(G)]
-        e_planes = [e_tiles[g][:].rearrange("p (t r) -> p t r", t=PACK) for g in range(G)]
+        e_tiles = [xm_raw[1][1][:].rearrange("p c d -> p (c d)").bitcast(BF16), held("e1", [P, PACK * KP], BF16)[:]]
+        e_planes = [e_tiles[g].rearrange("p (t r) -> p t r", t=PACK) for g in range(G)]
         th = {(t, g): zT_raw[g][:, t, :] for t in range(PACK) for g in range(G)}
         th.update({(2 + e, 1): e_tiles[0][:, 2 * e * KP : 2 * (e + 1) * KP].bitcast(F32) for e in range(2)})
 
@@ -86,6 +86,7 @@ def tile_attend_gdi_lch_wz_kernel(tc, zT, wT, xm, wt, zm, cs, offs, out_0, out_1
         dw = [held("dw%d" % t, [P, N], F32)[:] for t in (0, 2, 3)]
         dw.insert(1, e_tiles[1][:, : 2 * N].bitcast(F32))
 
+        staged = [zT_raw[1][:, 2 * h : 2 * h + 2, HALF:] for h in range(2)]
         early_mx = mx_operand("early", 7 * HALF)
         wi_mx = [cols(mx_operand("wi0", HALF), 0, HALF), cols(early_mx, 0, HALF)]
         zT_mx = [cols(early_mx, HALF, 3 * HALF), cols(early_mx, 5 * HALF, 7 * HALF)]
@@ -155,19 +156,26 @@ def tile_attend_gdi_lch_wz_kernel(tc, zT, wT, xm, wt, zm, cs, offs, out_0, out_1
             for s in range(PACK):
                 nc.tensor.transpose(wt_bank[g][:, s:KP:PACK], wt_rows[:, g, s : s + 1].to_broadcast([P, P]), ident[:])
 
-        def residual(u, g, h, b):
+        def residual(u, g, h, b, staged=None):
             bank = banks[b][:].rearrange("p (c m) -> p c m", c=2)
             for c in range(2):
                 first = (2 * h + c) * P
                 mm(bank[:, c, :], cols(zT_mx[g], first, first + P), E4M3, wi_mx[u])
             diff[u, g, h] = ring.tile([P, 2, 2 * P], F32, name="diff", bufs=2 * PACK, align_bytes=256)
             rows = xm_raw[g][h][:].rearrange("p c d -> p (c d)")
-            nc.vector.tensor_tensor(
-                diff[u, g, h][:].rearrange("p c (n k e) -> p (c n) k e", k=2, e=2),
-                bank.rearrange("p c (n e k) -> p (c n) k e", e=2, k=2),
-                rows.rearrange("p (n k u e) -> p u n k e", k=2, u=2, e=2)[:, u],
-                SUB,
-            )
+            rec = bank.rearrange("p c (n e k) -> p c n k e", e=2, k=2)
+            rows = rows.rearrange("p (c n u e) -> p u c n e", c=2, u=2, e=2)[:, u]
+            out = diff[u, g, h][:].rearrange("p c (n e) -> p c n e", e=2)
+            if staged is None:
+                nc.vector.tensor_tensor(
+                    out.rearrange("p c (n k) e -> p (c n) k e", k=2),
+                    rec.rearrange("p c n k e -> p (c n) k e"),
+                    rows.rearrange("p c (n k) e -> p (c n) k e", k=2),
+                    SUB,
+                )
+                return
+            nc.scalar.copy(out=staged.rearrange("p c (n k e) -> p c n k e", k=2, e=2), in_=rec)
+            nc.gpsimd.tensor_tensor(out, staged.rearrange("p c (n e) -> p c n e", e=2), rows, SUB)
 
         def squash(t, g, b):
             u, e = divmod(t, 2)
@@ -247,18 +255,19 @@ def tile_attend_gdi_lch_wz_kernel(tc, zT, wT, xm, wt, zm, cs, offs, out_0, out_1
         quantize_early(2, 3)
         deal_shared(zT_words[1], zT_raw[1], 0)
         quantize_early(3, 5)
-        interleave(nc.gpsimd, zm_words[0], zm_raw[0], 0, N)
-
-        for g in range(G):
-            for h in range(2):
-                for u in range(2):
-                    residual(u, g, h, (PACK * g + 2 * h + u) % WORK_BANKS)
-                    if (g, h, u) == (0, 0, 0):
-                        quantize_early(5, 7)
-        for g in range(G):
-            for t in range(PACK if g == 0 else 2):
-                squash(t, g, (2 + PACK * g + t) % WORK_BANKS)
-                weigh(t, g)
+        residual(0, 0, 0, 0)
+        quantize_early(5, 7)
+        residual(1, 0, 0, 1, staged[0])
+        residual(0, 0, 1, 2)
+        residual(1, 0, 1, 3, staged[1])
+        for h, pair in enumerate(((4, 5), (1, 3))):
+            for u in range(2):
+                residual(u, 1, h, pair[u])
+        interleave(nc.gpsimd, zm_words[0], zm_raw[0], 0, N - P)
+        for (t, g), b in zip(((0, 0), (1, 0), (2, 0), (3, 0), (0, 1), (1, 1)), (0, 2, 4, 5, 1, 3)):
+            squash(t, g, b)
+            weigh(t, g)
+        interleave(nc.scalar, zm_words[0], zm_raw[0], N - P, N)
         interleave(nc.vector, zm_words[1], zm_raw[1], 0, N)
         turn_error(0, 4)
         quantize(zm_mx[0], E4M3, zm_words[0])
@@ -268,32 +277,33 @@ def tile_attend_gdi_lch_wz_kernel(tc, zT, wT, xm, wt, zm, cs, offs, out_0, out_1
         for h in range(2):
             deal(nc.scalar, ed_words[0], e_planes[0], h, 0, HALF)
         turn_error(1, 5)
-        for t in range(2, PACK):
-            turn_words(e_planes[0][:, t, :], t - 2, 0)
+        for t, b in ((2, 1), (3, 3)):
+            turn_words(e_planes[0][:, t, :], b, 0)
         quantize(ed_mx[0], E5M2, ed_words[0])
         quantize(er_mx[1], E5M2, er_words[1])
-        for t in range(2, PACK):
-            squash(t, 1, t)
+        for t, b in ((2, 0), (3, 2)):
+            squash(t, 1, b)
             weigh(t, 1)
 
         code_grad(0, 0, 4)
-        turn_error(2, 0, 1)
-        turn_error(3, 1, 1)
+        turn_error(2, 1, 1)
+        turn_error(3, 3, 1)
         code_grad(0, 1, 5)
         deal(nc.gpsimd, ed_words[1], e_planes[1], 0, 0, HALF)
         deal(nc.gpsimd, ed_words[1], e_planes[1], 1, 0, P)
         deal(nc.scalar, ed_words[1], e_planes[1], 1, P, HALF)
         atom_grad(1, 5)
-        code_grad(0, 2, 0)
-        code_grad(0, 3, 1)
+        code_grad(0, 2, 1)
+        code_grad(0, 3, 3)
         scatter(0)
-        quantize(cols(last_mx, 0, 4 * HALF), E5M2, last[:])
+        quantize(cols(last_mx, KP, 2 * KP), E5M2, slots(last, 2, 4))
+        quantize(ed_mx[1], E5M2, ed_words[1])
         scatter(1)
         atom_grad(2, 6)
-        for s, b in enumerate((2, 3)):
+        for s, b in enumerate((0, 2)):
             code_grad(1, s, b)
         atom_grad(3, 4)
-        for s, b in enumerate((7, 0)):
+        for s, b in enumerate((7, 1)):
             code_grad(1, 2 + s, b)
         scatter(2)
         scatter(3)

@@ -97,7 +97,7 @@ def tile_attend_gdi_lch_wz_kernel(tc, zT, wT, xm, wt, zm, cs, offs, out_0, out_1
         er_mx = [cols(mx_operand("er%d" % t, HALF), 0, HALF) for t in range(2)]
         er_mx += [cols(last_mx, t * HALF, (t + 1) * HALF) for t in range(2, PACK)]
         ed_mx = [cols(mx_operand("ed0", KP), 0, KP), cols(last_mx, 0, KP)]
-        diff, gz = {}, {}
+        diff, turned, gz = {}, {}, {}
 
         wT_planes = wT.rearrange("(p t) c -> p t c", t=PACK)
         out0_planes = out_0.rearrange("(p t) c -> p t c", t=PACK)
@@ -167,13 +167,16 @@ def tile_attend_gdi_lch_wz_kernel(tc, zT, wT, xm, wt, zm, cs, offs, out_0, out_1
             rows = rows.rearrange("p (c n u e) -> p u c n e", c=2, u=2, e=2)[:, u]
             out = diff[u, g, h][:].rearrange("p c (n e) -> p c n e", e=2)
             if staged is None:
+                planes = diff[u, g, h][:].rearrange("p e (n k) -> p n e k", k=2)
                 nc.vector.tensor_tensor(
-                    out.rearrange("p c (n k) e -> p (c n) k e", k=2),
-                    rec.rearrange("p c n k e -> p (c n) k e"),
-                    rows.rearrange("p c (n k) e -> p (c n) k e", k=2),
+                    planes,
+                    rec.rearrange("p c n k e -> p (c n) e k"),
+                    rows.rearrange("p c (n k) e -> p (c n) e k", k=2),
                     SUB,
                 )
+                turned[u, g, h] = [[diff[u, g, h][:, e, c * P : (c + 1) * P] for c in range(2)] for e in range(2)]
                 return
+            turned[u, g, h] = [[diff[u, g, h][:, c, e : 2 * P : 2] for c in range(2)] for e in range(2)]
             nc.scalar.copy(out=staged.rearrange("p c (n k e) -> p c n k e", k=2, e=2), in_=rec)
             nc.gpsimd.tensor_tensor(out, staged.rearrange("p c (n e) -> p c n e", e=2), rows, SUB)
 
@@ -181,7 +184,7 @@ def tile_attend_gdi_lch_wz_kernel(tc, zT, wT, xm, wt, zm, cs, offs, out_0, out_1
             u, e = divmod(t, 2)
             for c in range(PACK):
                 nc.tensor.transpose(
-                    banks[b][:, c * P : (c + 1) * P], diff[u, g, c // 2][:, c % 2, e : 2 * P : 2], ident[:]
+                    banks[b][:, c * P : (c + 1) * P], turned[u, g, c // 2][e][c % 2], ident[:]
                 )
             nc.scalar.activation(
                 th[t, g].rearrange("p (h m c) -> p h m c", h=2, c=2),

@@ -17,6 +17,7 @@ MULT = mybir.AluOpType.mult
 ADD = mybir.AluOpType.add
 SUB = mybir.AluOpType.subtract
 TANH = mybir.ActivationFunctionType.Tanh
+COPY = mybir.ActivationFunctionType.Copy
 
 P = 128
 PACK = 4
@@ -25,7 +26,7 @@ G = R // KP
 HALF = KP // 2
 SLOT = HALF * PACK
 SHARE = 64
-WINDOWS = 3
+WINDOWS = 4
 WORK_BANKS = 6
 
 
@@ -212,7 +213,13 @@ def tile_attend_gdi_lch_wz_kernel(tc, zT, wT, xm, wt, zm, cs, offs, out_0, out_1
             nc.scalar.copy(out=dw[t], in_=banks[b][:])
 
         def scatter(t):
-            nc.vector.tensor_copy(window[t % WINDOWS][:].indirect(offsets[:]), dw[t])
+            if t == PACK - 1:
+                for h in range(2):
+                    nc.scalar.activation(
+                        window[t][:].indirect(offsets[:, h * 16 : (h + 1) * 16]), dw[t][:, h * HALF : (h + 1) * HALF], COPY
+                    )
+            else:
+                nc.vector.tensor_copy(window[t % WINDOWS][:].indirect(offsets[:]), dw[t])
             nc.sync.dma_start(out=out0_planes[:, t, :], in_=window[t % WINDOWS][:])
 
         def code_grad(g, s, b):

@@ -80,12 +80,13 @@ def tile_attend_gdi_lch_wz_kernel(tc, zT, wT, xm, wt, zm, cs, offs, out_0, out_1
         last = held("last", [P, 4 * SLOT], BF16)
         zm_words = [held("zm%d_words" % g, [P, 2 * SLOT], BF16)[:] for g in range(G)]
         wi_words = [held("wi0_words", [P, SLOT], BF16)[:], slots(early, 0, 1)]
-        er_words = [held("er0_words", [P, SLOT], BF16)[:], held("er1_words", [P, SLOT], BF16)[:], slots(last, 2, 3), slots(last, 3, 4)]
-        zT_words = [slots(early, 1, 3), slots(early, 5, 7)]
+        er_words = [held("er0_words", [P, SLOT], BF16)[:], held("er1_words", [P, SLOT], BF16)[:], slots(last, 0, 1), slots(last, 2, 3)]
+        zT_words = [[slots(early, a + h, a + h + 1) for h in range(2)] for a in (1, 5)]
         wd_words = slots(early, 3, 5)
-        ed_words = [held("ed0_words", [P, 2 * SLOT], BF16)[:], slots(last, 0, 2)]
-        dw = [held("dw%d" % t, [P, N], F32)[:] for t in (0, 2, 3)]
-        dw.insert(1, e_tiles[1][:, : 2 * N].bitcast(F32))
+        ed0_words = held("ed0_words", [P, 2 * SLOT], BF16)[:]
+        ed_words = [[slots(ed0_words, h, h + 1) for h in range(2)], [slots(last, 1, 2), slots(last, 3, 4)]]
+        dw_vector, dw_scalar = [held("dw%d" % k, [P, N], F32)[:] for k in range(2)]
+        dw = [dw_vector, dw_scalar, dw_scalar, dw_vector]
 
         staged = [zT_raw[1][:, 2 * h : 2 * h + 2, HALF:] for h in range(2)]
         early_mx = mx_operand("early", 7 * HALF)
@@ -96,8 +97,9 @@ def tile_attend_gdi_lch_wz_kernel(tc, zT, wT, xm, wt, zm, cs, offs, out_0, out_1
         zm_mx = [cols(zm_both, g * N, (g + 1) * N) for g in range(G)]
         last_mx = mx_operand("last", 4 * HALF)
         er_mx = [cols(mx_operand("er%d" % t, HALF), 0, HALF) for t in range(2)]
-        er_mx += [cols(last_mx, t * HALF, (t + 1) * HALF) for t in range(2, PACK)]
-        ed_mx = [cols(mx_operand("ed0", KP), 0, KP), cols(last_mx, 0, KP)]
+        er_mx += [cols(last_mx, a * HALF, (a + 1) * HALF) for a in (0, 2)]
+        ed0_mx = cols(mx_operand("ed0", KP), 0, KP)
+        ed_mx = [[cols(ed0_mx, h * HALF, (h + 1) * HALF) for h in range(2)], [cols(last_mx, a * HALF, (a + 1) * HALF) for a in (1, 3)]]
         diff, turned, gz = {}, {}, {}
 
         wT_planes = wT.rearrange("(p t) c -> p t c", t=PACK)
@@ -113,7 +115,7 @@ def tile_attend_gdi_lch_wz_kernel(tc, zT, wT, xm, wt, zm, cs, offs, out_0, out_1
             copy(out=dst.rearrange("p (c i) t -> p c t i", i=4), in_=src.rearrange("p t (c i) -> p c t i", i=4))
 
         def deal(engine, words, planes, h, a, b):
-            dst = words[:, h * SLOT : (h + 1) * SLOT].rearrange("p (c m t) -> p c m t", c=2, t=PACK)[:, :, a // 2 : b // 2]
+            dst = words[h].rearrange("p (c m t) -> p c m t", c=2, t=PACK)[:, :, a // 2 : b // 2]
             src = planes[:, :, h * HALF + a : h * HALF + b]
             if engine is nc.gpsimd:
                 engine.tensor_scalar(dst, src.rearrange("p t (m c) -> p c m t", c=2), 1.0, 0.0, MULT, ADD)
@@ -199,37 +201,45 @@ def tile_attend_gdi_lch_wz_kernel(tc, zT, wT, xm, wt, zm, cs, offs, out_0, out_1
                 e_planes[g][:, t, :], th[t, g], cs_cols[:, t : t + 1], wt_bank[g][:], MULT, MULT
             )
 
-        def turn_error(t, b, first=0):
+        def turn_error(t, b, engine, first=0):
             for g in range(first, G):
                 turn_words(e_planes[g][:, t, :], b, g)
-            nc.scalar.copy(
-                out=er_words[t].bitcast(F32).rearrange("p (g m v) -> p g m v", g=G, v=2),
-                in_=banks[b][:].rearrange("p (g v m) -> p g m v", g=G, v=2),
+            empty(
+                engine,
+                er_words[t].bitcast(F32).rearrange("p (g m v) -> p g m v", g=G, v=2),
+                banks[b][:].rearrange("p (g v m) -> p g m v", g=G, v=2),
             )
 
-        def atom_grad(t, b):
+        def queue(engine):
+            return nc.scalar if engine is nc.scalar else nc.sync
+
+        def empty(engine, out, in_):
+            copy = engine.tensor_copy if engine is nc.vector else engine.copy
+            copy(out=out, in_=in_)
+
+        def atom_grad(t, b, engine):
             for g in range(G):
                 mm(banks[b][:], cols(er_mx[t], g * P, (g + 1) * P), E5M2, zm_mx[g], g == 0, g == G - 1)
-            nc.scalar.copy(out=dw[t], in_=banks[b][:])
+            empty(engine, dw[t], banks[b][:])
 
-        def scatter(t):
-            if t == PACK - 1:
-                for h in range(2):
-                    nc.scalar.activation(
-                        window[t][:].indirect(offsets[:, h * 16 : (h + 1) * 16]), dw[t][:, h * HALF : (h + 1) * HALF], COPY
-                    )
+        def scatter(t, engine, a=0, z=N):
+            if engine is nc.vector:
+                nc.vector.tensor_copy(window[t][:].indirect(offsets[:, a // 16 : z // 16]), dw[t][:, a:z])
             else:
-                nc.vector.tensor_copy(window[t % WINDOWS][:].indirect(offsets[:]), dw[t])
-            nc.sync.dma_start(out=out0_planes[:, t, :], in_=window[t % WINDOWS][:])
+                for c in range(a, z, HALF):
+                    picked = offsets[:, c // 16 : (c + HALF) // 16]
+                    nc.scalar.activation(window[t][:].indirect(picked), dw[t][:, c : c + HALF], COPY)
+            if z == N:
+                queue(engine).dma_start(out=out0_planes[:, t, :], in_=window[t][:])
 
-        def code_grad(g, s, b):
-            mm(banks[b][:], cols(ed_mx[g], s * P, (s + 1) * P), E5M2, wd_mx)
+        def code_grad(g, s, b, engine, q=nc.sync):
+            mm(banks[b][:], cols(ed_mx[g][s // 2], s % 2 * P, (s % 2 + 1) * P), E5M2, wd_mx)
             if s % 2 == 0:
                 gz[g, s // 2] = ring.tile([P, 2, N], F32, name="gz", bufs=PACK, align_bytes=256)
-            nc.scalar.copy(out=gz[g, s // 2][:, s % 2, :], in_=banks[b][:])
+            empty(engine, gz[g, s // 2][:, s % 2, :], banks[b][:])
             if s % 2 == 1:
                 rows = out_1[0, g * KP : (g + 1) * KP, :].rearrange("(h m c) i -> m h c i", h=2, c=2)
-                nc.scalar.dma_start(out=rows[:, s // 2], in_=gz[g, s // 2][:])
+                q.dma_start(out=rows[:, s // 2], in_=gz[g, s // 2][:])
 
         nc.sync.dma_start(out=table[0][:], in_=wT_planes[:, 0, :])
         nc.sync.dma_start(offsets[:], offs)
@@ -277,43 +287,39 @@ def tile_attend_gdi_lch_wz_kernel(tc, zT, wT, xm, wt, zm, cs, offs, out_0, out_1
         for (t, g), b in zip(((0, 0), (1, 0), (2, 0), (3, 0), (0, 1), (1, 1)), (0, 2, 4, 5, 1, 3)):
             squash(t, g, b)
             weigh(t, g)
-        interleave(nc.scalar, zm_words[0], zm_raw[0], N - P, N)
-        interleave(nc.vector, zm_words[1], zm_raw[1], 0, N)
-        turn_error(0, 4)
+        V, S = nc.vector, nc.scalar
+        interleave(S, zm_words[0], zm_raw[0], N - P, N)
         quantize(zm_mx[0], E4M3, zm_words[0])
+        deal(V, ed_words[0], e_planes[0], 1, P, HALF)
+        interleave(V, zm_words[1], zm_raw[1], 0, N)
+        turn_error(0, 4, S)
+        deal(S, ed_words[0], e_planes[0], 0, 0, HALF)
+        deal(S, ed_words[0], e_planes[0], 1, 0, P)
         quantize(er_mx[0], E5M2, er_words[0])
         quantize(zm_mx[1], E4M3, zm_words[1])
-        atom_grad(0, 6)
-        for h in range(2):
-            deal(nc.scalar, ed_words[0], e_planes[0], h, 0, HALF)
-        turn_error(1, 5)
+        turn_error(1, 5, S)
         for t, b in ((2, 1), (3, 3)):
             turn_words(e_planes[0][:, t, :], b, 0)
-        quantize(ed_mx[0], E5M2, ed_words[0])
+        quantize(ed0_mx, E5M2, ed0_words)
         quantize(er_mx[1], E5M2, er_words[1])
         for t, b in ((2, 0), (3, 2)):
             squash(t, 1, b)
             weigh(t, 1)
-
-        code_grad(0, 0, 4)
-        turn_error(2, 1, 1)
-        turn_error(3, 3, 1)
-        code_grad(0, 1, 5)
-        deal(nc.gpsimd, ed_words[1], e_planes[1], 0, 0, HALF)
-        deal(nc.gpsimd, ed_words[1], e_planes[1], 1, 0, P)
-        deal(nc.scalar, ed_words[1], e_planes[1], 1, P, HALF)
-        atom_grad(1, 5)
-        code_grad(0, 2, 1)
-        code_grad(0, 3, 3)
-        scatter(0)
-        quantize(cols(last_mx, KP, 2 * KP), E5M2, slots(last, 2, 4))
-        quantize(ed_mx[1], E5M2, ed_words[1])
-        scatter(1)
-        atom_grad(2, 6)
-        for s, b in enumerate((0, 2)):
-            code_grad(1, s, b)
-        atom_grad(3, 4)
-        for s, b in enumerate((7, 1)):
-            code_grad(1, 2 + s, b)
-        scatter(2)
-        scatter(3)
+        atom_grad(0, 6, S)
+        for s, b in enumerate((4, 5, 0, 2)):
+            code_grad(0, s, b, S)
+        scatter(0, V)
+        for h in range(2):
+            deal(nc.gpsimd, ed_words[1], e_planes[1], h, 0, HALF)
+        atom_grad(1, 7, S)
+        scatter(1, S)
+        turn_error(2, 1, V, 1)
+        turn_error(3, 3, V, 1)
+        for a in (0, 2):
+            quantize(cols(last_mx, a * HALF, (a + 2) * HALF), E5M2, slots(last, a, a + 2))
+        atom_grad(2, 6, S)
+        for s, b in enumerate((0, 5, 2, 4)):
+            code_grad(1, s, b, V)
+        scatter(2, S)
+        atom_grad(3, 1, V)
+        scatter(3, V)

@@ -74,19 +74,18 @@ def tile_attend_gdi_lch_wz_kernel(tc, zT, wT, xm, wt, zm, cs, offs, out_0, out_1
         e_tiles = [xm_raw[1][1][:].rearrange("p c d -> p (c d)").bitcast(BF16), held("e1", [P, PACK * KP], BF16)[:]]
         e_planes = [e_tiles[g].rearrange("p (t r) -> p t r", t=PACK) for g in range(G)]
         th = {(t, g): zT_raw[g][:, t, :] for t in range(PACK) for g in range(G)}
-        th.update({(2 + e, 1): e_tiles[0][:, 2 * e * KP : 2 * (e + 1) * KP].bitcast(F32) for e in range(2)})
+        th[3, 1] = e_tiles[0][:, : 2 * KP].bitcast(F32)
 
         early = held("early", [P, 7 * SLOT], BF16)
-        last = held("last", [P, 4 * SLOT], BF16)
+        er_all = held("er_words", [P, PACK * SLOT], BF16)
         zm_words = [held("zm%d_words" % g, [P, 2 * SLOT], BF16)[:] for g in range(G)]
         wi_words = [held("wi0_words", [P, SLOT], BF16)[:], slots(early, 0, 1)]
-        er_words = [held("er0_words", [P, SLOT], BF16)[:], held("er1_words", [P, SLOT], BF16)[:], slots(last, 0, 1), slots(last, 2, 3)]
+        er_words = [slots(er_all, t, t + 1) for t in range(PACK)]
         zT_words = [[slots(early, a + h, a + h + 1) for h in range(2)] for a in (1, 5)]
         wd_words = slots(early, 3, 5)
-        ed0_words = held("ed0_words", [P, 2 * SLOT], BF16)[:]
-        ed_words = [[slots(ed0_words, h, h + 1) for h in range(2)], [slots(last, 1, 2), slots(last, 3, 4)]]
-        dw_vector, dw_scalar = [held("dw%d" % k, [P, N], F32)[:] for k in range(2)]
-        dw = [dw_vector, dw_scalar, dw_scalar, dw_vector]
+        ed_both = [held("ed%d_words" % g, [P, 2 * SLOT], BF16)[:] for g in range(G)]
+        ed_words = [[slots(ed_both[g], h, h + 1) for h in range(2)] for g in range(G)]
+        dw = [held("dw%d" % t, [P, N], F32)[:] for t in range(PACK)]
 
         staged = [zT_raw[1][:, 2 * h : 2 * h + 2, HALF:] for h in range(2)]
         early_mx = mx_operand("early", 7 * HALF)
@@ -95,11 +94,10 @@ def tile_attend_gdi_lch_wz_kernel(tc, zT, wT, xm, wt, zm, cs, offs, out_0, out_1
         wd_mx = cols(early_mx, 3 * HALF, 5 * HALF)
         zm_both = mx_operand("zm", G * N)
         zm_mx = [cols(zm_both, g * N, (g + 1) * N) for g in range(G)]
-        last_mx = mx_operand("last", 4 * HALF)
-        er_mx = [cols(mx_operand("er%d" % t, HALF), 0, HALF) for t in range(2)]
-        er_mx += [cols(last_mx, a * HALF, (a + 1) * HALF) for a in (0, 2)]
-        ed0_mx = cols(mx_operand("ed0", KP), 0, KP)
-        ed_mx = [[cols(ed0_mx, h * HALF, (h + 1) * HALF) for h in range(2)], [cols(last_mx, a * HALF, (a + 1) * HALF) for a in (1, 3)]]
+        er_codes = mx_operand("er", PACK * HALF)
+        er_mx = [cols(er_codes, t * HALF, (t + 1) * HALF) for t in range(PACK)]
+        ed_codes = [cols(mx_operand("ed%d" % g, KP), 0, KP) for g in range(G)]
+        ed_mx = [[cols(ed_codes[g], h * HALF, (h + 1) * HALF) for h in range(2)] for g in range(G)]
         diff, turned, gz = {}, {}, {}
 
         wT_planes = wT.rearrange("(p t) c -> p t c", t=PACK)
@@ -210,19 +208,19 @@ def tile_attend_gdi_lch_wz_kernel(tc, zT, wT, xm, wt, zm, cs, offs, out_0, out_1
                 banks[b][:].rearrange("p (g v m) -> p g m v", g=G, v=2),
             )
 
-        def queue(engine):
-            return nc.scalar if engine is nc.scalar else nc.sync
-
         def empty(engine, out, in_):
             copy = engine.tensor_copy if engine is nc.vector else engine.copy
             copy(out=out, in_=in_)
+
+        def quantize_er(a, z):
+            quantize(cols(er_codes, a * HALF, z * HALF), E5M2, slots(er_all, a, z))
 
         def atom_grad(t, b, engine):
             for g in range(G):
                 mm(banks[b][:], cols(er_mx[t], g * P, (g + 1) * P), E5M2, zm_mx[g], g == 0, g == G - 1)
             empty(engine, dw[t], banks[b][:])
 
-        def scatter(t, engine, a=0, z=N):
+        def scatter(t, engine, a=0, z=N, q=nc.sync):
             if engine is nc.vector:
                 nc.vector.tensor_copy(window[t][:].indirect(offsets[:, a // 16 : z // 16]), dw[t][:, a:z])
             else:
@@ -230,7 +228,7 @@ def tile_attend_gdi_lch_wz_kernel(tc, zT, wT, xm, wt, zm, cs, offs, out_0, out_1
                     picked = offsets[:, c // 16 : (c + HALF) // 16]
                     nc.scalar.activation(window[t][:].indirect(picked), dw[t][:, c : c + HALF], COPY)
             if z == N:
-                queue(engine).dma_start(out=out0_planes[:, t, :], in_=window[t][:])
+                q.dma_start(out=out0_planes[:, t, :], in_=window[t][:])
 
         def code_grad(g, s, b, engine, q=nc.sync):
             mm(banks[b][:], cols(ed_mx[g][s // 2], s % 2 * P, (s % 2 + 1) * P), E5M2, wd_mx)
@@ -283,43 +281,43 @@ def tile_attend_gdi_lch_wz_kernel(tc, zT, wT, xm, wt, zm, cs, offs, out_0, out_1
         for h, pair in enumerate(((4, 5), (1, 3))):
             for u in range(2):
                 residual(u, 1, h, pair[u])
-        interleave(nc.gpsimd, zm_words[0], zm_raw[0], 0, N - P)
-        for (t, g), b in zip(((0, 0), (1, 0), (2, 0), (3, 0), (0, 1), (1, 1)), (0, 2, 4, 5, 1, 3)):
+        interleave(nc.gpsimd, zm_words[0], zm_raw[0], 0, N)
+        for (t, g), b in zip(((0, 0), (1, 0), (2, 0), (3, 0), (0, 1), (1, 1), (2, 1)), (0, 2, 4, 5, 1, 3, 0)):
             squash(t, g, b)
             weigh(t, g)
         V, S = nc.vector, nc.scalar
-        interleave(S, zm_words[0], zm_raw[0], N - P, N)
         quantize(zm_mx[0], E4M3, zm_words[0])
-        deal(V, ed_words[0], e_planes[0], 1, P, HALF)
         interleave(V, zm_words[1], zm_raw[1], 0, N)
         turn_error(0, 4, S)
-        deal(S, ed_words[0], e_planes[0], 0, 0, HALF)
         deal(S, ed_words[0], e_planes[0], 1, 0, P)
-        quantize(er_mx[0], E5M2, er_words[0])
+        deal(S, ed_words[0], e_planes[0], 0, 0, HALF)
+        deal(S, ed_words[0], e_planes[0], 1, P, HALF)
+        quantize_er(0, 1)
         quantize(zm_mx[1], E4M3, zm_words[1])
         turn_error(1, 5, S)
-        for t, b in ((2, 1), (3, 3)):
-            turn_words(e_planes[0][:, t, :], b, 0)
-        quantize(ed0_mx, E5M2, ed0_words)
-        quantize(er_mx[1], E5M2, er_words[1])
-        for t, b in ((2, 0), (3, 2)):
-            squash(t, 1, b)
-            weigh(t, 1)
+        turn_words(e_planes[0][:, 3, :], 3, 0)
+        quantize(ed_codes[0], E5M2, ed_both[0])
+        squash(3, 1, 2)
+        turn_error(2, 1, S)
+        weigh(3, 1)
+        quantize_er(1, 3)
         atom_grad(0, 6, S)
         for s, b in enumerate((4, 5, 0, 2)):
-            code_grad(0, s, b, S)
+            code_grad(0, s, b, S, S)
         scatter(0, V)
         for h in range(2):
             deal(nc.gpsimd, ed_words[1], e_planes[1], h, 0, HALF)
         atom_grad(1, 7, S)
-        scatter(1, S)
-        turn_error(2, 1, V, 1)
-        turn_error(3, 3, V, 1)
-        for a in (0, 2):
-            quantize(cols(last_mx, a * HALF, (a + 2) * HALF), E5M2, slots(last, a, a + 2))
         atom_grad(2, 6, S)
-        for s, b in enumerate((0, 5, 2, 4)):
+        scatter(1, S, 0, HALF)
+        scatter(2, S, 0, HALF)
+        quantize(ed_mx[1][0], E5M2, ed_words[1][0])
+        turn_error(3, 3, V, 1)
+        quantize(ed_mx[1][1], E5M2, ed_words[1][1])
+        quantize_er(3, 4)
+        for s, b in enumerate((4, 5, 0, 3)):
             code_grad(1, s, b, V)
-        scatter(2, S)
+        scatter(1, S, HALF, N)
+        scatter(2, S, HALF, N)
         atom_grad(3, 1, V)
-        scatter(3, V)
+        scatter(3, V, q=S)

@@ -24,14 +24,14 @@ PACK = 4
 KP = P * PACK
 G = R // KP
 HALF = KP // 2
-SLOT = HALF * PACK
+RUN = HALF * PACK
 SHARE = 64
-WINDOWS = 4
 WORK_BANKS = 6
 
 
 def tile_attend_gdi_lch_wz_kernel(tc, zT, wT, xm, wt, zm, cs, offs, out_0, out_1):
     nc = tc.nc
+    V, S = nc.vector, nc.scalar
     with ExitStack() as ctx:
         keep = ctx.enter_context(tc.tile_pool(name="keep", bufs=1))
         ring = ctx.enter_context(tc.tile_pool(name="ring", bufs=1))
@@ -46,8 +46,8 @@ def tile_attend_gdi_lch_wz_kernel(tc, zT, wT, xm, wt, zm, cs, offs, out_0, out_1
         def cols(operand, a, b):
             return operand[0][:, a:b], operand[1][:, a:b]
 
-        def slots(tile, a, b):
-            return tile[:, a * SLOT : b * SLOT]
+        def runs(tile, a, b):
+            return tile[:, a * RUN : b * RUN]
 
         def quantize(operand, fmt, words):
             nc.vector.quantize_mx(out=operand[0].bitcast(fmt), scales=operand[1], in_=words)
@@ -68,26 +68,26 @@ def tile_attend_gdi_lch_wz_kernel(tc, zT, wT, xm, wt, zm, cs, offs, out_0, out_1
         zT_raw = [held("zT_raw%d" % g, [P, PACK, KP], F32) for g in range(G)]
         zm_raw = [held("zm_raw%d" % g, [P, PACK, N], F32) for g in range(G)]
         xm_raw = [[held("xm_raw%d%d" % (g, h), [P, 2, D], F32) for h in range(2)] for g in range(G)]
-        window = [held("window%d" % t, [P, T], F32) for t in range(WINDOWS)]
+        window = [held("window%d" % t, [P, T], F32) for t in range(PACK)]
         ident = held("ident", [P, P], F32)
         atoms = held("atoms", [P, PACK * N], BF16)[:].rearrange("p (t i) -> p t i", t=PACK)
-        e_tiles = [xm_raw[1][1][:].rearrange("p c d -> p (c d)").bitcast(BF16), held("e1", [P, PACK * KP], BF16)[:]]
+        e_tiles = [xm_raw[1][0][:].rearrange("p c d -> p (c d)").bitcast(BF16), held("e1", [P, PACK * KP], BF16)[:]]
         e_planes = [e_tiles[g].rearrange("p (t r) -> p t r", t=PACK) for g in range(G)]
         th = {(t, g): zT_raw[g][:, t, :] for t in range(PACK) for g in range(G)}
         th[3, 1] = e_tiles[0][:, : 2 * KP].bitcast(F32)
 
-        early = held("early", [P, 7 * SLOT], BF16)
-        er_all = held("er_words", [P, PACK * SLOT], BF16)
-        zm_words = [held("zm%d_words" % g, [P, 2 * SLOT], BF16)[:] for g in range(G)]
-        wi_words = [held("wi0_words", [P, SLOT], BF16)[:], slots(early, 0, 1)]
-        er_words = [slots(er_all, t, t + 1) for t in range(PACK)]
-        zT_words = [[slots(early, a + h, a + h + 1) for h in range(2)] for a in (1, 5)]
-        wd_words = slots(early, 3, 5)
-        ed_both = [held("ed%d_words" % g, [P, 2 * SLOT], BF16)[:] for g in range(G)]
-        ed_words = [[slots(ed_both[g], h, h + 1) for h in range(2)] for g in range(G)]
+        early = held("early", [P, 7 * RUN], BF16)
+        er_all = held("er_words", [P, PACK * RUN], BF16)
+        zm_words = [held("zm%d_words" % g, [P, 2 * RUN], BF16)[:] for g in range(G)]
+        wi_words = [held("wi0_words", [P, RUN], BF16)[:], runs(early, 0, 1)]
+        er_words = [runs(er_all, t, t + 1) for t in range(PACK)]
+        zT_words = [[runs(early, a + h, a + h + 1) for h in range(2)] for a in (1, 5)]
+        wd_words = runs(early, 3, 5)
+        ed_both = [held("ed%d_words" % g, [P, 2 * RUN], BF16)[:] for g in range(G)]
+        ed_words = [[runs(ed_both[g], h, h + 1) for h in range(2)] for g in range(G)]
         dw = [held("dw%d" % t, [P, N], F32)[:] for t in range(PACK)]
 
-        staged = [zT_raw[1][:, 2 * h : 2 * h + 2, HALF:] for h in range(2)]
+        staged = [zT_raw[1][:, 2 * h : 2 * h + 2, HALF:] for h in range(2)] + [held("staged", [P, 2, HALF], F32)[:]]
         early_mx = mx_operand("early", 7 * HALF)
         wi_mx = [cols(mx_operand("wi0", HALF), 0, HALF), cols(early_mx, 0, HALF)]
         zT_mx = [cols(early_mx, HALF, 3 * HALF), cols(early_mx, 5 * HALF, 7 * HALF)]
@@ -103,14 +103,16 @@ def tile_attend_gdi_lch_wz_kernel(tc, zT, wT, xm, wt, zm, cs, offs, out_0, out_1
         wT_planes = wT.rearrange("(p t) c -> p t c", t=PACK)
         out0_planes = out_0.rearrange("(p t) c -> p t c", t=PACK)
 
+        def copy(engine, out, in_):
+            (engine.tensor_copy if engine is V else engine.copy)(out=out, in_=in_)
+
         def interleave(engine, words, planes, a, b):
             dst = words[:, a * PACK : b * PACK].rearrange("p (c t) -> p c t", t=PACK)
             src = planes[:, :, a:b]
             if engine is nc.gpsimd:
                 engine.tensor_scalar(dst, src.rearrange("p t c -> p c t"), 1.0, 0.0, MULT, ADD)
                 return
-            copy = engine.tensor_copy if engine is nc.vector else engine.copy
-            copy(out=dst.rearrange("p (c i) t -> p c t i", i=4), in_=src.rearrange("p t (c i) -> p c t i", i=4))
+            copy(engine, dst.rearrange("p (c i) t -> p c t i", i=4), src.rearrange("p t (c i) -> p c t i", i=4))
 
         def deal(engine, words, planes, h, a, b):
             dst = words[h].rearrange("p (c m t) -> p c m t", c=2, t=PACK)[:, :, a // 2 : b // 2]
@@ -118,24 +120,14 @@ def tile_attend_gdi_lch_wz_kernel(tc, zT, wT, xm, wt, zm, cs, offs, out_0, out_1
             if engine is nc.gpsimd:
                 engine.tensor_scalar(dst, src.rearrange("p t (m c) -> p c m t", c=2), 1.0, 0.0, MULT, ADD)
                 return
-            copy = engine.tensor_copy if engine is nc.vector else engine.copy
             copy(
-                out=dst.rearrange("p c (n k) t -> p n t k c", k=2),
-                in_=src.rearrange("p t (n k c) -> p n t k c", k=2, c=2),
+                engine,
+                dst.rearrange("p c (n k) t -> p n t k c", k=2),
+                src.rearrange("p t (n k c) -> p n t k c", k=2, c=2),
             )
 
-        def interleave_shared(words, planes, split):
-            interleave(nc.vector, words, planes, 0, split)
-            interleave(nc.scalar, words, planes, split, KP)
-
-        def deal_shared(words, planes, share):
-            deal(nc.vector, words, planes, 0, 0, HALF)
-            deal(nc.scalar, words, planes, 1, share, HALF)
-            if share:
-                deal(nc.vector, words, planes, 1, 0, share)
-
         def quantize_early(a, b):
-            quantize(cols(early_mx, a * HALF, b * HALF), E4M3, slots(early, a, b))
+            quantize(cols(early_mx, a * HALF, b * HALF), E4M3, runs(early, a, b))
 
         def turn_words(plane, b, half=0):
             pairs = plane.bitcast(F32)
@@ -157,7 +149,7 @@ def tile_attend_gdi_lch_wz_kernel(tc, zT, wT, xm, wt, zm, cs, offs, out_0, out_1
             for s in range(PACK):
                 nc.tensor.transpose(wt_bank[g][:, s:KP:PACK], wt_rows[:, g, s : s + 1].to_broadcast([P, P]), ident[:])
 
-        def residual(u, g, h, b, staged=None):
+        def residual(u, g, h, b, stage=None):
             bank = banks[b][:].rearrange("p (c m) -> p c m", c=2)
             for c in range(2):
                 first = (2 * h + c) * P
@@ -167,7 +159,7 @@ def tile_attend_gdi_lch_wz_kernel(tc, zT, wT, xm, wt, zm, cs, offs, out_0, out_1
             rec = bank.rearrange("p c (n e k) -> p c n k e", e=2, k=2)
             rows = rows.rearrange("p (c n u e) -> p u c n e", c=2, u=2, e=2)[:, u]
             out = diff[u, g, h][:].rearrange("p c (n e) -> p c n e", e=2)
-            if staged is None:
+            if stage is None:
                 planes = diff[u, g, h][:].rearrange("p e (n k) -> p n e k", k=2)
                 nc.vector.tensor_tensor(
                     planes,
@@ -178,8 +170,8 @@ def tile_attend_gdi_lch_wz_kernel(tc, zT, wT, xm, wt, zm, cs, offs, out_0, out_1
                 turned[u, g, h] = [[diff[u, g, h][:, e, c * P : (c + 1) * P] for c in range(2)] for e in range(2)]
                 return
             turned[u, g, h] = [[diff[u, g, h][:, c, e : 2 * P : 2] for c in range(2)] for e in range(2)]
-            nc.scalar.copy(out=staged.rearrange("p c (n k e) -> p c n k e", k=2, e=2), in_=rec)
-            nc.gpsimd.tensor_tensor(out, staged.rearrange("p c (n e) -> p c n e", e=2), rows, SUB)
+            nc.scalar.copy(out=stage.rearrange("p c (n k e) -> p c n k e", k=2, e=2), in_=rec)
+            nc.gpsimd.tensor_tensor(out, stage.rearrange("p c (n e) -> p c n e", e=2), rows, SUB)
 
         def squash(t, g, b):
             u, e = divmod(t, 2)
@@ -202,42 +194,37 @@ def tile_attend_gdi_lch_wz_kernel(tc, zT, wT, xm, wt, zm, cs, offs, out_0, out_1
         def turn_error(t, b, engine, first=0):
             for g in range(first, G):
                 turn_words(e_planes[g][:, t, :], b, g)
-            empty(
+            copy(
                 engine,
                 er_words[t].bitcast(F32).rearrange("p (g m v) -> p g m v", g=G, v=2),
                 banks[b][:].rearrange("p (g v m) -> p g m v", g=G, v=2),
             )
 
-        def empty(engine, out, in_):
-            copy = engine.tensor_copy if engine is nc.vector else engine.copy
-            copy(out=out, in_=in_)
-
         def quantize_er(a, z):
-            quantize(cols(er_codes, a * HALF, z * HALF), E5M2, slots(er_all, a, z))
+            quantize(cols(er_codes, a * HALF, z * HALF), E5M2, runs(er_all, a, z))
 
         def atom_grad(t, b, engine):
             for g in range(G):
                 mm(banks[b][:], cols(er_mx[t], g * P, (g + 1) * P), E5M2, zm_mx[g], g == 0, g == G - 1)
-            empty(engine, dw[t], banks[b][:])
+            copy(engine, dw[t], banks[b][:])
 
-        def scatter(t, engine, a=0, z=N, q=nc.sync):
-            if engine is nc.vector:
-                nc.vector.tensor_copy(window[t][:].indirect(offsets[:, a // 16 : z // 16]), dw[t][:, a:z])
+        def scatter(t, engine, a, z, queue=nc.sync):
+            target = window[t][:].indirect(offsets[:, a // 16 : z // 16])
+            if engine is V:
+                V.tensor_copy(target, dw[t][:, a:z])
             else:
-                for c in range(a, z, HALF):
-                    picked = offsets[:, c // 16 : (c + HALF) // 16]
-                    nc.scalar.activation(window[t][:].indirect(picked), dw[t][:, c : c + HALF], COPY)
+                S.activation(target, dw[t][:, a:z], COPY)
             if z == N:
-                q.dma_start(out=out0_planes[:, t, :], in_=window[t][:])
+                queue.dma_start(out=out0_planes[:, t, :], in_=window[t][:])
 
-        def code_grad(g, s, b, engine, q=nc.sync):
+        def code_grad(g, s, b, engine, queue):
             mm(banks[b][:], cols(ed_mx[g][s // 2], s % 2 * P, (s % 2 + 1) * P), E5M2, wd_mx)
             if s % 2 == 0:
                 gz[g, s // 2] = ring.tile([P, 2, N], F32, name="gz", bufs=PACK, align_bytes=256)
-            empty(engine, gz[g, s // 2][:, s % 2, :], banks[b][:])
+            copy(engine, gz[g, s // 2][:, s % 2, :], banks[b][:])
             if s % 2 == 1:
                 rows = out_1[0, g * KP : (g + 1) * KP, :].rearrange("(h m c) i -> m h c i", h=2, c=2)
-                q.dma_start(out=rows[:, s // 2], in_=gz[g, s // 2][:])
+                queue.dma_start(out=rows[:, s // 2], in_=gz[g, s // 2][:])
 
         nc.sync.dma_start(out=table[0][:], in_=wT_planes[:, 0, :])
         nc.sync.dma_start(offsets[:], offs)
@@ -256,7 +243,7 @@ def tile_attend_gdi_lch_wz_kernel(tc, zT, wT, xm, wt, zm, cs, offs, out_0, out_1
         for g in range(G):
             nc.sync.dma_start(out=zm_raw[g][:], in_=zm[0, g * KP : (g + 1) * KP, :].rearrange("(p j) i -> p j i", j=PACK))
         nc.vector.memset(window[0][:], 0.0)
-        for t in range(1, WINDOWS):
+        for t in range(1, PACK):
             nc.gpsimd.memset(window[t][:], 0.0)
 
         for t in range(2):
@@ -266,12 +253,14 @@ def tile_attend_gdi_lch_wz_kernel(tc, zT, wT, xm, wt, zm, cs, offs, out_0, out_1
             spread_wt(g)
         for t in range(2, PACK):
             gather_and_turn(t)
-        interleave_shared(wd_words, atoms, HALF)
+        interleave(V, wd_words, atoms, 0, HALF)
+        interleave(S, wd_words, atoms, HALF, KP)
         for h in range(2):
-            deal(nc.vector, zT_words[0], zT_raw[0], h, 0, HALF)
+            deal(V, zT_words[0], zT_raw[0], h, 0, HALF)
         quantize_early(0, 2)
         quantize_early(2, 3)
-        deal_shared(zT_words[1], zT_raw[1], 0)
+        for h, engine in enumerate((V, S)):
+            deal(engine, zT_words[1], zT_raw[1], h, 0, HALF)
         quantize_early(3, 5)
         residual(0, 0, 0, 0)
         quantize_early(5, 7)
@@ -280,18 +269,20 @@ def tile_attend_gdi_lch_wz_kernel(tc, zT, wT, xm, wt, zm, cs, offs, out_0, out_1
         residual(1, 0, 1, 3, staged[1])
         for h, pair in enumerate(((4, 5), (1, 3))):
             for u in range(2):
-                residual(u, 1, h, pair[u])
+                residual(u, 1, h, pair[u], staged[2] if u and h else None)
+
         interleave(nc.gpsimd, zm_words[0], zm_raw[0], 0, N)
         for (t, g), b in zip(((0, 0), (1, 0), (2, 0), (3, 0), (0, 1), (1, 1), (2, 1)), (0, 2, 4, 5, 1, 3, 0)):
             squash(t, g, b)
             weigh(t, g)
-        V, S = nc.vector, nc.scalar
+
         quantize(zm_mx[0], E4M3, zm_words[0])
+        deal(V, ed_words[0], e_planes[0], 1, HALF - SHARE, HALF)
         interleave(V, zm_words[1], zm_raw[1], 0, N)
         turn_error(0, 4, S)
         deal(S, ed_words[0], e_planes[0], 1, 0, P)
         deal(S, ed_words[0], e_planes[0], 0, 0, HALF)
-        deal(S, ed_words[0], e_planes[0], 1, P, HALF)
+        deal(S, ed_words[0], e_planes[0], 1, P, HALF - SHARE)
         quantize_er(0, 1)
         quantize(zm_mx[1], E4M3, zm_words[1])
         turn_error(1, 5, S)
@@ -302,13 +293,15 @@ def tile_attend_gdi_lch_wz_kernel(tc, zT, wT, xm, wt, zm, cs, offs, out_0, out_1
         weigh(3, 1)
         quantize_er(1, 3)
         atom_grad(0, 6, S)
+
         for s, b in enumerate((4, 5, 0, 2)):
             code_grad(0, s, b, S, S)
-        scatter(0, V)
+        scatter(0, V, 0, N)
         for h in range(2):
             deal(nc.gpsimd, ed_words[1], e_planes[1], h, 0, HALF)
         atom_grad(1, 7, S)
         atom_grad(2, 6, S)
+
         scatter(1, S, 0, HALF)
         scatter(2, S, 0, HALF)
         quantize(ed_mx[1][0], E5M2, ed_words[1][0])
@@ -316,8 +309,8 @@ def tile_attend_gdi_lch_wz_kernel(tc, zT, wT, xm, wt, zm, cs, offs, out_0, out_1
         quantize(ed_mx[1][1], E5M2, ed_words[1][1])
         quantize_er(3, 4)
         for s, b in enumerate((4, 5, 0, 3)):
-            code_grad(1, s, b, V)
+            code_grad(1, s, b, V, nc.sync)
         scatter(1, S, HALF, N)
         scatter(2, S, HALF, N)
         atom_grad(3, 1, V)
-        scatter(3, V, q=S)
+        scatter(3, V, 0, N, S)

from contextlib import ExitStack

import concourse.mybir as mybir
from concourse.masks import make_identity

N, T, D, R = 512, 2048, 512, 1024
FLOPS = 3 * 2 * R * D * N

F32 = mybir.dt.float32
BF16 = mybir.dt.bfloat16
U32 = mybir.dt.uint32
U16 = mybir.dt.uint16
U8 = mybir.dt.uint8
E4M3 = mybir.dt.float8_e4m3fn_x4
E5M2 = mybir.dt.float8_e5m2_x4
MULT = mybir.AluOpType.mult
ADD = mybir.AluOpType.add
SUB = mybir.AluOpType.subtract
TANH = mybir.ActivationFunctionType.Tanh
COPY = mybir.ActivationFunctionType.Copy

P = 128
PACK = 4
KP = P * PACK
G = R // KP
HALF = KP // 2
RUN = HALF * PACK
SHARE = 64
WORK_BANKS = 6


def tile_attend_gdi_lch_wz_kernel(tc, zT, wT, xm, wt, zm, cs, offs, out_0, out_1):
    nc = tc.nc
    V, S = nc.vector, nc.scalar
    with ExitStack() as ctx:
        keep = ctx.enter_context(tc.tile_pool(name="keep", bufs=1))
        ring = ctx.enter_context(tc.tile_pool(name="ring", bufs=1))
        psum = ctx.enter_context(tc.psum_pool(name="psum", bufs=1))

        def held(name, shape, dtype):
            return keep.tile(shape, dtype, name=name, align_bytes=256)

        def mx_operand(name, width):
            return held(name + "_codes", [P, width], U32), held(name + "_scales", [P, width], U8)

        def cols(operand, a, b):
            return operand[0][:, a:b], operand[1][:, a:b]

        def runs(tile, a, b):
            return tile[:, a * RUN : b * RUN]

        def quantize(operand, fmt, words):
            nc.vector.quantize_mx(out=operand[0].bitcast(fmt), scales=operand[1], in_=words)

        def mm(out, lhsT, lhsT_fmt, rhs, start=True, stop=True):
            nc.tensor.matmul_mx(
                out=out, lhsT=lhsT[0].bitcast(lhsT_fmt), lhsT_scale=lhsT[1],
                rhs=rhs[0].bitcast(E4M3), rhs_scale=rhs[1], start=start, stop=stop,
            )

        banks = [psum.tile([P, KP], F32, name="bank%d" % b) for b in range(WORK_BANKS + G)]
        wt_bank = banks[WORK_BANKS:]

        offsets = keep.tile([P, N // 16], U16, name="offsets")
        wt_rows = held("wt_rows", [P, G, PACK], F32)
        cs_cols = held("cs_cols", [P, PACK], F32)
        table = [held("table%d" % t, [P, T], F32) for t in range(PACK)]
        zT_raw = [held("zT_raw%d" % g, [P, PACK, KP], F32) for g in range(G)]
        zm_raw = [held("zm_raw%d" % g, [P, PACK, N], F32) for g in range(G)]
        xm_raw = [[held("xm_raw%d%d" % (g, h), [P, 2, D], F32) for h in range(2)] for g in range(G)]
        window = [held("window%d" % t, [P, T], F32) for t in range(PACK)]
        ident = held("ident", [P, P], F32)
        atoms = held("atoms", [P, PACK * N], BF16)[:].rearrange("p (t i) -> p t i", t=PACK)
        e_tiles = [xm_raw[1][0][:].rearrange("p c d -> p (c d)").bitcast(BF16), held("e1", [P, PACK * KP], BF16)[:]]
        e_planes = [e_tiles[g].rearrange("p (t r) -> p t r", t=PACK) for g in range(G)]
        th = {(t, g): zT_raw[g][:, t, :] for t in range(PACK) for g in range(G)}
        th[3, 1] = e_tiles[0][:, : 2 * KP].bitcast(F32)

        early = held("early", [P, 7 * RUN], BF16)
        er_all = held("er_words", [P, PACK * RUN], BF16)
        zm_words = [held("zm%d_words" % g, [P, 2 * RUN], BF16)[:] for g in range(G)]
        wi_words = [held("wi0_words", [P, RUN], BF16)[:], runs(early, 0, 1)]
        er_words = [runs(er_all, t, t + 1) for t in range(PACK)]
        zT_words = [[runs(early, a + h, a + h + 1) for h in range(2)] for a in (1, 5)]
        wd_words = runs(early, 3, 5)
        ed_both = [held("ed%d_words" % g, [P, 2 * RUN], BF16)[:] for g in range(G)]
        ed_words = [[runs(ed_both[g], h, h + 1) for h in range(2)] for g in range(G)]
        dw = [held("dw%d" % t, [P, N], F32)[:] for t in range(PACK)]

        staged = [zT_raw[1][:, 2 * h : 2 * h + 2, HALF:] for h in range(2)] + [held("staged", [P, 2, HALF], F32)[:]]
        early_mx = mx_operand("early", 7 * HALF)
        wi_mx = [cols(mx_operand("wi0", HALF), 0, HALF), cols(early_mx, 0, HALF)]
        zT_mx = [cols(early_mx, HALF, 3 * HALF), cols(early_mx, 5 * HALF, 7 * HALF)]
        wd_mx = cols(early_mx, 3 * HALF, 5 * HALF)
        zm_both = mx_operand("zm", G * N)
        zm_mx = [cols(zm_both, g * N, (g + 1) * N) for g in range(G)]
        er_codes = mx_operand("er", PACK * HALF)
        er_mx = [cols(er_codes, t * HALF, (t + 1) * HALF) for t in range(PACK)]
        ed_codes = [cols(mx_operand("ed%d" % g, KP), 0, KP) for g in range(G)]
        ed_mx = [[cols(ed_codes[g], h * HALF, (h + 1) * HALF) for h in range(2)] for g in range(G)]
        diff, turned, gz = {}, {}, {}

        wT_planes = wT.rearrange("(p t) c -> p t c", t=PACK)
        out0_planes = out_0.rearrange("(p t) c -> p t c", t=PACK)

        def copy(engine, out, in_):
            (engine.tensor_copy if engine is V else engine.copy)(out=out, in_=in_)

        def interleave(engine, words, planes, a, b):
            dst = words[:, a * PACK : b * PACK].rearrange("p (c t) -> p c t", t=PACK)
            src = planes[:, :, a:b]
            if engine is nc.gpsimd:
                engine.tensor_scalar(dst, src.rearrange("p t c -> p c t"), 1.0, 0.0, MULT, ADD)
                return
            copy(engine, dst.rearrange("p (c i) t -> p c t i", i=4), src.rearrange("p t (c i) -> p c t i", i=4))

        def deal(engine, words, planes, h, a, b):
            dst = words[h].rearrange("p (c m t) -> p c m t", c=2, t=PACK)[:, :, a // 2 : b // 2]
            src = planes[:, :, h * HALF + a : h * HALF + b]
            if engine is nc.gpsimd:
                engine.tensor_scalar(dst, src.rearrange("p t (m c) -> p c m t", c=2), 1.0, 0.0, MULT, ADD)
                return
            copy(
                engine,
                dst.rearrange("p c (n k) t -> p n t k c", k=2),
                src.rearrange("p t (n k c) -> p n t k c", k=2, c=2),
            )

        def quantize_early(a, b):
            quantize(cols(early_mx, a * HALF, b * HALF), E4M3, runs(early, a, b))

        def turn_words(plane, b, half=0):
            pairs = plane.bitcast(F32)
            bank = banks[b][:, half * HALF : (half + 1) * HALF].rearrange("p (v m) -> p v m", v=2)
            for v in range(2):
                nc.tensor.transpose(bank[:, v, :], pairs[:, v : 2 * P : 2], ident[:])
            return bank

        def gather_and_turn(t):
            u, e = divmod(t, 2)
            nc.vector.tensor_copy(atoms[:, t, :], table[t][:].indirect(offsets[:]))
            bank = turn_words(atoms[:, t, :], (PACK + t) % WORK_BANKS)
            nc.scalar.copy(
                out=wi_words[u].bitcast(F32).rearrange("p (n e k v) -> p e n k v", e=2, k=2, v=2)[:, e],
                in_=bank.rearrange("p v (n k) -> p n k v", k=2),
            )

        def spread_wt(g):
            for s in range(PACK):
                nc.tensor.transpose(wt_bank[g][:, s:KP:PACK], wt_rows[:, g, s : s + 1].to_broadcast([P, P]), ident[:])

        def residual(u, g, h, b, stage=None):
            bank = banks[b][:].rearrange("p (c m) -> p c m", c=2)
            for c in range(2):
                first = (2 * h + c) * P
                mm(bank[:, c, :], cols(zT_mx[g], first, first + P), E4M3, wi_mx[u])
            diff[u, g, h] = ring.tile([P, 2, 2 * P], F32, name="diff", bufs=2 * PACK, align_bytes=256)
            rows = xm_raw[g][h][:].rearrange("p c d -> p (c d)")
            rec = bank.rearrange("p c (n e k) -> p c n k e", e=2, k=2)
            rows = rows.rearrange("p (c n u e) -> p u c n e", c=2, u=2, e=2)[:, u]
            out = diff[u, g, h][:].rearrange("p c (n e) -> p c n e", e=2)
            if stage is None:
                planes = diff[u, g, h][:].rearrange("p e (n k) -> p n e k", k=2)
                nc.vector.tensor_tensor(
                    planes,
                    rec.rearrange("p c n k e -> p (c n) e k"),
                    rows.rearrange("p c (n k) e -> p (c n) e k", k=2),
                    SUB,
                )
                turned[u, g, h] = [[diff[u, g, h][:, e, c * P : (c + 1) * P] for c in range(2)] for e in range(2)]
                return
            turned[u, g, h] = [[diff[u, g, h][:, c, e : 2 * P : 2] for c in range(2)] for e in range(2)]
            nc.scalar.copy(out=stage.rearrange("p c (n k e) -> p c n k e", k=2, e=2), in_=rec)
            nc.gpsimd.tensor_tensor(out, stage.rearrange("p c (n e) -> p c n e", e=2), rows, SUB)

        def squash(t, g, b):
            u, e = divmod(t, 2)
            for c in range(PACK):
                nc.tensor.transpose(
                    banks[b][:, c * P : (c + 1) * P], turned[u, g, c // 2][e][c % 2], ident[:]
                )
            nc.scalar.activation(
                th[t, g].rearrange("p (h m c) -> p h m c", h=2, c=2),
                banks[b][:].rearrange("p (h c m) -> p h m c", h=2, c=2),
                TANH,
                scale=cs_cols[:, t : t + 1],
            )

        def weigh(t, g):
            nc.vector.scalar_tensor_tensor(
                e_planes[g][:, t, :], th[t, g], cs_cols[:, t : t + 1], wt_bank[g][:], MULT, MULT
            )

        def turn_error(t, b, engine, first=0):
            for g in range(first, G):
                turn_words(e_planes[g][:, t, :], b, g)
            copy(
                engine,
                er_words[t].bitcast(F32).rearrange("p (g m v) -> p g m v", g=G, v=2),
                banks[b][:].rearrange("p (g v m) -> p g m v", g=G, v=2),
            )

        def quantize_er(a, z):
            quantize(cols(er_codes, a * HALF, z * HALF), E5M2, runs(er_all, a, z))

        def atom_grad(t, b, engine):
            for g in range(G):
                mm(banks[b][:], cols(er_mx[t], g * P, (g + 1) * P), E5M2, zm_mx[g], g == 0, g == G - 1)
            copy(engine, dw[t], banks[b][:])

        def scatter(t, engine, a, z, queue=nc.sync):
            target = window[t][:].indirect(offsets[:, a // 16 : z // 16])
            if engine is V:
                V.tensor_copy(target, dw[t][:, a:z])
            else:
                S.activation(target, dw[t][:, a:z], COPY)
            if z == N:
                queue.dma_start(out=out0_planes[:, t, :], in_=window[t][:])

        def code_grad(g, s, b, engine, queue):
            mm(banks[b][:], cols(ed_mx[g][s // 2], s % 2 * P, (s % 2 + 1) * P), E5M2, wd_mx)
            if s % 2 == 0:
                gz[g, s // 2] = ring.tile([P, 2, N], F32, name="gz", bufs=PACK, align_bytes=256)
            copy(engine, gz[g, s // 2][:, s % 2, :], banks[b][:])
            if s % 2 == 1:
                rows = out_1[0, g * KP : (g + 1) * KP, :].rearrange("(h m c) i -> m h c i", h=2, c=2)
                queue.dma_start(out=rows[:, s // 2], in_=gz[g, s // 2][:])

        nc.sync.dma_start(out=table[0][:], in_=wT_planes[:, 0, :])
        nc.sync.dma_start(offsets[:], offs)
        nc.scalar.dma_start(out=wt_rows[:], in_=wt[0].rearrange("(g p s) o -> p g (s o)", p=P, s=PACK))
        nc.scalar.dma_start(out=cs_cols[:], in_=cs[0].rearrange("(p t) -> p t", t=PACK))
        make_identity(nc, ident[:])
        for t in range(1, PACK):
            nc.sync.dma_start(out=table[t][:], in_=wT_planes[:, t, :])
        zT_rows = zT[0].rearrange("(p j) r -> p j r", j=PACK)
        for g in range(G):
            nc.sync.dma_start(out=zT_raw[g][:], in_=zT_rows[:, :, g * KP : (g + 1) * KP])
        for g in range(G):
            rows = xm[0, g * KP : (g + 1) * KP, :].rearrange("(h p c) d -> p h c d", h=2, c=2)
            for h in range(2):
                nc.sync.dma_start(out=xm_raw[g][h][:], in_=rows[:, h])
        for g in range(G):
            nc.sync.dma_start(out=zm_raw[g][:], in_=zm[0, g * KP : (g + 1) * KP, :].rearrange("(p j) i -> p j i", j=PACK))
        nc.vector.memset(window[0][:], 0.0)
        for t in range(1, PACK):
            nc.gpsimd.memset(window[t][:], 0.0)

        for t in range(2):
            gather_and_turn(t)
        quantize(wi_mx[0], E4M3, wi_words[0])
        for g in range(G):
            spread_wt(g)
        for t in range(2, PACK):
            gather_and_turn(t)
        interleave(V, wd_words, atoms, 0, HALF)
        interleave(S, wd_words, atoms, HALF, KP)
        for h in range(2):
            deal(V, zT_words[0], zT_raw[0], h, 0, HALF)
        quantize_early(0, 2)
        quantize_early(2, 3)
        for h, engine in enumerate((V, S)):
            deal(engine, zT_words[1], zT_raw[1], h, 0, HALF)
        quantize_early(3, 5)
        residual(0, 0, 0, 0)
        quantize_early(5, 7)
        residual(1, 0, 0, 1, staged[0])
        residual(0, 0, 1, 2)
        residual(1, 0, 1, 3, staged[1])
        for h, pair in enumerate(((4, 5), (1, 3))):
            for u in range(2):
                residual(u, 1, h, pair[u], staged[2] if u and h else None)

        interleave(nc.gpsimd, zm_words[0], zm_raw[0], 0, N)
        for (t, g), b in zip(((0, 0), (1, 0), (2, 0), (3, 0), (0, 1), (1, 1), (2, 1)), (0, 2, 4, 5, 1, 3, 0)):
            squash(t, g, b)
            weigh(t, g)

        quantize(zm_mx[0], E4M3, zm_words[0])
        deal(V, ed_words[0], e_planes[0], 1, HALF - SHARE, HALF)
        interleave(V, zm_words[1], zm_raw[1], 0, N)
        turn_error(0, 4, S)
        deal(S, ed_words[0], e_planes[0], 1, 0, P)
        deal(S, ed_words[0], e_planes[0], 0, 0, HALF)
        deal(S, ed_words[0], e_planes[0], 1, P, HALF - SHARE)
        quantize_er(0, 1)
        quantize(zm_mx[1], E4M3, zm_words[1])
        turn_error(1, 5, S)
        turn_words(e_planes[0][:, 3, :], 3, 0)
        quantize(ed_codes[0], E5M2, ed_both[0])
        squash(3, 1, 2)
        turn_error(2, 1, S)
        weigh(3, 1)
        quantize_er(1, 3)
        atom_grad(0, 6, S)

        for s, b in enumerate((4, 5, 0, 2)):
            code_grad(0, s, b, S, S)
        scatter(0, V, 0, N)
        for h in range(2):
            deal(nc.gpsimd, ed_words[1], e_planes[1], h, 0, HALF)
        atom_grad(1, 7, S)
        atom_grad(2, 6, S)

        scatter(1, S, 0, HALF)
        scatter(2, S, 0, HALF)
        quantize(ed_mx[1][0], E5M2, ed_words[1][0])
        turn_error(3, 3, V, 1)
        quantize(ed_mx[1][1], E5M2, ed_words[1][1])
        quantize_er(3, 4)
        for s, b in enumerate((4, 5, 0, 3)):
            code_grad(1, s, b, V, nc.sync)
        scatter(1, S, HALF, N)
        scatter(2, S, HALF, N)
        atom_grad(3, 1, V)
        scatter(3, V, 0, N, S)
